import numpy as np
import ml_dtypes


def mxq(x, axis, fmt="e4m3"):
    dtype, down = {"e4m3": (ml_dtypes.float8_e4m3fn, 7), "e5m2": (ml_dtypes.float8_e5m2, 14)}[fmt]
    v = np.moveaxis(np.asarray(x, np.float32).astype(ml_dtypes.bfloat16).astype(np.float64), axis, -1)
    blocks = v.reshape(v.shape[:-1] + (-1, 32))
    amax = np.abs(blocks).max(-1, keepdims=True)
    byte = np.maximum(np.where(amax > 0, np.frexp(amax)[1] - 1 + 127, 0) - down, 1)
    scale = np.exp2(byte - 127.0)
    codes = (blocks / scale).astype(np.float32).astype(dtype).astype(np.float64)
    return np.moveaxis((codes * scale).reshape(v.shape), -1, axis)


WIDE = False


def mx_kscale(k):
    if not WIDE:
        return np.ones(k)
    levels = np.array([10, -10, 5, -5, 0])
    if k % 512:
        return np.exp2(np.random.permutation(np.resize(levels, k // 32))).repeat(32)
    a = np.empty((k // 512, 16))
    for p in range(k // 512):
        a[p, :8] = np.random.permutation(np.resize(levels, 8))
        for g in range(8):
            far = levels[np.abs(levels - a[p, g]) >= 10]
            a[p, g + 8] = far[np.random.randint(len(far))]
    return np.exp2(a.ravel()).repeat(32)


def f64(x):
    return np.asarray(x).astype(np.float64)


def striped(idx):
    return np.tile(idx.reshape(-1, 16).T, (8, 1)).astype(np.uint16)


def unstriped(offs):
    return offs[:16].T.reshape(-1).astype(np.int64)


E2M1 = np.array([0.0, 0.5, 1.0, 1.5, 2.0, 3.0, 4.0, 6.0, -0.0, -0.5, -1.0, -1.5, -2.0, -3.0, -4.0, -6.0])


def pack_weight(w, fmt):
    k, n = w.shape
    w = f64(np.asarray(w, np.float32).astype(ml_dtypes.bfloat16)).reshape(k // 32, 32, n)
    amax = np.abs(w).max(1)
    if fmt == "e4m3":
        byte = np.frexp(amax)[1] - 1 + 127 - 7
    else:
        mant, ex = np.frexp(amax / 6.0)
        byte = np.where(mant > 0.5, ex, ex - 1) + 127
    byte = np.clip(np.where(amax > 0, byte, 1), 1, 254)
    scaled = (w * np.exp2(127.0 - byte)[:, None, :]).reshape(k, n).astype(np.float32)
    by_word = np.ascontiguousarray(scaled.reshape(k // 512, 128, 4, n).transpose(0, 1, 3, 2))
    if fmt == "e4m3":
        words = by_word.astype(ml_dtypes.float8_e4m3fn).view(np.uint8)
    else:
        c = by_word.astype(ml_dtypes.float4_e2m1fn).view(np.uint8) & 0xF
        words = (c[..., 0::2] | (c[..., 1::2] << 4)).reshape(k // 512, 128, 2 * n)
    return np.ascontiguousarray(words), np.ascontiguousarray(byte.astype(np.uint8).reshape(k // 512, 16, n))


def unpack_weight(words, scales, fmt):
    g, _, n = scales.shape
    words = np.ascontiguousarray(words).reshape(g, 128, n, -1)
    if fmt == "e4m3":
        vals = words.view(ml_dtypes.float8_e4m3fn).astype(np.float64)
    else:
        nib = np.empty((g, 128, n, 4), np.uint8)
        nib[..., 0::2] = words & 0xF
        nib[..., 1::2] = words >> 4
        vals = E2M1[nib]
    vals = vals * np.repeat(np.exp2(scales.astype(np.float64) - 127.0), 8, axis=1)[..., None]
    return vals.transpose(0, 1, 3, 2).reshape(g * 512, n)


def gelu(v):
    return 0.5 * v * (1.0 + np.tanh(np.sqrt(2.0 / np.pi) * (v + 0.044715 * v**3)))


K, T, S, H, N = 1024, 2048, 1024, 1024, 256

def setup_inputs():
    n = np.random.standard_normal
    s = mx_kscale(K)[:, None]
    u = mx_kscale(H)[:, None]
    tab_words, tab_scales = pack_weight(n((K, T)) * s, "e4m3")
    wg_words, wg_scales = pack_weight(n((K, H)) / np.sqrt(K) / s, "e2m1")
    wd_words, wd_scales = pack_weight(1.5 * n((H, N)) / np.sqrt(H) / u, "e4m3")
    return {
        "tab_words": tab_words, "tab_scales": tab_scales,
        "offs": striped(np.random.permutation(T)[:S]),
        "wg_words": wg_words, "wg_scales": wg_scales,
        "bg": (0.5 * n(H)).astype(np.float32),
        "wv": (n((K, H)) / np.sqrt(K) / s * u.T).astype(np.float32),
        "wd_words": wd_words, "wd_scales": wd_scales,
        "bd": (0.3 * n(N)).astype(np.float32),
    }

def reference(tab_words, tab_scales, offs, wg_words, wg_scales, bg, wv, wd_words, wd_scales, bd):
    v = unpack_weight(tab_words, tab_scales, "e4m3")[:, unstriped(offs)]
    wg = unpack_weight(wg_words, wg_scales, "e2m1")
    wd = unpack_weight(wd_words, wd_scales, "e4m3")
    wvq = mxq(f64(wv), 0, "e4m3")
    g = wg.T @ v
    a = wvq.T @ v
    gate = 1.0 / (1.0 + np.exp(-(g + f64(bg)[:, None])))
    h = mxq(a * gate, 0, "e4m3")
    y = wd.T @ h
    return y + f64(bd)[:, None]

@@ -1,0 +1,256 @@
+from contextlib import ExitStack
+
+import concourse.mybir as mybir
+
+K, T, S, H, N = 1024, 2048, 1024, 1024, 256
+FLOPS = 2 * K * H * S * 2 + 2 * H * N * S
+
+F32 = mybir.dt.float32
+BF16 = mybir.dt.bfloat16
+I32 = mybir.dt.int32
+U32 = mybir.dt.uint32
+U16 = mybir.dt.uint16
+U8 = mybir.dt.uint8
+FP8X4 = mybir.dt.float8_e4m3fn_x4
+FP4X4 = mybir.dt.float4_e2m1fn_x4
+ACT = mybir.ActivationFunctionType
+MULT = mybir.AluOpType.mult
+
+P = 128
+HALF = 512
+
+
+def tile_list_clicked_item_candidates_kernel(
+    tc, tab_words, tab_scales, offs, wg_words, wg_scales, bg, wv, wd_words, wd_scales, bd, out
+):
+    nc = tc.nc
+    with ExitStack() as ctx:
+        keep = ctx.enter_context(tc.tile_pool(name="keep", bufs=1))
+        psum = ctx.enter_context(tc.psum_pool(name="psum", bufs=8))
+
+        offsets = keep.tile([P, S // 16], U16, name="offsets")
+        tab_w = [keep.tile([P, T], I32, name="tab_w%d" % a, align_bytes=64) for a in range(2)]
+        tab_s = keep.tile([P, 2, T // 4], I32, name="tab_s", align_bytes=64)
+        wg_w_raw = keep.tile([P, 2, H // 2], I32, name="wg_w_raw", align_bytes=64)
+        wg_s_raw = keep.tile([P, 2, H // 4], I32, name="wg_s_raw", align_bytes=64)
+        wg_w = keep.tile([P, 2, 2 * H], U8, name="wg_w", align_bytes=64)
+        wg_s = keep.tile([P, 2, H], U8, name="wg_s", align_bytes=64)
+        wd_w = keep.tile([P, 2, N], I32, name="wd_w", align_bytes=64)
+        wd_s = keep.tile([P, 2, N // 4], I32, name="wd_s", align_bytes=64)
+        bg_sb = keep.tile([P, 2, 4], F32, name="bg_sb")
+        bd_sb = keep.tile([P, 2], F32, name="bd_sb")
+        warm = keep.tile([P, 1], F32, name="warm")
+        v_w = keep.tile([P, 2, S], U32, name="v_w", align_bytes=64)
+        v_s = keep.tile([P, 2, S], U8, name="v_s", align_bytes=64)
+        wv_raw = {}
+        wv_bf = {}
+        gate = {}
+        h_bf = {}
+        for x in range(2):
+            for y in range(2):
+                wv_raw[x, y] = keep.tile([P, 4, HALF], F32, name="wv_raw%d%d" % (x, y), align_bytes=64)
+                wv_bf[x, y] = keep.tile([P, 4 * HALF], BF16, name="wv_bf%d%d" % (x, y), align_bytes=64)
+                gate[x, y] = keep.tile([P, 4, HALF], F32, name="gate%d%d" % (x, y), align_bytes=64)
+                h_bf[x, y] = keep.tile([P, 4 * HALF], BF16, name="h_bf%d%d" % (x, y), align_bytes=64)
+        wv_w = keep.tile([P, 2, H], U32, name="wv_w", align_bytes=64)
+        wv_s = keep.tile([P, 2, H], U8, name="wv_s", align_bytes=64)
+        h_w = keep.tile([P, 2, S], U32, name="h_w", align_bytes=64)
+        h_s = keep.tile([P, 2, S], U8, name="h_s", align_bytes=64)
+        y_sb = keep.tile([P, 2, S], F32, name="y_sb", align_bytes=64)
+
+        def load_scales(engine, tile, src):
+            for q in range(4):
+                engine.dma_start(
+                    out=tile[32 * q : 32 * q + 4, :, :],
+                    in_=src[:, 4 * q : 4 * q + 4, :].bitcast(I32).rearrange("a r w -> r a w"),
+                )
+
+        nc.vector.memset(tab_s[:], 0)
+        nc.vector.memset(wg_s_raw[:], 0)
+        nc.vector.memset(wd_s[:], 0)
+
+        def load_table(a):
+            nc.sync.dma_start(out=tab_w[a][:], in_=tab_words[a].rearrange("p n t -> p (n t)").bitcast(I32))
+
+        def load_wv(a, b):
+            nc.sync.dma_start(
+                out=wv_raw[a, b][:],
+                in_=wv[a * HALF : (a + 1) * HALF, b * HALF : (b + 1) * HALF].rearrange("(p j) c -> p j c", j=4),
+            )
+
+        nc.sync.dma_start(offsets[:], offs)
+        nc.sync.dma_start(out=wg_w_raw[:], in_=wg_words.bitcast(I32).rearrange("a p w -> p a w"))
+        load_scales(nc.sync, tab_s, tab_scales)
+        load_scales(nc.sync, wg_s_raw, wg_scales)
+        load_table(0)
+        nc.sync.dma_start(out=bg_sb[:], in_=bg.rearrange("(b p t) -> p b t", b=2, t=4))
+        load_wv(0, 0)
+        load_table(1)
+        load_wv(1, 0)
+        load_wv(0, 1)
+        load_wv(1, 1)
+        nc.sync.dma_start(out=wd_w[:], in_=wd_words.rearrange("a p n t -> p a (n t)").bitcast(I32))
+        load_scales(nc.sync, wd_s, wd_scales)
+        with nc.allow_non_contiguous_dma(reason="one bias value for each partition"):
+            nc.sync.dma_start(out=bd_sb[:], in_=bd.rearrange("(h p) -> p h", h=2))
+
+        nc.scalar.activation(out=warm[:], in_=bg_sb[:, 0, 0:1], func=ACT.Sigmoid)
+
+        def permute_wg(a):
+            nc.vector.tensor_copy(
+                out=wg_w[:, a, :].bitcast(U16).rearrange("p (b t m) -> p b t m", b=2, t=4),
+                in_=wg_w_raw[:, a, :].bitcast(U16).rearrange("p (b m t) -> p b t m", b=2, t=4),
+            )
+            nc.vector.tensor_copy(
+                out=wg_s[:, a, :].rearrange("p (b t m) -> p b t m", b=2, t=4),
+                in_=wg_s_raw[:, a, :].bitcast(U8).rearrange("p (b m t) -> p b t m", b=2, t=4),
+            )
+
+        def picks(h):
+            return offsets[:, h * (HALF // 16) : (h + 1) * (HALF // 16)]
+
+        def gather_scales(a, h):
+            nc.vector.tensor_copy(
+                out=v_s[:, a, h * HALF : (h + 1) * HALF], in_=tab_s[:, a, :].bitcast(U8).indirect(picks(h))
+            )
+
+        def gather_words(a, h):
+            nc.vector.tensor_copy(
+                out=v_w[:, a, h * HALF : (h + 1) * HALF], in_=tab_w[a][:].bitcast(U32).indirect(picks(h))
+            )
+
+        def cast_wv(engine, a, b):
+            dst = wv_bf[a, b][:].rearrange("p (t m j) -> p m j t", t=4, j=4)
+            src = wv_raw[a, b][:].rearrange("p j (m t) -> p m j t", t=4)
+            if engine is nc.scalar:
+                nc.scalar.copy(out=dst, in_=src)
+            else:
+                engine.tensor_copy(out=dst, in_=src)
+
+        def quantize_wv(a, b):
+            cols = slice(b * HALF, (b + 1) * HALF)
+            nc.vector.quantize_mx(out=wv_w[:, a, cols].bitcast(FP8X4), scales=wv_s[:, a, cols], in_=wv_bf[a, b][:])
+
+        def gate_pass(bank, a, b, t, h):
+            c0 = b * HALF + t * P
+            cols = slice(h * HALF, (h + 1) * HALF)
+            nc.tensor.matmul_mx(
+                out=bank[:],
+                lhsT=wg_w[:, a, 2 * c0 : 2 * c0 + 2 * P].bitcast(FP4X4),
+                lhsT_scale=wg_s[:, a, c0 : c0 + P],
+                rhs=v_w[:, a, cols].bitcast(FP8X4),
+                rhs_scale=v_s[:, a, cols],
+                start=(a == 0),
+                stop=(a == 1),
+            )
+
+        def sigmoid(bank, b, t, h):
+            nc.scalar.activation(out=gate[b, h][:, t, :], in_=bank[:], func=ACT.Sigmoid, bias=bg_sb[:, b, t : t + 1])
+
+        def gates(b, h):
+            for t in range(4):
+                bank = psum.tile([P, HALF], F32, name="bank")
+                for a in range(2):
+                    gate_pass(bank, a, b, t, h)
+                sigmoid(bank, b, t, h)
+
+        def values(b, h, c):
+            bank = psum.tile([P, HALF], F32, name="bank")
+            cols = slice(h * HALF + c * P, h * HALF + (c + 1) * P)
+            for t in range(4):
+                c0 = b * HALF + t * P
+                for a in range(2):
+                    nc.tensor.matmul_mx(
+                        out=bank[:, t * P : (t + 1) * P],
+                        lhsT=wv_w[:, a, c0 : c0 + P].bitcast(FP8X4),
+                        lhsT_scale=wv_s[:, a, c0 : c0 + P],
+                        rhs=v_w[:, a, cols].bitcast(FP8X4),
+                        rhs_scale=v_s[:, a, cols],
+                        start=(a == 0),
+                        stop=(a == 1),
+                    )
+            nc.vector.tensor_tensor(
+                out=h_bf[b, h][:, c * HALF : (c + 1) * HALF].rearrange("p (c i t) -> p c t i", i=2, t=4),
+                in0=bank[:].rearrange("p (t c i) -> p c t i", t=4, i=2),
+                in1=gate[b, h][:, :, c * P : (c + 1) * P].rearrange("p t (c i) -> p c t i", i=2),
+                op=MULT,
+            )
+
+        def quantize_h(b, h, c0, c1):
+            cols = slice(h * HALF + c0 * P, h * HALF + c1 * P)
+            nc.vector.quantize_mx(
+                out=h_w[:, b, cols].bitcast(FP8X4), scales=h_s[:, b, cols], in_=h_bf[b, h][:, c0 * HALF : c1 * HALF]
+            )
+
+        def project(j0, j1):
+            cols = slice(j0, j1)
+            for n in range(2):
+                bank = psum.tile([P, HALF], F32, name="bank")
+                for b in range(2):
+                    nc.tensor.matmul_mx(
+                        out=bank[:, 0 : j1 - j0],
+                        lhsT=wd_w[:, b, n * P : (n + 1) * P].bitcast(FP8X4),
+                        lhsT_scale=wd_s[:, b, :].bitcast(U8)[:, n * P : (n + 1) * P],
+                        rhs=h_w[:, b, cols].bitcast(FP8X4),
+                        rhs_scale=h_s[:, b, cols],
+                        start=(b == 0),
+                        stop=(b == 1),
+                    )
+                nc.scalar.activation(
+                    out=y_sb[:, n, cols], in_=bank[:, 0 : j1 - j0], func=ACT.Identity, bias=bd_sb[:, n : n + 1]
+                )
+            nc.sync.dma_start(out=out.rearrange("(n p) j -> p n j", n=2)[:, :, cols], in_=y_sb[:, :, cols])
+
+        permute_wg(0)
+        gather_scales(0, 0)
+        permute_wg(1)
+        gather_scales(1, 0)
+        gather_words(0, 0)
+        first = {}
+        for b in range(2):
+            for t in range(4):
+                first[b, t] = psum.tile([P, HALF], F32, name="bank")
+                gate_pass(first[b, t], 0, b, t, 0)
+        cast_wv(nc.scalar, 0, 0)
+        gather_words(1, 0)
+        for b in range(2):
+            for t in range(4):
+                gate_pass(first[b, t], 1, b, t, 0)
+                sigmoid(first[b, t], b, t, 0)
+        gather_scales(0, 1)
+        gather_scales(1, 1)
+        gather_words(0, 1)
+        gather_words(1, 1)
+        cast_wv(nc.vector, 1, 0)
+        quantize_wv(0, 0)
+        quantize_wv(1, 0)
+        gates(0, 1)
+        values(0, 0, 0)
+        values(0, 0, 1)
+        values(0, 0, 2)
+        cast_wv(nc.scalar, 0, 1)
+        cast_wv(nc.scalar, 1, 1)
+        values(0, 0, 3)
+        values(0, 1, 0)
+        quantize_h(0, 0, 0, 4)
+        values(0, 1, 1)
+        gates(1, 1)
+        values(0, 1, 2)
+        quantize_wv(0, 1)
+        quantize_wv(1, 1)
+        values(0, 1, 3)
+        values(1, 0, 0)
+        quantize_h(0, 1, 0, 4)
+        values(1, 0, 1)
+        values(1, 0, 2)
+        values(1, 0, 3)
+        values(1, 1, 0)
+        quantize_h(1, 0, 0, 4)
+        project(0, 512)
+        values(1, 1, 1)
+        values(1, 1, 2)
+        quantize_h(1, 1, 0, 2)
+        project(512, 768)
+        values(1, 1, 3)
+        quantize_h(1, 1, 2, 4)
+        project(768, 1024)

@@ -30,18 +30,20 @@ def tile_list_clicked_item_candidates_kernel(
 
         offsets = keep.tile([P, S // 16], U16, name="offsets")
         tab_w = [keep.tile([P, T], I32, name="tab_w%d" % a, align_bytes=64) for a in range(2)]
-        tab_s = keep.tile([P, 2, T // 4], I32, name="tab_s", align_bytes=64)
-        wg_w_raw = keep.tile([P, 2, H // 2], I32, name="wg_w_raw", align_bytes=64)
-        wg_s_raw = keep.tile([P, 2, H // 4], I32, name="wg_s_raw", align_bytes=64)
+        tab_s = keep.tile([P, T // 4], I32, name="tab_s", align_bytes=64)
+        wg_w_raw = [keep.tile([P, 2, H // 4], I32, name="wg_w_raw%d" % b, align_bytes=64) for b in range(2)]
+        wg_s_raw = keep.tile([P, H // 4], I32, name="wg_s_raw", align_bytes=64)
         wg_w = keep.tile([P, 2, 2 * H], U8, name="wg_w", align_bytes=64)
-        wg_s = keep.tile([P, 2, H], U8, name="wg_s", align_bytes=64)
+        wg_s = keep.tile([P, H], U8, name="wg_s", align_bytes=64)
+        wg_s1 = keep.tile([P, H // 4], I32, name="wg_s1", align_bytes=64)
         wd_w = keep.tile([P, 2, N], I32, name="wd_w", align_bytes=64)
         wd_s = keep.tile([P, 2, N // 4], I32, name="wd_s", align_bytes=64)
         bg_sb = keep.tile([P, 2, 4], F32, name="bg_sb")
         bd_sb = keep.tile([P, 2], F32, name="bd_sb")
         warm = keep.tile([P, 1], F32, name="warm")
         v_w = keep.tile([P, 2, S], U32, name="v_w", align_bytes=64)
-        v_s = keep.tile([P, 2, S], U8, name="v_s", align_bytes=64)
+        v_s = keep.tile([P, S], U8, name="v_s", align_bytes=64)
+        v_s1 = keep.tile([P, S // 4], I32, name="v_s1", align_bytes=64)
         wv_raw = {}
         wv_bf = {}
         gate = {}
@@ -65,67 +67,85 @@ def tile_list_clicked_item_candidates_kernel(
                     in_=src[:, 4 * q : 4 * q + 4, :].bitcast(I32).rearrange("a r w -> r a w"),
                 )
 
-        nc.vector.memset(tab_s[:], 0)
-        nc.vector.memset(wg_s_raw[:], 0)
-        nc.vector.memset(wd_s[:], 0)
-
         def load_table(a):
             nc.sync.dma_start(out=tab_w[a][:], in_=tab_words[a].rearrange("p n t -> p (n t)").bitcast(I32))
 
-        def load_wv(a, b):
+        def load_wg(b):
             nc.sync.dma_start(
-                out=wv_raw[a, b][:],
-                in_=wv[a * HALF : (a + 1) * HALF, b * HALF : (b + 1) * HALF].rearrange("(p j) c -> p j c", j=4),
+                out=wg_w_raw[b][:],
+                in_=wg_words.bitcast(I32)[:, :, b * (H // 4) : (b + 1) * (H // 4)].rearrange("a p w -> p a w"),
             )
+
+        def load_wv(a, b, c0=0, c1=HALF):
+            nc.sync.dma_start(
+                out=wv_raw[a, b][:, :, c0:c1],
+                in_=wv[a * HALF : (a + 1) * HALF, b * HALF + c0 : b * HALF + c1].rearrange("(p j) c -> p j c", j=4),
+            )
+
+        nc.vector.memset(tab_s[:], 0)
+        nc.vector.memset(wg_s_raw[:], 0)
+        nc.vector.memset(v_s1[:], 0)
+        nc.vector.memset(wg_s1[:], 0)
+        nc.vector.memset(wd_s[:], 0)
 
         nc.sync.dma_start(offsets[:], offs)
-        nc.sync.dma_start(out=wg_w_raw[:], in_=wg_words.bitcast(I32).rearrange("a p w -> p a w"))
-        load_scales(nc.sync, tab_s, tab_scales)
-        load_scales(nc.sync, wg_s_raw, wg_scales)
+        for q in range(4):
+            nc.sync.dma_start(out=tab_s[32 * q : 32 * q + 8, :], in_=tab_scales[:, 4 * q : 4 * q + 4, :].bitcast(I32))
+        load_wg(0)
         load_table(0)
-        nc.sync.dma_start(out=bg_sb[:], in_=bg.rearrange("(b p t) -> p b t", b=2, t=4))
-        load_wv(0, 0)
-        load_table(1)
-        load_wv(1, 0)
-        load_wv(0, 1)
-        load_wv(1, 1)
-        nc.sync.dma_start(out=wd_w[:], in_=wd_words.rearrange("a p n t -> p a (n t)").bitcast(I32))
-        load_scales(nc.sync, wd_s, wd_scales)
-        with nc.allow_non_contiguous_dma(reason="one bias value for each partition"):
-            nc.sync.dma_start(out=bd_sb[:], in_=bd.rearrange("(h p) -> p h", h=2))
-
-        nc.scalar.activation(out=warm[:], in_=bg_sb[:, 0, 0:1], func=ACT.Sigmoid)
-
-        def permute_wg(a):
-            nc.vector.tensor_copy(
-                out=wg_w[:, a, :].bitcast(U16).rearrange("p (b t m) -> p b t m", b=2, t=4),
-                in_=wg_w_raw[:, a, :].bitcast(U16).rearrange("p (b m t) -> p b t m", b=2, t=4),
+        for q in range(4):
+            nc.scalar.dma_start(
+                out=wg_s_raw[32 * q : 32 * q + 8, :], in_=wg_scales[:, 4 * q : 4 * q + 4, :].bitcast(I32)
             )
+        nc.scalar.dma_start(out=bg_sb[:], in_=bg.rearrange("(b p t) -> p b t", b=2, t=4))
+        nc.scalar.activation(out=warm[:], in_=bg_sb[:, 0, 0:1], func=ACT.Sigmoid)
+        load_wv(0, 0, 0, HALF // 2)
+
+        load_table(1)
+
+        def late_loads():
+            load_wv(0, 0, HALF // 2, HALF)
+            load_wv(1, 0, 0, HALF // 2)
+            load_wv(1, 0, HALF // 2, HALF)
+            load_wg(1)
+            load_wv(0, 1)
+            load_wv(1, 1)
+            nc.sync.dma_start(out=wd_w[:], in_=wd_words.rearrange("a p n t -> p a (n t)").bitcast(I32))
+            load_scales(nc.sync, wd_s, wd_scales)
+            with nc.allow_non_contiguous_dma(reason="one bias value for each partition"):
+                nc.sync.dma_start(out=bd_sb[:], in_=bd.rearrange("(h p) -> p h", h=2))
+
+        def lower_rows(dst, src):
+            nc.scalar.dma_start(out=dst[0:100, :], in_=src[4:104, :].bitcast(I32))
+
+        def permute_wg_words(b):
             nc.vector.tensor_copy(
-                out=wg_s[:, a, :].rearrange("p (b t m) -> p b t m", b=2, t=4),
-                in_=wg_s_raw[:, a, :].bitcast(U8).rearrange("p (b m t) -> p b t m", b=2, t=4),
+                out=wg_w[:, :, 2 * b * HALF : 2 * (b + 1) * HALF].bitcast(U16).rearrange("p a (t m) -> p a t m", t=4),
+                in_=wg_w_raw[b][:].bitcast(U16).rearrange("p a (m t) -> p a t m", t=4),
+            )
+
+        def permute_wg_scales():
+            nc.vector.tensor_copy(
+                out=wg_s[:].rearrange("p (b t m) -> p b t m", b=2, t=4),
+                in_=wg_s_raw[:].bitcast(U8).rearrange("p (b m t) -> p b t m", b=2, t=4),
             )
 
         def picks(h):
             return offsets[:, h * (HALF // 16) : (h + 1) * (HALF // 16)]
 
-        def gather_scales(a, h):
-            nc.vector.tensor_copy(
-                out=v_s[:, a, h * HALF : (h + 1) * HALF], in_=tab_s[:, a, :].bitcast(U8).indirect(picks(h))
-            )
+        def gather_scales():
+            nc.vector.tensor_copy(out=v_s[:], in_=tab_s[:].bitcast(U8).indirect(offsets[:]))
 
         def gather_words(a, h):
             nc.vector.tensor_copy(
                 out=v_w[:, a, h * HALF : (h + 1) * HALF], in_=tab_w[a][:].bitcast(U32).indirect(picks(h))
             )
 
-        def cast_wv(engine, a, b):
+        def cast_wv(copy, a, b, m0=0, m1=P):
             dst = wv_bf[a, b][:].rearrange("p (t m j) -> p m j t", t=4, j=4)
             src = wv_raw[a, b][:].rearrange("p j (m t) -> p m j t", t=4)
-            if engine is nc.scalar:
-                nc.scalar.copy(out=dst, in_=src)
-            else:
-                engine.tensor_copy(out=dst, in_=src)
+            for t in (0, 2):
+                copy(out=dst[:, m0:m1, :, t : t + 2], in_=src[:, m0:m1, :, t : t + 2])
 
         def quantize_wv(a, b):
             cols = slice(b * HALF, (b + 1) * HALF)
@@ -137,9 +157,9 @@ def tile_list_clicked_item_candidates_kernel(
             nc.tensor.matmul_mx(
                 out=bank[:],
                 lhsT=wg_w[:, a, 2 * c0 : 2 * c0 + 2 * P].bitcast(FP4X4),
-                lhsT_scale=wg_s[:, a, c0 : c0 + P],
+                lhsT_scale=(wg_s[:] if a == 0 else wg_s1[:].bitcast(U8))[:, c0 : c0 + P],
                 rhs=v_w[:, a, cols].bitcast(FP8X4),
-                rhs_scale=v_s[:, a, cols],
+                rhs_scale=(v_s[:] if a == 0 else v_s1[:].bitcast(U8))[:, cols],
                 start=(a == 0),
                 stop=(a == 1),
             )
@@ -165,7 +185,7 @@ def tile_list_clicked_item_candidates_kernel(
                         lhsT=wv_w[:, a, c0 : c0 + P].bitcast(FP8X4),
                         lhsT_scale=wv_s[:, a, c0 : c0 + P],
                         rhs=v_w[:, a, cols].bitcast(FP8X4),
-                        rhs_scale=v_s[:, a, cols],
+                        rhs_scale=v_s[4 * a : P, cols],
                         start=(a == 0),
                         stop=(a == 1),
                     )
@@ -196,49 +216,62 @@ def tile_list_clicked_item_candidates_kernel(
                         start=(b == 0),
                         stop=(b == 1),
                     )
-                nc.scalar.activation(
-                    out=y_sb[:, n, cols], in_=bank[:, 0 : j1 - j0], func=ACT.Identity, bias=bd_sb[:, n : n + 1]
-                )
+                if n == 1 and j1 == S:
+                    nc.vector.tensor_scalar(
+                        out=y_sb[:, n, cols],
+                        in0=bank[:, 0 : j1 - j0],
+                        scalar1=bd_sb[:, n : n + 1],
+                        scalar2=None,
+                        op0=mybir.AluOpType.add,
+                    )
+                else:
+                    nc.scalar.activation(
+                        out=y_sb[:, n, cols], in_=bank[:, 0 : j1 - j0], func=ACT.Identity, bias=bd_sb[:, n : n + 1]
+                    )
             nc.sync.dma_start(out=out.rearrange("(n p) j -> p n j", n=2)[:, :, cols], in_=y_sb[:, :, cols])
 
-        permute_wg(0)
-        gather_scales(0, 0)
-        permute_wg(1)
-        gather_scales(1, 0)
+        gather_scales()
+        lower_rows(v_s1, v_s)
+        permute_wg_words(0)
+        permute_wg_scales()
+        lower_rows(wg_s1, wg_s)
         gather_words(0, 0)
+        late_loads()
         first = {}
-        for b in range(2):
+        for h in range(2):
+            if h == 1:
+                gather_words(0, 1)
             for t in range(4):
-                first[b, t] = psum.tile([P, HALF], F32, name="bank")
-                gate_pass(first[b, t], 0, b, t, 0)
-        cast_wv(nc.scalar, 0, 0)
-        gather_words(1, 0)
-        for b in range(2):
+                first[h, t] = psum.tile([P, HALF], F32, name="bank")
+                gate_pass(first[h, t], 0, 0, t, h)
+        cast_wv(nc.scalar.copy, 0, 0, 0, P // 2)
+        cast_wv(nc.scalar.copy, 0, 0, P // 2, P)
+        for h in range(2):
+            gather_words(1, h)
             for t in range(4):
-                gate_pass(first[b, t], 1, b, t, 0)
-                sigmoid(first[b, t], b, t, 0)
-        gather_scales(0, 1)
-        gather_scales(1, 1)
-        gather_words(0, 1)
-        gather_words(1, 1)
-        cast_wv(nc.vector, 1, 0)
+                gate_pass(first[h, t], 1, 0, t, h)
+                sigmoid(first[h, t], 0, t, h)
         quantize_wv(0, 0)
+        cast_wv(nc.vector.tensor_copy, 1, 0, 0, P // 2)
+        cast_wv(nc.vector.tensor_copy, 1, 0, P // 2, P)
+        permute_wg_words(1)
         quantize_wv(1, 0)
-        gates(0, 1)
         values(0, 0, 0)
         values(0, 0, 1)
+        cast_wv(nc.scalar.copy, 0, 1)
+        cast_wv(nc.scalar.copy, 1, 1, 0, P // 2)
         values(0, 0, 2)
-        cast_wv(nc.scalar, 0, 1)
-        cast_wv(nc.scalar, 1, 1)
         values(0, 0, 3)
+        gates(1, 0)
         values(0, 1, 0)
         quantize_h(0, 0, 0, 4)
         values(0, 1, 1)
-        gates(1, 1)
-        values(0, 1, 2)
         quantize_wv(0, 1)
-        quantize_wv(1, 1)
+        values(0, 1, 2)
+        cast_wv(nc.vector.tensor_copy, 1, 1, P // 2, P)
         values(0, 1, 3)
+        quantize_wv(1, 1)
+        gates(1, 1)
         values(1, 0, 0)
         quantize_h(0, 1, 0, 4)
         values(1, 0, 1)
@@ -246,11 +279,13 @@ def tile_list_clicked_item_candidates_kernel(
         values(1, 0, 3)
         values(1, 1, 0)
         quantize_h(1, 0, 0, 4)
-        project(0, 512)
         values(1, 1, 1)
+        project(0, 512)
         values(1, 1, 2)
         quantize_h(1, 1, 0, 2)
-        project(512, 768)
         values(1, 1, 3)
-        quantize_h(1, 1, 2, 4)
-        project(768, 1024)
+        project(512, 768)
+        quantize_h(1, 1, 2, 3)
+        project(768, 896)
+        quantize_h(1, 1, 3, 4)
+        project(896, 1024)

@@ -14,10 +14,11 @@ U8 = mybir.dt.uint8
 FP8X4 = mybir.dt.float8_e4m3fn_x4
 FP4X4 = mybir.dt.float4_e2m1fn_x4
 ACT = mybir.ActivationFunctionType
-MULT = mybir.AluOpType.mult
+ALU = mybir.AluOpType
 
 P = 128
 HALF = 512
+QUARTER = 256
 
 
 def tile_list_clicked_item_candidates_kernel(
@@ -26,157 +27,131 @@ def tile_list_clicked_item_candidates_kernel(
     nc = tc.nc
     with ExitStack() as ctx:
         keep = ctx.enter_context(tc.tile_pool(name="keep", bufs=1))
-        psum = ctx.enter_context(tc.psum_pool(name="psum", bufs=8))
+        psum = ctx.enter_context(tc.psum_pool(name="psum", bufs=4))
+        sb = {}
+
+        def new(name, shape, dtype, after=None):
+            tag = name if after is None else sb[after + " tag"]
+            sb[name] = keep.tile(shape, dtype, name=name, tag=tag, align_bytes=64)
+            sb[name + " tag"] = tag
+            return sb[name]
 
         offsets = keep.tile([P, S // 16], U16, name="offsets")
-        tab_w = [keep.tile([P, T], I32, name="tab_w%d" % a, align_bytes=64) for a in range(2)]
-        tab_s = keep.tile([P, T // 4], I32, name="tab_s", align_bytes=64)
-        wg_w_raw = [keep.tile([P, 2, H // 4], I32, name="wg_w_raw%d" % b, align_bytes=64) for b in range(2)]
-        wg_s_raw = keep.tile([P, H // 4], I32, name="wg_s_raw", align_bytes=64)
-        wg_w = keep.tile([P, 2, 2 * H], U8, name="wg_w", align_bytes=64)
-        wg_s = keep.tile([P, H], U8, name="wg_s", align_bytes=64)
-        wg_s1 = keep.tile([P, H // 4], I32, name="wg_s1", align_bytes=64)
-        wd_w = keep.tile([P, 2, N], I32, name="wd_w", align_bytes=64)
-        wd_s = keep.tile([P, 2, N // 4], I32, name="wd_s", align_bytes=64)
-        bg_sb = keep.tile([P, 2, 4], F32, name="bg_sb")
-        bd_sb = keep.tile([P, 2], F32, name="bd_sb")
-        warm = keep.tile([P, 1], F32, name="warm")
-        v_w = keep.tile([P, 2, S], U32, name="v_w", align_bytes=64)
-        v_s = keep.tile([P, S], U8, name="v_s", align_bytes=64)
-        v_s1 = keep.tile([P, S // 4], I32, name="v_s1", align_bytes=64)
-        wv_raw = {}
-        wv_bf = {}
-        gate = {}
-        h_bf = {}
-        for x in range(2):
-            for y in range(2):
-                wv_raw[x, y] = keep.tile([P, 4, HALF], F32, name="wv_raw%d%d" % (x, y), align_bytes=64)
-                wv_bf[x, y] = keep.tile([P, 4 * HALF], BF16, name="wv_bf%d%d" % (x, y), align_bytes=64)
-                gate[x, y] = keep.tile([P, 4, HALF], F32, name="gate%d%d" % (x, y), align_bytes=64)
-                h_bf[x, y] = keep.tile([P, 4 * HALF], BF16, name="h_bf%d%d" % (x, y), align_bytes=64)
-        wv_w = keep.tile([P, 2, H], U32, name="wv_w", align_bytes=64)
-        wv_s = keep.tile([P, 2, H], U8, name="wv_s", align_bytes=64)
-        h_w = keep.tile([P, 2, S], U32, name="h_w", align_bytes=64)
-        h_s = keep.tile([P, 2, S], U8, name="h_s", align_bytes=64)
-        y_sb = keep.tile([P, 2, S], F32, name="y_sb", align_bytes=64)
+        bg_sb = new("bg_sb", [P, 2, 4], F32)
+        warm = new("warm", [P, 1], F32)
+        wg_w = new("wg_w", [P, 2, 2 * H], U8)
+        wv_w = new("wv_w", [P, 2, H], U32)
+        wv_s = new("wv_s", [P, 2, H], U8)
+        h_w = new("h_w", [P, 2, S], U32)
+        h_s = new("h_s", [P, 2, S], U8)
+        y_sb = new("y_sb", [P, 2, S], F32)
+        v_s0 = new("v_s0", [P, S], U8)
+        v_s1 = new("v_s1", [P, S // 4], I32)
+        tab_s = new("tab_s", [P, T // 4], I32)
+        wd_s = new("wd_s", [P, 2, N // 4], I32)
+        wg_s_raw = new("wg_s_raw", [P, 2, H // 4], I32)
+        for b in range(2):
+            for h in range(2):
+                new("gate%d%d" % (b, h), [P, 4, HALF], F32)
+                new("h_bf%d%d" % (b, h), [P, 4 * HALF], BF16)
+                new("wv_bf%d%d" % (b, h), [P, 4 * HALF], BF16)
 
-        def load_scales(engine, tile, src):
+        def load_scales(tile, src):
             for q in range(4):
-                engine.dma_start(
+                nc.sync.dma_start(
                     out=tile[32 * q : 32 * q + 4, :, :],
                     in_=src[:, 4 * q : 4 * q + 4, :].bitcast(I32).rearrange("a r w -> r a w"),
                 )
 
         def load_table(a):
-            nc.sync.dma_start(out=tab_w[a][:], in_=tab_words[a].rearrange("p n t -> p (n t)").bitcast(I32))
+            tile = new("tab_w%d" % a, [P, T], I32)
+            nc.sync.dma_start(out=tile[:], in_=tab_words[a].rearrange("p n t -> p (n t)").bitcast(I32))
 
-        def load_wg(b):
+        def load_wg(b, after=None):
+            tile = new("wg_w_raw%d" % b, [P, 2, H // 4], I32, after)
             nc.sync.dma_start(
-                out=wg_w_raw[b][:],
+                out=tile[:],
                 in_=wg_words.bitcast(I32)[:, :, b * (H // 4) : (b + 1) * (H // 4)].rearrange("a p w -> p a w"),
             )
 
-        def load_wv(a, b, c0=0, c1=HALF):
+        def load_wv(a, b, c0, c1, after=None):
+            if c0 == 0:
+                new("wv_raw%d%d" % (a, b), [P, 4 * HALF], F32, after)
             nc.sync.dma_start(
-                out=wv_raw[a, b][:, :, c0:c1],
+                out=sb["wv_raw%d%d" % (a, b)][:, 4 * c0 : 4 * c1].rearrange("p (j c) -> p j c", j=4),
                 in_=wv[a * HALF : (a + 1) * HALF, b * HALF + c0 : b * HALF + c1].rearrange("(p j) c -> p j c", j=4),
             )
 
-        nc.vector.memset(tab_s[:], 0)
-        nc.vector.memset(wg_s_raw[:], 0)
-        nc.vector.memset(v_s1[:], 0)
-        nc.vector.memset(wg_s1[:], 0)
-        nc.vector.memset(wd_s[:], 0)
+        def cast_wv(copy, a, b, piece, c0, c1):
+            dst = sb["wv_bf%d%d" % (a, b)][:].rearrange("p (t m j) -> p m j t", t=4, j=4)[:, c0 // 4 : c1 // 4, :, :]
+            raw = sb["wv_raw%d%d" % (a, b)][:, 4 * piece[0] : 4 * piece[1]].rearrange("p (j m t) -> p m j t", j=4, t=4)
+            src = raw[:, (c0 - piece[0]) // 4 : (c1 - piece[0]) // 4, :, :]
+            for t in (0, 2):
+                copy(out=dst[:, :, :, t : t + 2], in_=src[:, :, :, t : t + 2])
 
-        nc.sync.dma_start(offsets[:], offs)
-        for q in range(4):
-            nc.sync.dma_start(out=tab_s[32 * q : 32 * q + 8, :], in_=tab_scales[:, 4 * q : 4 * q + 4, :].bitcast(I32))
-        load_wg(0)
-        load_table(0)
-        for q in range(4):
-            nc.scalar.dma_start(
-                out=wg_s_raw[32 * q : 32 * q + 8, :], in_=wg_scales[:, 4 * q : 4 * q + 4, :].bitcast(I32)
+        def quantize_wv(a, b):
+            cols = slice(b * HALF, (b + 1) * HALF)
+            nc.vector.quantize_mx(
+                out=wv_w[:, a, cols].bitcast(FP8X4), scales=wv_s[:, a, cols], in_=sb["wv_bf%d%d" % (a, b)][:]
             )
-        nc.scalar.dma_start(out=bg_sb[:], in_=bg.rearrange("(b p t) -> p b t", b=2, t=4))
-        nc.scalar.activation(out=warm[:], in_=bg_sb[:, 0, 0:1], func=ACT.Sigmoid)
-        load_wv(0, 0, 0, HALF // 2)
-
-        load_table(1)
-
-        def late_loads():
-            load_wv(0, 0, HALF // 2, HALF)
-            load_wv(1, 0, 0, HALF // 2)
-            load_wv(1, 0, HALF // 2, HALF)
-            load_wg(1)
-            load_wv(0, 1)
-            load_wv(1, 1)
-            nc.sync.dma_start(out=wd_w[:], in_=wd_words.rearrange("a p n t -> p a (n t)").bitcast(I32))
-            load_scales(nc.sync, wd_s, wd_scales)
-            with nc.allow_non_contiguous_dma(reason="one bias value for each partition"):
-                nc.sync.dma_start(out=bd_sb[:], in_=bd.rearrange("(h p) -> p h", h=2))
-
-        def lower_rows(dst, src):
-            nc.scalar.dma_start(out=dst[0:100, :], in_=src[4:104, :].bitcast(I32))
 
         def permute_wg_words(b):
             nc.vector.tensor_copy(
                 out=wg_w[:, :, 2 * b * HALF : 2 * (b + 1) * HALF].bitcast(U16).rearrange("p a (t m) -> p a t m", t=4),
-                in_=wg_w_raw[b][:].bitcast(U16).rearrange("p a (m t) -> p a t m", t=4),
+                in_=sb["wg_w_raw%d" % b][:].bitcast(U16).rearrange("p a (m t) -> p a t m", t=4),
             )
 
-        def permute_wg_scales():
+        def permute_wg_scales(b, after=None):
+            tile = new("wg_s%d" % b, [P, 2, HALF], U8, after)
             nc.vector.tensor_copy(
-                out=wg_s[:].rearrange("p (b t m) -> p b t m", b=2, t=4),
-                in_=wg_s_raw[:].bitcast(U8).rearrange("p (b m t) -> p b t m", b=2, t=4),
+                out=tile[:].rearrange("p a (t m) -> p a t m", t=4),
+                in_=wg_s_raw[:].bitcast(U8)[:, :, b * HALF : (b + 1) * HALF].rearrange("p a (m t) -> p a t m", t=4),
             )
 
         def picks(h):
             return offsets[:, h * (HALF // 16) : (h + 1) * (HALF // 16)]
 
         def gather_scales():
-            nc.vector.tensor_copy(out=v_s[:], in_=tab_s[:].bitcast(U8).indirect(offsets[:]))
+            nc.vector.tensor_copy(out=v_s0[:], in_=tab_s[:].bitcast(U8).indirect(offsets[:]))
 
-        def gather_words(a, h):
-            nc.vector.tensor_copy(
-                out=v_w[:, a, h * HALF : (h + 1) * HALF], in_=tab_w[a][:].bitcast(U32).indirect(picks(h))
-            )
+        def move_scale_rows():
+            for q in range(4):
+                nc.sync.dma_start(out=v_s1[32 * q : 32 * q + 4, :], in_=v_s0[16 + 4 * q : 20 + 4 * q, :].bitcast(I32))
 
-        def cast_wv(copy, a, b, m0=0, m1=P):
-            dst = wv_bf[a, b][:].rearrange("p (t m j) -> p m j t", t=4, j=4)
-            src = wv_raw[a, b][:].rearrange("p j (m t) -> p m j t", t=4)
-            for t in (0, 2):
-                copy(out=dst[:, m0:m1, :, t : t + 2], in_=src[:, m0:m1, :, t : t + 2])
+        def gather_words(a, h, after=None):
+            tile = new("v_w%d%d" % (a, h), [P, HALF], U32, after)
+            nc.vector.tensor_copy(out=tile[:], in_=sb["tab_w%d" % a][:].bitcast(U32).indirect(picks(h)))
 
-        def quantize_wv(a, b):
-            cols = slice(b * HALF, (b + 1) * HALF)
-            nc.vector.quantize_mx(out=wv_w[:, a, cols].bitcast(FP8X4), scales=wv_s[:, a, cols], in_=wv_bf[a, b][:])
+        def v_scales(a, h, c0, c1):
+            plane = v_s0[:] if a == 0 else v_s1[:].bitcast(U8)
+            return plane[:, h * HALF + c0 : h * HALF + c1]
 
         def gate_pass(bank, a, b, t, h):
             c0 = b * HALF + t * P
-            cols = slice(h * HALF, (h + 1) * HALF)
             nc.tensor.matmul_mx(
                 out=bank[:],
                 lhsT=wg_w[:, a, 2 * c0 : 2 * c0 + 2 * P].bitcast(FP4X4),
-                lhsT_scale=(wg_s[:] if a == 0 else wg_s1[:].bitcast(U8))[:, c0 : c0 + P],
-                rhs=v_w[:, a, cols].bitcast(FP8X4),
-                rhs_scale=(v_s[:] if a == 0 else v_s1[:].bitcast(U8))[:, cols],
+                lhsT_scale=sb["wg_s%d" % b][:, a, t * P : (t + 1) * P],
+                rhs=sb["v_w%d%d" % (a, h)][:].bitcast(FP8X4),
+                rhs_scale=v_scales(a, h, 0, HALF),
                 start=(a == 0),
                 stop=(a == 1),
             )
 
         def sigmoid(bank, b, t, h):
-            nc.scalar.activation(out=gate[b, h][:, t, :], in_=bank[:], func=ACT.Sigmoid, bias=bg_sb[:, b, t : t + 1])
+            nc.scalar.activation(
+                out=sb["gate%d%d" % (b, h)][:, t, :], in_=bank[:], func=ACT.Sigmoid, bias=bg_sb[:, b, t : t + 1]
+            )
 
         def gates(b, h):
             for t in range(4):
-                bank = psum.tile([P, HALF], F32, name="bank")
+                bank = psum.tile([P, HALF], F32, name="gate_bank", tag="gate")
                 for a in range(2):
                     gate_pass(bank, a, b, t, h)
                 sigmoid(bank, b, t, h)
 
         def values(b, h, c):
-            bank = psum.tile([P, HALF], F32, name="bank")
-            cols = slice(h * HALF + c * P, h * HALF + (c + 1) * P)
+            bank = psum.tile([P, HALF], F32, name="value_bank", tag="value")
             for t in range(4):
                 c0 = b * HALF + t * P
                 for a in range(2):
@@ -184,106 +159,141 @@ def tile_list_clicked_item_candidates_kernel(
                         out=bank[:, t * P : (t + 1) * P],
                         lhsT=wv_w[:, a, c0 : c0 + P].bitcast(FP8X4),
                         lhsT_scale=wv_s[:, a, c0 : c0 + P],
-                        rhs=v_w[:, a, cols].bitcast(FP8X4),
-                        rhs_scale=v_s[4 * a : P, cols],
+                        rhs=sb["v_w%d%d" % (a, h)][:, c * P : (c + 1) * P].bitcast(FP8X4),
+                        rhs_scale=v_scales(a, h, c * P, (c + 1) * P),
                         start=(a == 0),
                         stop=(a == 1),
                     )
             nc.vector.tensor_tensor(
-                out=h_bf[b, h][:, c * HALF : (c + 1) * HALF].rearrange("p (c i t) -> p c t i", i=2, t=4),
+                out=sb["h_bf%d%d" % (b, h)][:, c * HALF : (c + 1) * HALF].rearrange("p (c i t) -> p c t i", i=2, t=4),
                 in0=bank[:].rearrange("p (t c i) -> p c t i", t=4, i=2),
-                in1=gate[b, h][:, :, c * P : (c + 1) * P].rearrange("p t (c i) -> p c t i", i=2),
-                op=MULT,
+                in1=sb["gate%d%d" % (b, h)][:, :, c * P : (c + 1) * P].rearrange("p t (c i) -> p c t i", i=2),
+                op=ALU.mult,
             )
 
         def quantize_h(b, h, c0, c1):
             cols = slice(h * HALF + c0 * P, h * HALF + c1 * P)
             nc.vector.quantize_mx(
-                out=h_w[:, b, cols].bitcast(FP8X4), scales=h_s[:, b, cols], in_=h_bf[b, h][:, c0 * HALF : c1 * HALF]
+                out=h_w[:, b, cols].bitcast(FP8X4),
+                scales=h_s[:, b, cols],
+                in_=sb["h_bf%d%d" % (b, h)][:, c0 * HALF : c1 * HALF],
             )
+
+        def load_wd():
+            wd_w = new("wd_w", [P, 2, N], I32)
+            bd_sb = new("bd_sb", [P, 2], F32)
+            nc.sync.dma_start(out=wd_w[:], in_=wd_words.rearrange("a p n t -> p a (n t)").bitcast(I32))
+            load_scales(wd_s, wd_scales)
+            with nc.allow_non_contiguous_dma(reason="one bias value for each partition"):
+                nc.sync.dma_start(out=bd_sb[:], in_=bd.rearrange("(h p) -> p h", h=2))
 
         def project(j0, j1):
             cols = slice(j0, j1)
             for n in range(2):
-                bank = psum.tile([P, HALF], F32, name="bank")
-                for b in range(2):
+                bank = psum.tile([P, HALF], F32, name="out_bank", tag="gate")
+                for b in (1, 0):
                     nc.tensor.matmul_mx(
                         out=bank[:, 0 : j1 - j0],
-                        lhsT=wd_w[:, b, n * P : (n + 1) * P].bitcast(FP8X4),
-                        lhsT_scale=wd_s[:, b, :].bitcast(U8)[:, n * P : (n + 1) * P],
+                        lhsT=sb["wd_w"][:, b, n * P : (n + 1) * P].bitcast(FP8X4),
+                        lhsT_scale=sb["wd_s"][:, b, :].bitcast(U8)[:, n * P : (n + 1) * P],
                         rhs=h_w[:, b, cols].bitcast(FP8X4),
                         rhs_scale=h_s[:, b, cols],
-                        start=(b == 0),
-                        stop=(b == 1),
+                        start=(b == 1),
+                        stop=(b == 0),
                     )
+                bias = sb["bd_sb"][:, n : n + 1]
                 if n == 1 and j1 == S:
                     nc.vector.tensor_scalar(
-                        out=y_sb[:, n, cols],
-                        in0=bank[:, 0 : j1 - j0],
-                        scalar1=bd_sb[:, n : n + 1],
-                        scalar2=None,
-                        op0=mybir.AluOpType.add,
+                        out=y_sb[:, n, cols], in0=bank[:, 0 : j1 - j0], scalar1=bias, scalar2=None, op0=ALU.add
                     )
                 else:
-                    nc.scalar.activation(
-                        out=y_sb[:, n, cols], in_=bank[:, 0 : j1 - j0], func=ACT.Identity, bias=bd_sb[:, n : n + 1]
-                    )
+                    nc.scalar.activation(out=y_sb[:, n, cols], in_=bank[:, 0 : j1 - j0], func=ACT.Identity, bias=bias)
             nc.sync.dma_start(out=out.rearrange("(n p) j -> p n j", n=2)[:, :, cols], in_=y_sb[:, :, cols])
 
-        gather_scales()
-        lower_rows(v_s1, v_s)
+        nc.vector.memset(tab_s[:], 0)
+        nc.vector.memset(wg_s_raw[:], 0)
+        nc.vector.memset(v_s1[:], 0)
+        nc.vector.memset(wd_s[:], 0)
+
+        nc.sync.dma_start(offsets[:], offs)
+        load_wg(0)
+        tab_rows = tab_scales.rearrange("a q t -> (a q) t").bitcast(I32)
+        nc.sync.dma_start(out=tab_s[0:32, :], in_=tab_rows)
+        for q in range(1, 4):
+            nc.sync.dma_start(out=tab_s[32 * q : 32 * q + 4, :], in_=tab_rows[4 * q : 4 * q + 4, :])
+        load_table(0)
+        nc.scalar.dma_start(out=bg_sb[:], in_=bg.rearrange("(b p t) -> p b t", b=2, t=4))
+        nc.scalar.activation(out=warm[:], in_=bg_sb[:, 0, 0:1], func=ACT.Sigmoid)
+        load_scales(wg_s_raw, wg_scales)
+        load_wv(0, 0, 0, QUARTER)
+        load_wv(0, 0, QUARTER, HALF)
+        load_table(1)
+        load_wv(1, 0, 0, QUARTER)
         permute_wg_words(0)
-        permute_wg_scales()
-        lower_rows(wg_s1, wg_s)
+        gather_scales()
+        move_scale_rows()
+        load_wv(1, 0, QUARTER, HALF)
+        load_wv(0, 1, 0, HALF)
+        load_wg(1)
+        load_wv(1, 1, 0, HALF)
+        load_wd()
+
         gather_words(0, 0)
-        late_loads()
+        permute_wg_scales(0)
+        permute_wg_scales(1)
         first = {}
         for h in range(2):
             if h == 1:
-                gather_words(0, 1)
+                gather_words(0, 1, "wg_s_raw")
             for t in range(4):
-                first[h, t] = psum.tile([P, HALF], F32, name="bank")
+                first[h, t] = psum.tile([P, HALF], F32, name="first_bank", tag=("value", "gate")[h])
                 gate_pass(first[h, t], 0, 0, t, h)
-        cast_wv(nc.scalar.copy, 0, 0, 0, P // 2)
-        cast_wv(nc.scalar.copy, 0, 0, P // 2, P)
-        for h in range(2):
-            gather_words(1, h)
-            for t in range(4):
-                gate_pass(first[h, t], 1, 0, t, h)
-                sigmoid(first[h, t], 0, t, h)
+        cast_wv(nc.scalar.copy, 0, 0, (0, QUARTER), 0, QUARTER)
+        cast_wv(nc.scalar.copy, 0, 0, (QUARTER, HALF), QUARTER, HALF)
         quantize_wv(0, 0)
-        cast_wv(nc.vector.tensor_copy, 1, 0, 0, P // 2)
-        cast_wv(nc.vector.tensor_copy, 1, 0, P // 2, P)
-        permute_wg_words(1)
+        gather_words(1, 0)
+        cast_wv(nc.scalar.copy, 1, 0, (0, QUARTER), 0, QUARTER)
+        for t in range(4):
+            gate_pass(first[0, t], 1, 0, t, 0)
+            sigmoid(first[0, t], 0, t, 0)
+        gather_words(1, 1)
+        cast_wv(nc.vector.tensor_copy, 1, 0, (QUARTER, HALF), QUARTER, HALF)
         quantize_wv(1, 0)
+        cast_wv(nc.vector.tensor_copy, 0, 1, (0, HALF), QUARTER, HALF)
+        permute_wg_words(1)
         values(0, 0, 0)
         values(0, 0, 1)
-        cast_wv(nc.scalar.copy, 0, 1)
-        cast_wv(nc.scalar.copy, 1, 1, 0, P // 2)
         values(0, 0, 2)
         values(0, 0, 3)
-        gates(1, 0)
+        for t in range(4):
+            gate_pass(first[1, t], 1, 0, t, 1)
+            sigmoid(first[1, t], 0, t, 1)
+        cast_wv(nc.scalar.copy, 0, 1, (0, HALF), 0, QUARTER)
+        cast_wv(nc.scalar.copy, 1, 1, (0, HALF), 0, QUARTER)
+        cast_wv(nc.vector.tensor_copy, 1, 1, (0, HALF), QUARTER, HALF)
         values(0, 1, 0)
         quantize_h(0, 0, 0, 4)
-        values(0, 1, 1)
+        gates(1, 0)
         quantize_wv(0, 1)
+        values(0, 1, 1)
         values(0, 1, 2)
-        cast_wv(nc.vector.tensor_copy, 1, 1, P // 2, P)
         values(0, 1, 3)
         quantize_wv(1, 1)
-        gates(1, 1)
         values(1, 0, 0)
-        quantize_h(0, 1, 0, 4)
         values(1, 0, 1)
         values(1, 0, 2)
         values(1, 0, 3)
+        quantize_h(0, 1, 0, 4)
+        gates(1, 1)
         values(1, 1, 0)
-        quantize_h(1, 0, 0, 4)
         values(1, 1, 1)
-        project(0, 512)
+        quantize_h(1, 0, 0, 2)
+        quantize_h(1, 0, 2, 4)
+        project(0, 256)
         values(1, 1, 2)
         quantize_h(1, 1, 0, 2)
         values(1, 1, 3)
+        project(256, 512)
         project(512, 768)
         quantize_h(1, 1, 2, 3)
         project(768, 896)

@@ -19,6 +19,8 @@ ALU = mybir.AluOpType
 P = 128
 HALF = 512
 QUARTER = 256
+TAIL = 384
+BANKS_PER_SET = 4
 
 
 def tile_list_clicked_item_candidates_kernel(
@@ -27,165 +29,146 @@ def tile_list_clicked_item_candidates_kernel(
     nc = tc.nc
     with ExitStack() as ctx:
         keep = ctx.enter_context(tc.tile_pool(name="keep", bufs=1))
-        psum = ctx.enter_context(tc.psum_pool(name="psum", bufs=4))
-        sb = {}
+        psum = ctx.enter_context(tc.psum_pool(name="psum", bufs=BANKS_PER_SET))
 
-        def new(name, shape, dtype, after=None):
-            tag = name if after is None else sb[after + " tag"]
-            sb[name] = keep.tile(shape, dtype, name=name, tag=tag, align_bytes=64)
-            sb[name + " tag"] = tag
-            return sb[name]
+        def sbuf(name, shape, dtype, tag=None):
+            return keep.tile(shape, dtype, name=name, tag=tag or name, align_bytes=64)
 
+        pairs = [(x, y) for x in range(2) for y in range(2)]
         offsets = keep.tile([P, S // 16], U16, name="offsets")
-        bg_sb = new("bg_sb", [P, 2, 4], F32)
-        warm = new("warm", [P, 1], F32)
-        wg_w = new("wg_w", [P, 2, 2 * H], U8)
-        wv_w = new("wv_w", [P, 2, H], U32)
-        wv_s = new("wv_s", [P, 2, H], U8)
-        h_w = new("h_w", [P, 2, S], U32)
-        h_s = new("h_s", [P, 2, S], U8)
-        y_sb = new("y_sb", [P, 2, S], F32)
-        v_s0 = new("v_s0", [P, S], U8)
-        v_s1 = new("v_s1", [P, S // 4], I32)
-        tab_s = new("tab_s", [P, T // 4], I32)
-        wd_s = new("wd_s", [P, 2, N // 4], I32)
-        wg_s_raw = new("wg_s_raw", [P, 2, H // 4], I32)
-        for b in range(2):
-            for h in range(2):
-                new("gate%d%d" % (b, h), [P, 4, HALF], F32)
-                new("h_bf%d%d" % (b, h), [P, 4 * HALF], BF16)
-                new("wv_bf%d%d" % (b, h), [P, 4 * HALF], BF16)
+        bg_sb = sbuf("bg_sb", [P, 2, 4], F32)
+        bd_sb = sbuf("bd_sb", [P, 2], F32)
+        warm = sbuf("warm", [P, 1], F32)
+        tab_w = [sbuf("tab_w%d" % a, [P, T], I32) for a in range(2)]
+        tab_s = sbuf("tab_s", [P, T // 4], I32)
+        v_s = sbuf("v_s", [P, S], U8)
+        v_s_moved = sbuf("v_s_moved", [P, S // 4], I32)
+        v_w = {}
+        wg_w_raw = [sbuf("wg_w_raw%d" % b, [P, 2, HALF // 2], I32) for b in range(2)]
+        wg_s_raw = sbuf("wg_s_raw", [P, 2, H // 4], I32)
+        wg_w = [sbuf("wg_w%d" % b, [P, 2, 2 * HALF], U8) for b in range(2)]
+        wg_s = [sbuf("wg_s%d" % b, [P, 2, HALF], U8) for b in range(2)]
+        wv_raw = {(a, b): sbuf("wv_raw%d%d" % (a, b), [P, 4 * HALF], F32) for a, b in pairs}
+        wv_bf = {(a, b): sbuf("wv_bf%d%d" % (a, b), [P, 4 * HALF], BF16) for a, b in pairs}
+        wv_w = sbuf("wv_w", [P, 2, H], U32)
+        wv_s = sbuf("wv_s", [P, 2, H], U8)
+        gate = {(b, u): sbuf("gate%d%d" % (b, u), [P, 4, HALF], F32) for b, u in pairs}
+        h_bf = {(b, u): sbuf("h_bf%d%d" % (b, u), [P, 4 * HALF], BF16) for b, u in pairs}
+        h_w = sbuf("h_w", [P, 2, S], U32)
+        h_s = sbuf("h_s", [P, 2, S], U8)
+        wd_w = sbuf("wd_w", [P, 2, N], I32)
+        wd_s = sbuf("wd_s", [P, 2, N // 4], I32)
+        y_sb = sbuf("y_sb", [P, 2, S], F32)
 
-        def load_scales(tile, src):
-            for q in range(4):
-                nc.sync.dma_start(
-                    out=tile[32 * q : 32 * q + 4, :, :],
-                    in_=src[:, 4 * q : 4 * q + 4, :].bitcast(I32).rearrange("a r w -> r a w"),
-                )
+        def scale_rows(scales, s):
+            return scales.bitcast(I32).rearrange("a (q s) w -> s q a w", s=4)[s]
 
-        def load_table(a):
-            tile = new("tab_w%d" % a, [P, T], I32)
-            nc.sync.dma_start(out=tile[:], in_=tab_words[a].rearrange("p n t -> p (n t)").bitcast(I32))
+        def load_planes(planes, scales):
+            for s in range(4):
+                nc.sync.dma_start(out=planes[s:P:32, :, :], in_=scale_rows(scales, s))
 
-        def load_wg(b, after=None):
-            tile = new("wg_w_raw%d" % b, [P, 2, H // 4], I32, after)
-            nc.sync.dma_start(
-                out=tile[:],
-                in_=wg_words.bitcast(I32)[:, :, b * (H // 4) : (b + 1) * (H // 4)].rearrange("a p w -> p a w"),
-            )
+        def load_table_scales():
+            for s in range(4):
+                nc.sync.dma_start(out=tab_s[s:P:16, :], in_=scale_rows(tab_scales, s))
 
-        def load_wv(a, b, c0, c1, after=None):
-            if c0 == 0:
-                new("wv_raw%d%d" % (a, b), [P, 4 * HALF], F32, after)
-            nc.sync.dma_start(
-                out=sb["wv_raw%d%d" % (a, b)][:, 4 * c0 : 4 * c1].rearrange("p (j c) -> p j c", j=4),
-                in_=wv[a * HALF : (a + 1) * HALF, b * HALF + c0 : b * HALF + c1].rearrange("(p j) c -> p j c", j=4),
-            )
+        def load_table_words(a):
+            nc.sync.dma_start(out=tab_w[a][:], in_=tab_words[a].rearrange("p n i -> p (n i)").bitcast(I32))
 
-        def cast_wv(copy, a, b, piece, c0, c1):
-            dst = sb["wv_bf%d%d" % (a, b)][:].rearrange("p (t m j) -> p m j t", t=4, j=4)[:, c0 // 4 : c1 // 4, :, :]
-            raw = sb["wv_raw%d%d" % (a, b)][:, 4 * piece[0] : 4 * piece[1]].rearrange("p (j m t) -> p m j t", j=4, t=4)
-            src = raw[:, (c0 - piece[0]) // 4 : (c1 - piece[0]) // 4, :, :]
+        def load_wg_words(b):
+            words = wg_words.bitcast(I32)[:, :, b * (HALF // 2) : (b + 1) * (HALF // 2)]
+            nc.sync.dma_start(out=wg_w_raw[b][:], in_=words.rearrange("a p w -> p a w"))
+
+        def wv_piece(a, b, c0, c1):
+            return wv_raw[a, b][:, 4 * c0 : 4 * c1].rearrange("p (i c) -> p i c", i=4)
+
+        def load_wv(a, b, c0, c1):
+            rows = wv[a * HALF : (a + 1) * HALF, b * HALF + c0 : b * HALF + c1]
+            nc.sync.dma_start(out=wv_piece(a, b, c0, c1), in_=rows.rearrange("(p i) c -> p i c", i=4))
+
+        def round_wv(copy, a, b, loaded, c0, c1):
+            dst = wv_bf[a, b][:].rearrange("p (t m i) -> p m i t", t=4, i=4)[:, c0 // 4 : c1 // 4, :, :]
+            src = wv_piece(a, b, *loaded)[:, :, c0 - loaded[0] : c1 - loaded[0]].rearrange("p i (m t) -> p m i t", t=4)
             for t in (0, 2):
                 copy(out=dst[:, :, :, t : t + 2], in_=src[:, :, :, t : t + 2])
 
-        def quantize_wv(a, b):
-            cols = slice(b * HALF, (b + 1) * HALF)
+        def quantize_wv(a, b, t0, t1):
+            cols = slice(b * HALF + t0 * P, b * HALF + t1 * P)
             nc.vector.quantize_mx(
-                out=wv_w[:, a, cols].bitcast(FP8X4), scales=wv_s[:, a, cols], in_=sb["wv_bf%d%d" % (a, b)][:]
+                out=wv_w[:, a, cols].bitcast(FP8X4), scales=wv_s[:, a, cols], in_=wv_bf[a, b][:, t0 * HALF : t1 * HALF]
             )
 
-        def permute_wg_words(b):
+        def reorder_wg_words(b):
             nc.vector.tensor_copy(
-                out=wg_w[:, :, 2 * b * HALF : 2 * (b + 1) * HALF].bitcast(U16).rearrange("p a (t m) -> p a t m", t=4),
-                in_=sb["wg_w_raw%d" % b][:].bitcast(U16).rearrange("p a (m t) -> p a t m", t=4),
+                out=wg_w[b][:].bitcast(U16).rearrange("p a (t m) -> p a t m", t=4),
+                in_=wg_w_raw[b][:].bitcast(U16).rearrange("p a (m t) -> p a t m", t=4),
             )
 
-        def permute_wg_scales(b, after=None):
-            tile = new("wg_s%d" % b, [P, 2, HALF], U8, after)
+        def reorder_wg_scales(b):
             nc.vector.tensor_copy(
-                out=tile[:].rearrange("p a (t m) -> p a t m", t=4),
+                out=wg_s[b][:].rearrange("p a (t m) -> p a t m", t=4),
                 in_=wg_s_raw[:].bitcast(U8)[:, :, b * HALF : (b + 1) * HALF].rearrange("p a (m t) -> p a t m", t=4),
             )
 
-        def picks(h):
-            return offsets[:, h * (HALF // 16) : (h + 1) * (HALF // 16)]
-
         def gather_scales():
-            nc.vector.tensor_copy(out=v_s0[:], in_=tab_s[:].bitcast(U8).indirect(offsets[:]))
+            nc.vector.tensor_copy(out=v_s[:], in_=tab_s[:].bitcast(U8).indirect(offsets[:]))
+            for s in range(4):
+                nc.sync.dma_start(out=v_s_moved[s:P:32, :], in_=v_s[16 + s : P : 32, :].bitcast(I32))
 
-        def move_scale_rows():
-            for q in range(4):
-                nc.sync.dma_start(out=v_s1[32 * q : 32 * q + 4, :], in_=v_s0[16 + 4 * q : 20 + 4 * q, :].bitcast(I32))
+        def gather_words(a, u, tag=None):
+            v_w[a, u] = sbuf("v_w%d%d" % (a, u), [P, HALF], U32, tag)
+            picks = offsets[:, u * (HALF // 16) : (u + 1) * (HALF // 16)]
+            nc.vector.tensor_copy(out=v_w[a, u][:], in_=tab_w[a][:].bitcast(U32).indirect(picks))
 
-        def gather_words(a, h, after=None):
-            tile = new("v_w%d%d" % (a, h), [P, HALF], U32, after)
-            nc.vector.tensor_copy(out=tile[:], in_=sb["tab_w%d" % a][:].bitcast(U32).indirect(picks(h)))
+        def v_plane(a, j0, j1):
+            return (v_s[:] if a == 0 else v_s_moved[:].bitcast(U8))[:, j0:j1]
 
-        def v_scales(a, h, c0, c1):
-            plane = v_s0[:] if a == 0 else v_s1[:].bitcast(U8)
-            return plane[:, h * HALF + c0 : h * HALF + c1]
-
-        def gate_pass(bank, a, b, t, h):
-            c0 = b * HALF + t * P
+        def gate_pass(bank, a, b, t, u):
             nc.tensor.matmul_mx(
                 out=bank[:],
-                lhsT=wg_w[:, a, 2 * c0 : 2 * c0 + 2 * P].bitcast(FP4X4),
-                lhsT_scale=sb["wg_s%d" % b][:, a, t * P : (t + 1) * P],
-                rhs=sb["v_w%d%d" % (a, h)][:].bitcast(FP8X4),
-                rhs_scale=v_scales(a, h, 0, HALF),
+                lhsT=wg_w[b][:, a, 2 * t * P : 2 * (t + 1) * P].bitcast(FP4X4),
+                lhsT_scale=wg_s[b][:, a, t * P : (t + 1) * P],
+                rhs=v_w[a, u][:].bitcast(FP8X4),
+                rhs_scale=v_plane(a, u * HALF, (u + 1) * HALF),
                 start=(a == 0),
                 stop=(a == 1),
             )
 
-        def sigmoid(bank, b, t, h):
-            nc.scalar.activation(
-                out=sb["gate%d%d" % (b, h)][:, t, :], in_=bank[:], func=ACT.Sigmoid, bias=bg_sb[:, b, t : t + 1]
-            )
+        def sigmoid(bank, b, t, u):
+            nc.scalar.activation(out=gate[b, u][:, t, :], in_=bank[:], func=ACT.Sigmoid, bias=bg_sb[:, b, t : t + 1])
 
-        def gates(b, h):
+        def gates(b, u):
             for t in range(4):
                 bank = psum.tile([P, HALF], F32, name="gate_bank", tag="gate")
                 for a in range(2):
-                    gate_pass(bank, a, b, t, h)
-                sigmoid(bank, b, t, h)
+                    gate_pass(bank, a, b, t, u)
+                sigmoid(bank, b, t, u)
 
-        def values(b, h, c):
+        def gated_values(b, u, c):
             bank = psum.tile([P, HALF], F32, name="value_bank", tag="value")
             for t in range(4):
-                c0 = b * HALF + t * P
+                cols = slice(b * HALF + t * P, b * HALF + (t + 1) * P)
                 for a in range(2):
                     nc.tensor.matmul_mx(
                         out=bank[:, t * P : (t + 1) * P],
-                        lhsT=wv_w[:, a, c0 : c0 + P].bitcast(FP8X4),
-                        lhsT_scale=wv_s[:, a, c0 : c0 + P],
-                        rhs=sb["v_w%d%d" % (a, h)][:, c * P : (c + 1) * P].bitcast(FP8X4),
-                        rhs_scale=v_scales(a, h, c * P, (c + 1) * P),
+                        lhsT=wv_w[:, a, cols].bitcast(FP8X4),
+                        lhsT_scale=wv_s[:, a, cols],
+                        rhs=v_w[a, u][:, c * P : (c + 1) * P].bitcast(FP8X4),
+                        rhs_scale=v_plane(a, u * HALF + c * P, u * HALF + (c + 1) * P),
                         start=(a == 0),
                         stop=(a == 1),
                     )
             nc.vector.tensor_tensor(
-                out=sb["h_bf%d%d" % (b, h)][:, c * HALF : (c + 1) * HALF].rearrange("p (c i t) -> p c t i", i=2, t=4),
-                in0=bank[:].rearrange("p (t c i) -> p c t i", t=4, i=2),
-                in1=sb["gate%d%d" % (b, h)][:, :, c * P : (c + 1) * P].rearrange("p t (c i) -> p c t i", i=2),
+                out=h_bf[b, u][:, c * HALF : (c + 1) * HALF].rearrange("p (j e t) -> p j t e", e=2, t=4),
+                in0=bank[:].rearrange("p (t j e) -> p j t e", t=4, e=2),
+                in1=gate[b, u][:, :, c * P : (c + 1) * P].rearrange("p t (j e) -> p j t e", e=2),
                 op=ALU.mult,
             )
 
-        def quantize_h(b, h, c0, c1):
-            cols = slice(h * HALF + c0 * P, h * HALF + c1 * P)
+        def quantize_h(b, u, c0, c1):
+            cols = slice(u * HALF + c0 * P, u * HALF + c1 * P)
             nc.vector.quantize_mx(
-                out=h_w[:, b, cols].bitcast(FP8X4),
-                scales=h_s[:, b, cols],
-                in_=sb["h_bf%d%d" % (b, h)][:, c0 * HALF : c1 * HALF],
+                out=h_w[:, b, cols].bitcast(FP8X4), scales=h_s[:, b, cols], in_=h_bf[b, u][:, c0 * HALF : c1 * HALF]
             )
-
-        def load_wd():
-            wd_w = new("wd_w", [P, 2, N], I32)
-            bd_sb = new("bd_sb", [P, 2], F32)
-            nc.sync.dma_start(out=wd_w[:], in_=wd_words.rearrange("a p n t -> p a (n t)").bitcast(I32))
-            load_scales(wd_s, wd_scales)
-            with nc.allow_non_contiguous_dma(reason="one bias value for each partition"):
-                nc.sync.dma_start(out=bd_sb[:], in_=bd.rearrange("(h p) -> p h", h=2))
 
         def project(j0, j1):
             cols = slice(j0, j1)
@@ -194,14 +177,14 @@ def tile_list_clicked_item_candidates_kernel(
                 for b in (1, 0):
                     nc.tensor.matmul_mx(
                         out=bank[:, 0 : j1 - j0],
-                        lhsT=sb["wd_w"][:, b, n * P : (n + 1) * P].bitcast(FP8X4),
-                        lhsT_scale=sb["wd_s"][:, b, :].bitcast(U8)[:, n * P : (n + 1) * P],
+                        lhsT=wd_w[:, b, n * P : (n + 1) * P].bitcast(FP8X4),
+                        lhsT_scale=wd_s[:, b, :].bitcast(U8)[:, n * P : (n + 1) * P],
                         rhs=h_w[:, b, cols].bitcast(FP8X4),
                         rhs_scale=h_s[:, b, cols],
                         start=(b == 1),
                         stop=(b == 0),
                     )
-                bias = sb["bd_sb"][:, n : n + 1]
+                bias = bd_sb[:, n : n + 1]
                 if n == 1 and j1 == S:
                     nc.vector.tensor_scalar(
                         out=y_sb[:, n, cols], in0=bank[:, 0 : j1 - j0], scalar1=bias, scalar2=None, op0=ALU.add
@@ -210,92 +193,88 @@ def tile_list_clicked_item_candidates_kernel(
                     nc.scalar.activation(out=y_sb[:, n, cols], in_=bank[:, 0 : j1 - j0], func=ACT.Identity, bias=bias)
             nc.sync.dma_start(out=out.rearrange("(n p) j -> p n j", n=2)[:, :, cols], in_=y_sb[:, :, cols])
 
-        nc.vector.memset(tab_s[:], 0)
-        nc.vector.memset(wg_s_raw[:], 0)
-        nc.vector.memset(v_s1[:], 0)
-        nc.vector.memset(wd_s[:], 0)
+        for planes in (tab_s, wg_s_raw, v_s_moved, wd_s):
+            nc.vector.memset(planes[:], 0)
 
         nc.sync.dma_start(offsets[:], offs)
-        load_wg(0)
-        tab_rows = tab_scales.rearrange("a q t -> (a q) t").bitcast(I32)
-        nc.sync.dma_start(out=tab_s[0:32, :], in_=tab_rows)
-        for q in range(1, 4):
-            nc.sync.dma_start(out=tab_s[32 * q : 32 * q + 4, :], in_=tab_rows[4 * q : 4 * q + 4, :])
-        load_table(0)
+        load_wg_words(0)
+        load_table_scales()
+        load_table_words(0)
         nc.scalar.dma_start(out=bg_sb[:], in_=bg.rearrange("(b p t) -> p b t", b=2, t=4))
         nc.scalar.activation(out=warm[:], in_=bg_sb[:, 0, 0:1], func=ACT.Sigmoid)
-        load_scales(wg_s_raw, wg_scales)
+        load_planes(wg_s_raw, wg_scales)
         load_wv(0, 0, 0, QUARTER)
+        load_table_words(1)
         load_wv(0, 0, QUARTER, HALF)
-        load_table(1)
-        load_wv(1, 0, 0, QUARTER)
-        permute_wg_words(0)
+        reorder_wg_words(0)
         gather_scales()
-        move_scale_rows()
-        load_wv(1, 0, QUARTER, HALF)
+        load_wg_words(1)
+        load_wv(1, 0, 0, TAIL)
+        load_wv(1, 0, TAIL, HALF)
         load_wv(0, 1, 0, HALF)
-        load_wg(1)
         load_wv(1, 1, 0, HALF)
-        load_wd()
+        nc.sync.dma_start(out=wd_w[:], in_=wd_words.rearrange("a p n i -> p a (n i)").bitcast(I32))
+        load_planes(wd_s, wd_scales)
+        with nc.allow_non_contiguous_dma(reason="one bias value for each partition"):
+            nc.sync.dma_start(out=bd_sb[:], in_=bd.rearrange("(n p) -> p n", n=2))
 
         gather_words(0, 0)
-        permute_wg_scales(0)
-        permute_wg_scales(1)
-        first = {}
-        for h in range(2):
-            if h == 1:
+        reorder_wg_scales(0)
+        reorder_wg_scales(1)
+        opened = {}
+        for u in range(2):
+            if u == 1:
                 gather_words(0, 1, "wg_s_raw")
             for t in range(4):
-                first[h, t] = psum.tile([P, HALF], F32, name="first_bank", tag=("value", "gate")[h])
-                gate_pass(first[h, t], 0, 0, t, h)
-        cast_wv(nc.scalar.copy, 0, 0, (0, QUARTER), 0, QUARTER)
-        cast_wv(nc.scalar.copy, 0, 0, (QUARTER, HALF), QUARTER, HALF)
-        quantize_wv(0, 0)
-        gather_words(1, 0)
-        cast_wv(nc.scalar.copy, 1, 0, (0, QUARTER), 0, QUARTER)
-        for t in range(4):
-            gate_pass(first[0, t], 1, 0, t, 0)
-            sigmoid(first[0, t], 0, t, 0)
-        gather_words(1, 1)
-        cast_wv(nc.vector.tensor_copy, 1, 0, (QUARTER, HALF), QUARTER, HALF)
-        quantize_wv(1, 0)
-        cast_wv(nc.vector.tensor_copy, 0, 1, (0, HALF), QUARTER, HALF)
-        permute_wg_words(1)
-        values(0, 0, 0)
-        values(0, 0, 1)
-        values(0, 0, 2)
-        values(0, 0, 3)
-        for t in range(4):
-            gate_pass(first[1, t], 1, 0, t, 1)
-            sigmoid(first[1, t], 0, t, 1)
-        cast_wv(nc.scalar.copy, 0, 1, (0, HALF), 0, QUARTER)
-        cast_wv(nc.scalar.copy, 1, 1, (0, HALF), 0, QUARTER)
-        cast_wv(nc.vector.tensor_copy, 1, 1, (0, HALF), QUARTER, HALF)
-        values(0, 1, 0)
-        quantize_h(0, 0, 0, 4)
+                opened[u, t] = psum.tile([P, HALF], F32, name="opened_bank", tag=("gate", "value")[u])
+                gate_pass(opened[u, t], 0, 0, t, u)
+        round_wv(nc.scalar.copy, 0, 0, (0, QUARTER), 0, QUARTER)
+        round_wv(nc.scalar.copy, 0, 0, (QUARTER, HALF), QUARTER, HALF)
+        for u in range(2):
+            gather_words(1, u)
+        for u in range(2):
+            for t in range(4):
+                gate_pass(opened[u, t], 1, 0, t, u)
+                sigmoid(opened[u, t], 0, t, u)
+
+        reorder_wg_words(1)
+        quantize_wv(0, 0, 0, 4)
+        round_wv(nc.vector.tensor_copy, 1, 0, (0, TAIL), 0, TAIL)
+        round_wv(nc.vector.tensor_copy, 1, 0, (TAIL, HALF), TAIL, HALF)
+        quantize_wv(1, 0, 0, 2)
+        quantize_wv(1, 0, 2, 4)
+
+        round_wv(nc.scalar.copy, 0, 1, (0, HALF), 0, QUARTER)
+        round_wv(nc.vector.tensor_copy, 0, 1, (0, HALF), QUARTER, HALF)
+        for c in range(3):
+            gated_values(0, 0, c)
         gates(1, 0)
-        quantize_wv(0, 1)
-        values(0, 1, 1)
-        values(0, 1, 2)
-        values(0, 1, 3)
-        quantize_wv(1, 1)
-        values(1, 0, 0)
-        values(1, 0, 1)
-        values(1, 0, 2)
-        values(1, 0, 3)
-        quantize_h(0, 1, 0, 4)
+        gated_values(0, 0, 3)
+        round_wv(nc.scalar.copy, 1, 1, (0, HALF), 0, QUARTER)
+        round_wv(nc.scalar.copy, 1, 1, (0, HALF), QUARTER, HALF)
+        gated_values(0, 1, 0)
+        gated_values(0, 1, 1)
+        quantize_wv(0, 1, 0, 4)
+        gated_values(0, 1, 2)
+        quantize_h(0, 0, 0, 4)
+        gated_values(0, 1, 3)
         gates(1, 1)
-        values(1, 1, 0)
-        values(1, 1, 1)
+        quantize_h(0, 1, 0, 4)
+        quantize_wv(1, 1, 0, 4)
+
+        for c in range(4):
+            gated_values(1, 0, c)
+        gated_values(1, 1, 0)
+        gated_values(1, 1, 1)
         quantize_h(1, 0, 0, 2)
         quantize_h(1, 0, 2, 4)
-        project(0, 256)
-        values(1, 1, 2)
+        project(0, 2 * P)
+        gated_values(1, 1, 2)
         quantize_h(1, 1, 0, 2)
-        values(1, 1, 3)
-        project(256, 512)
-        project(512, 768)
+        gated_values(1, 1, 3)
         quantize_h(1, 1, 2, 3)
-        project(768, 896)
+        project(2 * P, 4 * P)
+        project(4 * P, 6 * P)
+        project(6 * P, 7 * P)
         quantize_h(1, 1, 3, 4)
-        project(896, 1024)
+        project(7 * P, 8 * P)

@@ -20,7 +20,7 @@ P = 128
 HALF = 512
 QUARTER = 256
 TAIL = 384
-BANKS_PER_SET = 4
+SHIFT = 16
 
 
 def tile_list_clicked_item_candidates_kernel(
@@ -29,7 +29,8 @@ def tile_list_clicked_item_candidates_kernel(
     nc = tc.nc
     with ExitStack() as ctx:
         keep = ctx.enter_context(tc.tile_pool(name="keep", bufs=1))
-        psum = ctx.enter_context(tc.psum_pool(name="psum", bufs=BANKS_PER_SET))
+        psum = ctx.enter_context(tc.psum_pool(name="psum", bufs=1))
+        banks = [psum.tile([P, HALF], F32, name="bank%d" % i) for i in range(8)]
 
         def sbuf(name, shape, dtype, tag=None):
             return keep.tile(shape, dtype, name=name, tag=tag or name, align_bytes=64)
@@ -38,7 +39,7 @@ def tile_list_clicked_item_candidates_kernel(
         offsets = keep.tile([P, S // 16], U16, name="offsets")
         bg_sb = sbuf("bg_sb", [P, 2, 4], F32)
         bd_sb = sbuf("bd_sb", [P, 2], F32)
-        warm = sbuf("warm", [P, 1], F32)
+        warm = sbuf("warm", [P, 2], F32)
         tab_w = [sbuf("tab_w%d" % a, [P, T], I32) for a in range(2)]
         tab_s = sbuf("tab_s", [P, T // 4], I32)
         v_s = sbuf("v_s", [P, S], U8)
@@ -48,12 +49,19 @@ def tile_list_clicked_item_candidates_kernel(
         wg_s_raw = sbuf("wg_s_raw", [P, 2, H // 4], I32)
         wg_w = [sbuf("wg_w%d" % b, [P, 2, 2 * HALF], U8) for b in range(2)]
         wg_s = [sbuf("wg_s%d" % b, [P, 2, HALF], U8) for b in range(2)]
-        wv_raw = {(a, b): sbuf("wv_raw%d%d" % (a, b), [P, 4 * HALF], F32) for a, b in pairs}
-        wv_bf = {(a, b): sbuf("wv_bf%d%d" % (a, b), [P, 4 * HALF], BF16) for a, b in pairs}
+        wv_raw = {(a, b): sbuf("wv_raw%d%d" % (a, b), [P, 4 * HALF], F32)[:] for a, b in pairs[:3]}
+        shared = sbuf("shared", [P, 8 * HALF], F32)
+        wv_raw[1, 1] = shared[:, 2 * HALF : 6 * HALF]
+        wv_bf = {(a, b): sbuf("wv_bf%d%d" % (a, b), [P, 4 * HALF], BF16)[:] for a, b in pairs[:3]}
+        shared_bf = sbuf("shared_bf", [P, 6 * HALF], BF16)
+        wv_bf[1, 1] = shared_bf[:, 2 * HALF : 6 * HALF]
         wv_w = sbuf("wv_w", [P, 2, H], U32)
         wv_s = sbuf("wv_s", [P, 2, H], U8)
-        gate = {(b, u): sbuf("gate%d%d" % (b, u), [P, 4, HALF], F32) for b, u in pairs}
-        h_bf = {(b, u): sbuf("h_bf%d%d" % (b, u), [P, 4 * HALF], BF16) for b, u in pairs}
+        gate = {(b, u): sbuf("gate%d%d" % (b, u), [P, 4, HALF], F32)[:] for b, u in pairs[:2]}
+        for u in range(2):
+            gate[1, u] = shared[:, 4 * u * HALF : 4 * (u + 1) * HALF].rearrange("p (t j) -> p t j", t=4)
+        h_bf = {(b, u): sbuf("h_bf%d%d" % (b, u), [P, 4 * HALF], BF16)[:] for b, u in ((0, 0), (1, 0), (1, 1))}
+        h_bf[0, 1] = shared_bf[:, 0 : 4 * HALF]
         h_w = sbuf("h_w", [P, 2, S], U32)
         h_s = sbuf("h_s", [P, 2, S], U8)
         wd_w = sbuf("wd_w", [P, 2, N], I32)
@@ -81,15 +89,14 @@ def tile_list_clicked_item_candidates_kernel(
         def wv_piece(a, b, c0, c1):
             return wv_raw[a, b][:, 4 * c0 : 4 * c1].rearrange("p (i c) -> p i c", i=4)
 
-        def load_wv(a, b, c0, c1):
+        def load_wv(a, b, c0=0, c1=HALF):
             rows = wv[a * HALF : (a + 1) * HALF, b * HALF + c0 : b * HALF + c1]
             nc.sync.dma_start(out=wv_piece(a, b, c0, c1), in_=rows.rearrange("(p i) c -> p i c", i=4))
 
-        def round_wv(copy, a, b, loaded, c0, c1):
+        def round_wv(copy, a, b, t0, c0=0, c1=HALF):
             dst = wv_bf[a, b][:].rearrange("p (t m i) -> p m i t", t=4, i=4)[:, c0 // 4 : c1 // 4, :, :]
-            src = wv_piece(a, b, *loaded)[:, :, c0 - loaded[0] : c1 - loaded[0]].rearrange("p i (m t) -> p m i t", t=4)
-            for t in (0, 2):
-                copy(out=dst[:, :, :, t : t + 2], in_=src[:, :, :, t : t + 2])
+            src = wv_piece(a, b, c0, c1).rearrange("p i (m t) -> p m i t", t=4)
+            copy(out=dst[:, :, :, t0 : t0 + 2], in_=src[:, :, :, t0 : t0 + 2])
 
         def quantize_wv(a, b, t0, t1):
             cols = slice(b * HALF + t0 * P, b * HALF + t1 * P)
@@ -103,21 +110,20 @@ def tile_list_clicked_item_candidates_kernel(
                 in_=wg_w_raw[b][:].bitcast(U16).rearrange("p a (m t) -> p a t m", t=4),
             )
 
-        def reorder_wg_scales(b):
-            nc.vector.tensor_copy(
-                out=wg_s[b][:].rearrange("p a (t m) -> p a t m", t=4),
-                in_=wg_s_raw[:].bitcast(U8)[:, :, b * HALF : (b + 1) * HALF].rearrange("p a (m t) -> p a t m", t=4),
+        def reorder_wg_scales(b, a0, a1):
+            nc.gpsimd.tensor_copy(
+                out=wg_s[b][:, a0:a1, :].rearrange("p a (t m) -> p a t m", t=4),
+                in_=wg_s_raw[:].bitcast(U8)[:, a0:a1, b * HALF : (b + 1) * HALF].rearrange("p a (m t) -> p a t m", t=4),
             )
 
         def gather_scales():
             nc.vector.tensor_copy(out=v_s[:], in_=tab_s[:].bitcast(U8).indirect(offsets[:]))
-            for s in range(4):
-                nc.sync.dma_start(out=v_s_moved[s:P:32, :], in_=v_s[16 + s : P : 32, :].bitcast(I32))
+            nc.sync.dma_start(out=v_s_moved[0 : P - SHIFT, :], in_=v_s[SHIFT:P, :].bitcast(I32))
 
-        def gather_words(a, u, tag=None):
-            v_w[a, u] = sbuf("v_w%d%d" % (a, u), [P, HALF], U32, tag)
+        def gather_words(a, u, dst):
+            v_w[a, u] = dst
             picks = offsets[:, u * (HALF // 16) : (u + 1) * (HALF // 16)]
-            nc.vector.tensor_copy(out=v_w[a, u][:], in_=tab_w[a][:].bitcast(U32).indirect(picks))
+            nc.vector.tensor_copy(out=dst, in_=tab_w[a][:].bitcast(U32).indirect(picks))
 
         def v_plane(a, j0, j1):
             return (v_s[:] if a == 0 else v_s_moved[:].bitcast(U8))[:, j0:j1]
@@ -127,7 +133,7 @@ def tile_list_clicked_item_candidates_kernel(
                 out=bank[:],
                 lhsT=wg_w[b][:, a, 2 * t * P : 2 * (t + 1) * P].bitcast(FP4X4),
                 lhsT_scale=wg_s[b][:, a, t * P : (t + 1) * P],
-                rhs=v_w[a, u][:].bitcast(FP8X4),
+                rhs=v_w[a, u].bitcast(FP8X4),
                 rhs_scale=v_plane(a, u * HALF, (u + 1) * HALF),
                 start=(a == 0),
                 stop=(a == 1),
@@ -136,26 +142,27 @@ def tile_list_clicked_item_candidates_kernel(
         def sigmoid(bank, b, t, u):
             nc.scalar.activation(out=gate[b, u][:, t, :], in_=bank[:], func=ACT.Sigmoid, bias=bg_sb[:, b, t : t + 1])
 
-        def gates(b, u):
-            for t in range(4):
-                bank = psum.tile([P, HALF], F32, name="gate_bank", tag="gate")
+        def gate_sums(b, u, ts, used):
+            for t in ts:
                 for a in range(2):
-                    gate_pass(bank, a, b, t, u)
-                sigmoid(bank, b, t, u)
+                    gate_pass(banks[used[t]], a, b, t, u)
 
-        def gated_values(b, u, c):
-            bank = psum.tile([P, HALF], F32, name="value_bank", tag="value")
+        def sigmoids(b, u, used, ts=range(4)):
+            for t in ts:
+                sigmoid(banks[used[t]], b, t, u)
+
+        def gated_values(b, u, c, bank):
             for t in range(4):
                 cols = slice(b * HALF + t * P, b * HALF + (t + 1) * P)
-                for a in range(2):
+                for a in (1, 0):
                     nc.tensor.matmul_mx(
                         out=bank[:, t * P : (t + 1) * P],
                         lhsT=wv_w[:, a, cols].bitcast(FP8X4),
                         lhsT_scale=wv_s[:, a, cols],
                         rhs=v_w[a, u][:, c * P : (c + 1) * P].bitcast(FP8X4),
                         rhs_scale=v_plane(a, u * HALF + c * P, u * HALF + (c + 1) * P),
-                        start=(a == 0),
-                        stop=(a == 1),
+                        start=(a == 1),
+                        stop=(a == 0),
                     )
             nc.vector.tensor_tensor(
                 out=h_bf[b, u][:, c * HALF : (c + 1) * HALF].rearrange("p (j e t) -> p j t e", e=2, t=4),
@@ -170,111 +177,138 @@ def tile_list_clicked_item_candidates_kernel(
                 out=h_w[:, b, cols].bitcast(FP8X4), scales=h_s[:, b, cols], in_=h_bf[b, u][:, c0 * HALF : c1 * HALF]
             )
 
-        def project(j0, j1):
+        def project_pass(b, j0, j1, used, first=0):
+            for n in range(2):
+                nc.tensor.matmul_mx(
+                    out=banks[used[n]][:, 0 : j1 - j0],
+                    lhsT=wd_w[:, b, n * P : (n + 1) * P].bitcast(FP8X4),
+                    lhsT_scale=wd_s[:, b, :].bitcast(U8)[:, n * P : (n + 1) * P],
+                    rhs=h_w[:, b, j0:j1].bitcast(FP8X4),
+                    rhs_scale=h_s[:, b, j0:j1],
+                    start=(b == first),
+                    stop=(b != first),
+                )
+
+        def store(j0, j1, used):
             cols = slice(j0, j1)
             for n in range(2):
-                bank = psum.tile([P, HALF], F32, name="out_bank", tag="gate")
-                for b in (1, 0):
-                    nc.tensor.matmul_mx(
-                        out=bank[:, 0 : j1 - j0],
-                        lhsT=wd_w[:, b, n * P : (n + 1) * P].bitcast(FP8X4),
-                        lhsT_scale=wd_s[:, b, :].bitcast(U8)[:, n * P : (n + 1) * P],
-                        rhs=h_w[:, b, cols].bitcast(FP8X4),
-                        rhs_scale=h_s[:, b, cols],
-                        start=(b == 1),
-                        stop=(b == 0),
-                    )
+                sums = banks[used[n]][:, 0 : j1 - j0]
                 bias = bd_sb[:, n : n + 1]
-                if n == 1 and j1 == S:
-                    nc.vector.tensor_scalar(
-                        out=y_sb[:, n, cols], in0=bank[:, 0 : j1 - j0], scalar1=bias, scalar2=None, op0=ALU.add
-                    )
+                if n == 1 and j1 - j0 == P:
+                    nc.vector.tensor_scalar(out=y_sb[:, n, cols], in0=sums, scalar1=bias, scalar2=None, op0=ALU.add)
                 else:
-                    nc.scalar.activation(out=y_sb[:, n, cols], in_=bank[:, 0 : j1 - j0], func=ACT.Identity, bias=bias)
+                    nc.scalar.activation(out=y_sb[:, n, cols], in_=sums, func=ACT.Identity, bias=bias)
             nc.sync.dma_start(out=out.rearrange("(n p) j -> p n j", n=2)[:, :, cols], in_=y_sb[:, :, cols])
 
-        for planes in (tab_s, wg_s_raw, v_s_moved, wd_s):
-            nc.vector.memset(planes[:], 0)
+        nc.vector.memset(tab_s[:], 0)
+        nc.gpsimd.memset(warm[:], 0.0)
+        for planes in (wg_s_raw, v_s_moved, wd_s):
+            nc.gpsimd.memset(planes[:], 0)
+        nc.scalar.activation(out=warm[:, 1:2], in_=warm[:, 0:1], func=ACT.Sigmoid)
 
         nc.sync.dma_start(offsets[:], offs)
         load_wg_words(0)
         load_table_scales()
         load_table_words(0)
-        nc.scalar.dma_start(out=bg_sb[:], in_=bg.rearrange("(b p t) -> p b t", b=2, t=4))
-        nc.scalar.activation(out=warm[:], in_=bg_sb[:, 0, 0:1], func=ACT.Sigmoid)
         load_planes(wg_s_raw, wg_scales)
-        load_wv(0, 0, 0, QUARTER)
         load_table_words(1)
-        load_wv(0, 0, QUARTER, HALF)
+        nc.scalar.dma_start(out=bg_sb[:], in_=bg.rearrange("(b p t) -> p b t", b=2, t=4))
+        load_wv(0, 0)
         reorder_wg_words(0)
         gather_scales()
         load_wg_words(1)
         load_wv(1, 0, 0, TAIL)
         load_wv(1, 0, TAIL, HALF)
-        load_wv(0, 1, 0, HALF)
-        load_wv(1, 1, 0, HALF)
+        load_wv(0, 1, 0, QUARTER)
+        load_wv(0, 1, QUARTER, HALF)
+        load_wv(1, 1)
         nc.sync.dma_start(out=wd_w[:], in_=wd_words.rearrange("a p n i -> p a (n i)").bitcast(I32))
         load_planes(wd_s, wd_scales)
         with nc.allow_non_contiguous_dma(reason="one bias value for each partition"):
             nc.sync.dma_start(out=bd_sb[:], in_=bd.rearrange("(n p) -> p n", n=2))
 
-        gather_words(0, 0)
-        reorder_wg_scales(0)
-        reorder_wg_scales(1)
-        opened = {}
-        for u in range(2):
-            if u == 1:
-                gather_words(0, 1, "wg_s_raw")
-            for t in range(4):
-                opened[u, t] = psum.tile([P, HALF], F32, name="opened_bank", tag=("gate", "value")[u])
-                gate_pass(opened[u, t], 0, 0, t, u)
-        round_wv(nc.scalar.copy, 0, 0, (0, QUARTER), 0, QUARTER)
-        round_wv(nc.scalar.copy, 0, 0, (QUARTER, HALF), QUARTER, HALF)
-        for u in range(2):
-            gather_words(1, u)
-        for u in range(2):
-            for t in range(4):
-                gate_pass(opened[u, t], 1, 0, t, u)
-                sigmoid(opened[u, t], 0, t, u)
-
+        reorder_wg_scales(0, 0, 1)
+        reorder_wg_scales(0, 1, 2)
+        reorder_wg_scales(1, 0, 2)
+        v_all = sbuf("v_all", [P, 4 * HALF], U32)
+        for a in range(2):
+            for u in range(2):
+                gather_words(a, u, v_all[:, (2 * a + u) * HALF : (2 * a + u + 1) * HALF])
+        low, high = (0, 1, 2, 3), (4, 5, 6, 7)
+        round_wv(nc.scalar.copy, 0, 0, 0)
+        round_wv(nc.vector.tensor_copy, 0, 0, 2)
         reorder_wg_words(1)
+        for a in range(2):
+            for u in range(2):
+                for t in range(4):
+                    gate_pass(banks[4 * u + t], a, 0, t, u)
+        sigmoids(0, 0, low)
+        sigmoids(0, 1, high)
+        for t in range(4):
+            gate_sums(1, 0, [t], low)
+        sigmoids(1, 0, low, (0, 1))
+
         quantize_wv(0, 0, 0, 4)
-        round_wv(nc.vector.tensor_copy, 1, 0, (0, TAIL), 0, TAIL)
-        round_wv(nc.vector.tensor_copy, 1, 0, (TAIL, HALF), TAIL, HALF)
-        quantize_wv(1, 0, 0, 2)
+        for c0, c1 in ((0, TAIL), (TAIL, HALF)):
+            for t0 in (2, 0):
+                round_wv(nc.vector.tensor_copy, 1, 0, t0, c0, c1)
         quantize_wv(1, 0, 2, 4)
+        quantize_wv(1, 0, 0, 2)
+        for t0 in (0, 2):
+            round_wv(nc.vector.tensor_copy, 0, 1, t0, 0, QUARTER)
+        for t0 in (0, 2):
+            round_wv(nc.scalar.copy, 0, 1, t0, QUARTER, HALF)
+        for t0 in (2, 0):
+            round_wv(nc.scalar.copy, 1, 1, t0)
+        sigmoids(1, 0, low, (2, 3))
 
-        round_wv(nc.scalar.copy, 0, 1, (0, HALF), 0, QUARTER)
-        round_wv(nc.vector.tensor_copy, 0, 1, (0, HALF), QUARTER, HALF)
-        for c in range(3):
-            gated_values(0, 0, c)
-        gates(1, 0)
-        gated_values(0, 0, 3)
-        round_wv(nc.scalar.copy, 1, 1, (0, HALF), 0, QUARTER)
-        round_wv(nc.scalar.copy, 1, 1, (0, HALF), QUARTER, HALF)
-        gated_values(0, 1, 0)
-        gated_values(0, 1, 1)
-        quantize_wv(0, 1, 0, 4)
-        gated_values(0, 1, 2)
-        quantize_h(0, 0, 0, 4)
-        gated_values(0, 1, 3)
-        gates(1, 1)
-        quantize_h(0, 1, 0, 4)
-        quantize_wv(1, 1, 0, 4)
-
+        last = (4, 5, 0, 1)
         for c in range(4):
-            gated_values(1, 0, c)
-        gated_values(1, 1, 0)
-        gated_values(1, 1, 1)
-        quantize_h(1, 0, 0, 2)
-        quantize_h(1, 0, 2, 4)
-        project(0, 2 * P)
-        gated_values(1, 1, 2)
-        quantize_h(1, 1, 0, 2)
-        gated_values(1, 1, 3)
-        quantize_h(1, 1, 2, 3)
-        project(2 * P, 4 * P)
-        project(4 * P, 6 * P)
-        project(6 * P, 7 * P)
-        quantize_h(1, 1, 3, 4)
-        project(7 * P, 8 * P)
+            gated_values(0, 0, c, banks[high[c]])
+        gated_values(0, 1, 0, banks[0])
+        gate_sums(1, 1, [0], last)
+        gated_values(0, 1, 1, banks[1])
+        quantize_wv(0, 1, 0, 4)
+        gate_sums(1, 1, [1], last)
+        quantize_wv(1, 1, 0, 4)
+        quantize_h(0, 0, 0, 4)
+        gated_values(0, 1, 2, banks[6])
+        gated_values(0, 1, 3, banks[7])
+        gate_sums(1, 1, [2, 3], last)
+        sigmoids(1, 1, last)
+        ring = (2, 3, 6, 7)
+
+        def quantize_chunks(c0, c1):
+            quantize_h(1, c0 // 4, c0 % 4, c0 % 4 + c1 - c0)
+
+        def finish(c0, c1, used):
+            project_pass(1, c0 * P, c1 * P, used)
+            store(c0 * P, c1 * P, used)
+
+        def values(c):
+            gated_values(1, c // 4, c % 4, banks[ring[c % 4]])
+
+        values(0)
+        quantize_h(0, 1, 0, 4)
+        values(1)
+        values(2)
+        project_pass(0, 0, 2 * P, (4, 5))
+        quantize_chunks(0, 2)
+        finish(0, 2, (4, 5))
+        values(3)
+        values(4)
+        project_pass(0, 2 * P, 4 * P, (0, 1))
+        quantize_chunks(2, 4)
+        finish(2, 4, (0, 1))
+        values(5)
+        values(6)
+        project_pass(0, 4 * P, 6 * P, (4, 5))
+        quantize_chunks(4, 6)
+        finish(4, 6, (4, 5))
+        values(7)
+        project_pass(0, 6 * P, 7 * P, (2, 3))
+        project_pass(0, 7 * P, 8 * P, (0, 1))
+        quantize_chunks(6, 7)
+        quantize_chunks(7, 8)
+        finish(6, 7, (2, 3))
+        finish(7, 8, (0, 1))

@@ -20,6 +20,7 @@ P = 128
 HALF = 512
 QUARTER = 256
 TAIL = 384
+WARM_UPS = 3
 SHIFT = 16
 
 
@@ -49,17 +50,14 @@ def tile_list_clicked_item_candidates_kernel(
         wg_s_raw = sbuf("wg_s_raw", [P, 2, H // 4], I32)
         wg_w = [sbuf("wg_w%d" % b, [P, 2, 2 * HALF], U8) for b in range(2)]
         wg_s = [sbuf("wg_s%d" % b, [P, 2, HALF], U8) for b in range(2)]
-        wv_raw = {(a, b): sbuf("wv_raw%d%d" % (a, b), [P, 4 * HALF], F32)[:] for a, b in pairs[:3]}
-        shared = sbuf("shared", [P, 8 * HALF], F32)
-        wv_raw[1, 1] = shared[:, 2 * HALF : 6 * HALF]
+        wv_raw = {(a, b): sbuf("wv_raw%d%d" % (a, b), [P, 4 * HALF], F32)[:] for a, b in pairs}
         wv_bf = {(a, b): sbuf("wv_bf%d%d" % (a, b), [P, 4 * HALF], BF16)[:] for a, b in pairs[:3]}
         shared_bf = sbuf("shared_bf", [P, 6 * HALF], BF16)
         wv_bf[1, 1] = shared_bf[:, 2 * HALF : 6 * HALF]
         wv_w = sbuf("wv_w", [P, 2, H], U32)
         wv_s = sbuf("wv_s", [P, 2, H], U8)
-        gate = {(b, u): sbuf("gate%d%d" % (b, u), [P, 4, HALF], F32)[:] for b, u in pairs[:2]}
-        for u in range(2):
-            gate[1, u] = shared[:, 4 * u * HALF : 4 * (u + 1) * HALF].rearrange("p (t j) -> p t j", t=4)
+        gate = {(b, u): sbuf("gate%d%d" % (b, u), [P, 4, HALF], F32)[:] for b, u in pairs[:3]}
+        gate[1, 1] = wv_raw[1, 1].rearrange("p (t j) -> p t j", t=4)
         h_bf = {(b, u): sbuf("h_bf%d%d" % (b, u), [P, 4 * HALF], BF16)[:] for b, u in ((0, 0), (1, 0), (1, 1))}
         h_bf[0, 1] = shared_bf[:, 0 : 4 * HALF]
         h_w = sbuf("h_w", [P, 2, S], U32)
@@ -93,10 +91,10 @@ def tile_list_clicked_item_candidates_kernel(
             rows = wv[a * HALF : (a + 1) * HALF, b * HALF + c0 : b * HALF + c1]
             nc.sync.dma_start(out=wv_piece(a, b, c0, c1), in_=rows.rearrange("(p i) c -> p i c", i=4))
 
-        def round_wv(copy, a, b, t0, c0=0, c1=HALF):
+        def round_wv(copy, a, b, t0, c0=0, c1=HALF, width=2):
             dst = wv_bf[a, b][:].rearrange("p (t m i) -> p m i t", t=4, i=4)[:, c0 // 4 : c1 // 4, :, :]
             src = wv_piece(a, b, c0, c1).rearrange("p i (m t) -> p m i t", t=4)
-            copy(out=dst[:, :, :, t0 : t0 + 2], in_=src[:, :, :, t0 : t0 + 2])
+            copy(out=dst[:, :, :, t0 : t0 + width], in_=src[:, :, :, t0 : t0 + width])
 
         def quantize_wv(a, b, t0, t1):
             cols = slice(b * HALF + t0 * P, b * HALF + t1 * P)
@@ -213,10 +211,10 @@ def tile_list_clicked_item_candidates_kernel(
         load_planes(wg_s_raw, wg_scales)
         load_table_words(1)
         nc.scalar.dma_start(out=bg_sb[:], in_=bg.rearrange("(b p t) -> p b t", b=2, t=4))
-        load_wv(0, 0)
+        load_wg_words(1)
         reorder_wg_words(0)
         gather_scales()
-        load_wg_words(1)
+        load_wv(0, 0)
         load_wv(1, 0, 0, TAIL)
         load_wv(1, 0, TAIL, HALF)
         load_wv(0, 1, 0, QUARTER)
@@ -227,6 +225,16 @@ def tile_list_clicked_item_candidates_kernel(
         with nc.allow_non_contiguous_dma(reason="one bias value for each partition"):
             nc.sync.dma_start(out=bd_sb[:], in_=bd.rearrange("(n p) -> p n", n=2))
 
+        for warm_up in range(WARM_UPS):
+            nc.tensor.matmul_mx(
+                out=banks[7][:],
+                lhsT=wg_w[0][:, 0, 0 : 2 * P].bitcast(FP4X4),
+                lhsT_scale=tab_s[:].bitcast(U8)[:, 0:P],
+                rhs=tab_w[0][:, 0:HALF].bitcast(FP8X4),
+                rhs_scale=tab_s[:].bitcast(U8)[:, 0:HALF],
+                start=True,
+                stop=True,
+            )
         reorder_wg_scales(0, 0, 1)
         reorder_wg_scales(0, 1, 2)
         reorder_wg_scales(1, 0, 2)
@@ -235,9 +243,9 @@ def tile_list_clicked_item_candidates_kernel(
             for u in range(2):
                 gather_words(a, u, v_all[:, (2 * a + u) * HALF : (2 * a + u + 1) * HALF])
         low, high = (0, 1, 2, 3), (4, 5, 6, 7)
-        round_wv(nc.scalar.copy, 0, 0, 0)
-        round_wv(nc.vector.tensor_copy, 0, 0, 2)
         reorder_wg_words(1)
+        round_wv(nc.vector.tensor_copy, 0, 0, 0)
+        round_wv(nc.vector.tensor_copy, 0, 0, 2)
         for a in range(2):
             for u in range(2):
                 for t in range(4):
@@ -246,9 +254,10 @@ def tile_list_clicked_item_candidates_kernel(
         sigmoids(0, 1, high)
         for t in range(4):
             gate_sums(1, 0, [t], low)
-        sigmoids(1, 0, low, (0, 1))
+        sigmoids(1, 0, low)
 
-        quantize_wv(0, 0, 0, 4)
+        quantize_wv(0, 0, 0, 2)
+        quantize_wv(0, 0, 2, 4)
         for c0, c1 in ((0, TAIL), (TAIL, HALF)):
             for t0 in (2, 0):
                 round_wv(nc.vector.tensor_copy, 1, 0, t0, c0, c1)
@@ -256,20 +265,16 @@ def tile_list_clicked_item_candidates_kernel(
         quantize_wv(1, 0, 0, 2)
         for t0 in (0, 2):
             round_wv(nc.vector.tensor_copy, 0, 1, t0, 0, QUARTER)
-        for t0 in (0, 2):
-            round_wv(nc.scalar.copy, 0, 1, t0, QUARTER, HALF)
-        for t0 in (2, 0):
-            round_wv(nc.scalar.copy, 1, 1, t0)
-        sigmoids(1, 0, low, (2, 3))
+        round_wv(nc.scalar.copy, 0, 1, 0, QUARTER, HALF, 4)
+        round_wv(nc.scalar.copy, 1, 1, 0, 0, HALF, 4)
 
         last = (4, 5, 0, 1)
+        gate_sums(1, 1, [0, 1], last)
         for c in range(4):
-            gated_values(0, 0, c, banks[high[c]])
-        gated_values(0, 1, 0, banks[0])
-        gate_sums(1, 1, [0], last)
-        gated_values(0, 1, 1, banks[1])
+            gated_values(0, 0, c, banks[(6, 7, 0, 1)[c]])
+        gated_values(0, 1, 0, banks[2])
+        gated_values(0, 1, 1, banks[3])
         quantize_wv(0, 1, 0, 4)
-        gate_sums(1, 1, [1], last)
         quantize_wv(1, 1, 0, 4)
         quantize_h(0, 0, 0, 4)
         gated_values(0, 1, 2, banks[6])

@@ -21,6 +21,7 @@ HALF = 512
 QUARTER = 256
 TAIL = 384
 WARM_UPS = 3
+MX_ALIGN = 64
 SHIFT = 16
 
 
@@ -34,7 +35,7 @@ def tile_list_clicked_item_candidates_kernel(
         banks = [psum.tile([P, HALF], F32, name="bank%d" % i) for i in range(8)]
 
         def sbuf(name, shape, dtype, tag=None):
-            return keep.tile(shape, dtype, name=name, tag=tag or name, align_bytes=64)
+            return keep.tile(shape, dtype, name=name, tag=tag or name, align_bytes=MX_ALIGN)
 
         pairs = [(x, y) for x in range(2) for y in range(2)]
         offsets = keep.tile([P, S // 16], U16, name="offsets")
@@ -50,17 +51,32 @@ def tile_list_clicked_item_candidates_kernel(
         wg_s_raw = sbuf("wg_s_raw", [P, 2, H // 4], I32)
         wg_w = [sbuf("wg_w%d" % b, [P, 2, 2 * HALF], U8) for b in range(2)]
         wg_s = [sbuf("wg_s%d" % b, [P, 2, HALF], U8) for b in range(2)]
-        wv_raw = {(a, b): sbuf("wv_raw%d%d" % (a, b), [P, 4 * HALF], F32)[:] for a, b in pairs}
+        wv_raw = {(a, b): sbuf("wv_raw%d%d" % (a, b), [P, 4 * HALF], F32)[:] for a, b in pairs[:3]}
+        shared = sbuf("shared", [P, 8 * HALF], F32)
+        last_piece = shared[:, 2 * HALF : 8 * HALF].rearrange("p (i c) -> p i c", i=4)[:, :, 0:HALF]
         wv_bf = {(a, b): sbuf("wv_bf%d%d" % (a, b), [P, 4 * HALF], BF16)[:] for a, b in pairs[:3]}
-        shared_bf = sbuf("shared_bf", [P, 6 * HALF], BF16)
-        wv_bf[1, 1] = shared_bf[:, 2 * HALF : 6 * HALF]
+        turn = ctx.enter_context(tc.tile_pool(name="turn", bufs=1))
+
+        def placed(name, shape, dtype, offset):
+            return turn.tile(shape, dtype, name=name, align_bytes=MX_ALIGN, offset=offset)[:]
+
+        wv_bf[1, 1] = placed("wv_bf11", [P, 4 * HALF + MX_ALIGN // 2], BF16, 0)[:, 0 : 4 * HALF]
         wv_w = sbuf("wv_w", [P, 2, H], U32)
         wv_s = sbuf("wv_s", [P, 2, H], U8)
-        gate = {(b, u): sbuf("gate%d%d" % (b, u), [P, 4, HALF], F32)[:] for b, u in pairs[:3]}
-        gate[1, 1] = wv_raw[1, 1].rearrange("p (t j) -> p t j", t=4)
-        h_bf = {(b, u): sbuf("h_bf%d%d" % (b, u), [P, 4 * HALF], BF16)[:] for b, u in ((0, 0), (1, 0), (1, 1))}
-        h_bf[0, 1] = shared_bf[:, 0 : 4 * HALF]
-        h_w = sbuf("h_w", [P, 2, S], U32)
+        gate = {(b, u): sbuf("gate%d%d" % (b, u), [P, 4, HALF], F32)[:] for b, u in pairs[:2]}
+        for u in range(2):
+            gate[1, u] = shared[:, 4 * u * HALF : 4 * (u + 1) * HALF].rearrange("p (t j) -> p t j", t=4)
+        h_bf = {}
+        for b, u in pairs:
+            whole = sbuf("h_bf%d%d" % (b, u), [P, 4 * HALF], BF16)
+            for c0, c1 in ((0, 4), (0, 2), (2, 4)) + tuple((c, c + 1) for c in range(4)):
+                h_bf[b, u, c0, c1] = whole[:, c0 * HALF : c1 * HALF]
+        h_bf[0, 1, 2, 4] = placed("h_bf_late", [P, 2 * HALF], BF16, 0)
+        for c in (2, 3):
+            h_bf[0, 1, c, c + 1] = h_bf[0, 1, 2, 4][:, (c - 2) * HALF : (c - 1) * HALF]
+        h_w = {(b, u): sbuf("h_w%d%d" % (b, u), [P, HALF], U32)[:] for b, u in pairs[2:]}
+        for u in range(2):
+            h_w[0, u] = placed("h_w0%d" % u, [P, HALF], U32, 4 * HALF * (u + 1))
         h_s = sbuf("h_s", [P, 2, S], U8)
         wd_w = sbuf("wd_w", [P, 2, N], I32)
         wd_s = sbuf("wd_s", [P, 2, N // 4], I32)
@@ -85,6 +101,8 @@ def tile_list_clicked_item_candidates_kernel(
             nc.sync.dma_start(out=wg_w_raw[b][:], in_=words.rearrange("a p w -> p a w"))
 
         def wv_piece(a, b, c0, c1):
+            if (a, b) == (1, 1):
+                return last_piece
             return wv_raw[a, b][:, 4 * c0 : 4 * c1].rearrange("p (i c) -> p i c", i=4)
 
         def load_wv(a, b, c0=0, c1=HALF):
@@ -163,7 +181,7 @@ def tile_list_clicked_item_candidates_kernel(
                         stop=(a == 0),
                     )
             nc.vector.tensor_tensor(
-                out=h_bf[b, u][:, c * HALF : (c + 1) * HALF].rearrange("p (j e t) -> p j t e", e=2, t=4),
+                out=h_bf[b, u, c, c + 1].rearrange("p (j e t) -> p j t e", e=2, t=4),
                 in0=bank[:].rearrange("p (t j e) -> p j t e", t=4, e=2),
                 in1=gate[b, u][:, :, c * P : (c + 1) * P].rearrange("p t (j e) -> p j t e", e=2),
                 op=ALU.mult,
@@ -172,7 +190,9 @@ def tile_list_clicked_item_candidates_kernel(
         def quantize_h(b, u, c0, c1):
             cols = slice(u * HALF + c0 * P, u * HALF + c1 * P)
             nc.vector.quantize_mx(
-                out=h_w[:, b, cols].bitcast(FP8X4), scales=h_s[:, b, cols], in_=h_bf[b, u][:, c0 * HALF : c1 * HALF]
+                out=h_w[b, u][:, c0 * P : c1 * P].bitcast(FP8X4),
+                scales=h_s[:, b, cols],
+                in_=h_bf[b, u, c0, c1],
             )
 
         def project_pass(b, j0, j1, used, first=0):
@@ -181,7 +201,7 @@ def tile_list_clicked_item_candidates_kernel(
                     out=banks[used[n]][:, 0 : j1 - j0],
                     lhsT=wd_w[:, b, n * P : (n + 1) * P].bitcast(FP8X4),
                     lhsT_scale=wd_s[:, b, :].bitcast(U8)[:, n * P : (n + 1) * P],
-                    rhs=h_w[:, b, j0:j1].bitcast(FP8X4),
+                    rhs=h_w[b, j0 // HALF][:, j0 % HALF : j0 % HALF + j1 - j0].bitcast(FP8X4),
                     rhs_scale=h_s[:, b, j0:j1],
                     start=(b == first),
                     stop=(b != first),
@@ -254,7 +274,7 @@ def tile_list_clicked_item_candidates_kernel(
         sigmoids(0, 1, high)
         for t in range(4):
             gate_sums(1, 0, [t], low)
-        sigmoids(1, 0, low)
+        sigmoids(1, 0, low, (0, 1))
 
         quantize_wv(0, 0, 0, 2)
         quantize_wv(0, 0, 2, 4)
@@ -268,20 +288,22 @@ def tile_list_clicked_item_candidates_kernel(
         round_wv(nc.scalar.copy, 0, 1, 0, QUARTER, HALF, 4)
         round_wv(nc.scalar.copy, 1, 1, 0, 0, HALF, 4)
 
-        last = (4, 5, 0, 1)
+        sigmoids(1, 0, low, (2, 3))
+        last = (4, 5, 6, 7)
         gate_sums(1, 1, [0, 1], last)
         for c in range(4):
             gated_values(0, 0, c, banks[(6, 7, 0, 1)[c]])
-        gated_values(0, 1, 0, banks[2])
-        gated_values(0, 1, 1, banks[3])
+        gated_values(0, 1, 0, banks[6])
+        gated_values(0, 1, 1, banks[7])
         quantize_wv(0, 1, 0, 4)
         quantize_wv(1, 1, 0, 4)
         quantize_h(0, 0, 0, 4)
-        gated_values(0, 1, 2, banks[6])
-        gated_values(0, 1, 3, banks[7])
+        quantize_h(0, 1, 0, 2)
+        gated_values(0, 1, 2, banks[0])
+        gated_values(0, 1, 3, banks[1])
         gate_sums(1, 1, [2, 3], last)
         sigmoids(1, 1, last)
-        ring = (2, 3, 6, 7)
+        ring = (2, 3, 0, 1)
 
         def quantize_chunks(c0, c1):
             quantize_h(1, c0 // 4, c0 % 4, c0 % 4 + c1 - c0)
@@ -294,7 +316,7 @@ def tile_list_clicked_item_candidates_kernel(
             gated_values(1, c // 4, c % 4, banks[ring[c % 4]])
 
         values(0)
-        quantize_h(0, 1, 0, 4)
+        quantize_h(0, 1, 2, 4)
         values(1)
         values(2)
         project_pass(0, 0, 2 * P, (4, 5))
@@ -302,9 +324,9 @@ def tile_list_clicked_item_candidates_kernel(
         finish(0, 2, (4, 5))
         values(3)
         values(4)
-        project_pass(0, 2 * P, 4 * P, (0, 1))
+        project_pass(0, 2 * P, 4 * P, (6, 7))
         quantize_chunks(2, 4)
-        finish(2, 4, (0, 1))
+        finish(2, 4, (6, 7))
         values(5)
         values(6)
         project_pass(0, 4 * P, 6 * P, (4, 5))
@@ -312,8 +334,8 @@ def tile_list_clicked_item_candidates_kernel(
         finish(4, 6, (4, 5))
         values(7)
         project_pass(0, 6 * P, 7 * P, (2, 3))
-        project_pass(0, 7 * P, 8 * P, (0, 1))
+        project_pass(0, 7 * P, 8 * P, (6, 7))
         quantize_chunks(6, 7)
         quantize_chunks(7, 8)
         finish(6, 7, (2, 3))
-        finish(7, 8, (0, 1))
+        finish(7, 8, (6, 7))

@@ -20,7 +20,8 @@ P = 128
 HALF = 512
 QUARTER = 256
 TAIL = 384
-WARM_UPS = 3
+EARLY_WARM_UPS = 4
+WARM_UPS = 2
 MX_ALIGN = 64
 SHIFT = 16
 
@@ -222,6 +223,11 @@ def tile_list_clicked_item_candidates_kernel(
         nc.gpsimd.memset(warm[:], 0.0)
         for planes in (wg_s_raw, v_s_moved, wd_s):
             nc.gpsimd.memset(planes[:], 0)
+        zeros_bf = sbuf("zeros_bf", [P, 4 * P], BF16)
+        zeros_w = sbuf("zeros_w", [P, P], U32)
+        zeros_s = sbuf("zeros_s", [P, P], U8)
+        nc.vector.memset(zeros_bf[:].bitcast(I32), 0)
+        nc.vector.quantize_mx(out=zeros_w[:].bitcast(FP8X4), scales=zeros_s[:], in_=zeros_bf[:])
         nc.scalar.activation(out=warm[:, 1:2], in_=warm[:, 0:1], func=ACT.Sigmoid)
 
         nc.sync.dma_start(offsets[:], offs)
@@ -245,6 +251,16 @@ def tile_list_clicked_item_candidates_kernel(
         with nc.allow_non_contiguous_dma(reason="one bias value for each partition"):
             nc.sync.dma_start(out=bd_sb[:], in_=bd.rearrange("(n p) -> p n", n=2))
 
+        for warm_up in range(EARLY_WARM_UPS):
+            nc.tensor.matmul_mx(
+                out=banks[7][:],
+                lhsT=zeros_w[:].bitcast(FP8X4),
+                lhsT_scale=zeros_s[:],
+                rhs=wg_w_raw[0][:, 0, :].bitcast(U8).bitcast(FP4X4),
+                rhs_scale=tab_s[:].bitcast(U8)[:, 0:HALF],
+                start=True,
+                stop=True,
+            )
         for warm_up in range(WARM_UPS):
             nc.tensor.matmul_mx(
                 out=banks[7][:],

@@ -52,9 +52,9 @@ def tile_list_clicked_item_candidates_kernel(
         wg_s_raw = sbuf("wg_s_raw", [P, 2, H // 4], I32)
         wg_w = [sbuf("wg_w%d" % b, [P, 2, 2 * HALF], U8) for b in range(2)]
         wg_s = [sbuf("wg_s%d" % b, [P, 2, HALF], U8) for b in range(2)]
-        wv_raw = {(a, b): sbuf("wv_raw%d%d" % (a, b), [P, 4 * HALF], F32)[:] for a, b in pairs[:3]}
-        shared = sbuf("shared", [P, 8 * HALF], F32)
-        last_piece = shared[:, 2 * HALF : 8 * HALF].rearrange("p (i c) -> p i c", i=4)[:, :, 0:HALF]
+        wv_raw = {(a, b): sbuf("wv_raw%d%d" % (a, b), [P, 4 * HALF], F32)[:] for a, b in pairs}
+        shared = sbuf("shared", [P, 4, HALF], F32)
+        last_piece = shared[:, :, 0:QUARTER]
         wv_bf = {(a, b): sbuf("wv_bf%d%d" % (a, b), [P, 4 * HALF], BF16)[:] for a, b in pairs[:3]}
         turn = ctx.enter_context(tc.tile_pool(name="turn", bufs=1))
 
@@ -64,17 +64,13 @@ def tile_list_clicked_item_candidates_kernel(
         wv_bf[1, 1] = placed("wv_bf11", [P, 4 * HALF + MX_ALIGN // 2], BF16, 0)[:, 0 : 4 * HALF]
         wv_w = sbuf("wv_w", [P, 2, H], U32)
         wv_s = sbuf("wv_s", [P, 2, H], U8)
-        gate = {(b, u): sbuf("gate%d%d" % (b, u), [P, 4, HALF], F32)[:] for b, u in pairs[:2]}
-        for u in range(2):
-            gate[1, u] = shared[:, 4 * u * HALF : 4 * (u + 1) * HALF].rearrange("p (t j) -> p t j", t=4)
+        gate = {(b, u): sbuf("gate%d%d" % (b, u), [P, 4, HALF], F32)[:] for b, u in pairs[:3]}
+        gate[1, 1] = shared[:]
         h_bf = {}
         for b, u in pairs:
             whole = sbuf("h_bf%d%d" % (b, u), [P, 4 * HALF], BF16)
             for c0, c1 in ((0, 4), (0, 2), (2, 4)) + tuple((c, c + 1) for c in range(4)):
                 h_bf[b, u, c0, c1] = whole[:, c0 * HALF : c1 * HALF]
-        h_bf[0, 1, 2, 4] = placed("h_bf_late", [P, 2 * HALF], BF16, 0)
-        for c in (2, 3):
-            h_bf[0, 1, c, c + 1] = h_bf[0, 1, 2, 4][:, (c - 2) * HALF : (c - 1) * HALF]
         h_w = {(b, u): sbuf("h_w%d%d" % (b, u), [P, HALF], U32)[:] for b, u in pairs[2:]}
         for u in range(2):
             h_w[0, u] = placed("h_w0%d" % u, [P, HALF], U32, 4 * HALF * (u + 1))
@@ -102,7 +98,7 @@ def tile_list_clicked_item_candidates_kernel(
             nc.sync.dma_start(out=wg_w_raw[b][:], in_=words.rearrange("a p w -> p a w"))
 
         def wv_piece(a, b, c0, c1):
-            if (a, b) == (1, 1):
+            if (a, b, c1) == (1, 1, HALF):
                 return last_piece
             return wv_raw[a, b][:, 4 * c0 : 4 * c1].rearrange("p (i c) -> p i c", i=4)
 
@@ -135,7 +131,8 @@ def tile_list_clicked_item_candidates_kernel(
 
         def gather_scales():
             nc.vector.tensor_copy(out=v_s[:], in_=tab_s[:].bitcast(U8).indirect(offsets[:]))
-            nc.sync.dma_start(out=v_s_moved[0 : P - SHIFT, :], in_=v_s[SHIFT:P, :].bitcast(I32))
+            for s in range(4):
+                nc.sync.dma_start(out=v_s_moved[s:P:32, :], in_=v_s[SHIFT + s : P : 32, :].bitcast(I32))
 
         def gather_words(a, u, dst):
             v_w[a, u] = dst
@@ -168,25 +165,42 @@ def tile_list_clicked_item_candidates_kernel(
             for t in ts:
                 sigmoid(banks[used[t]], b, t, u)
 
-        def gated_values(b, u, c, bank):
+        def value_pass(b, u, c, bank, a, t, start, stop):
+            cols = slice(b * HALF + t * P, b * HALF + (t + 1) * P)
+            nc.tensor.matmul_mx(
+                out=bank[:, t * P : (t + 1) * P],
+                lhsT=wv_w[:, a, cols].bitcast(FP8X4),
+                lhsT_scale=wv_s[:, a, cols],
+                rhs=v_w[a, u][:, c * P : (c + 1) * P].bitcast(FP8X4),
+                rhs_scale=v_plane(a, u * HALF + c * P, u * HALF + (c + 1) * P),
+                start=start,
+                stop=stop,
+            )
+
+        def open_values(b, u, c, bank):
             for t in range(4):
-                cols = slice(b * HALF + t * P, b * HALF + (t + 1) * P)
-                for a in (1, 0):
-                    nc.tensor.matmul_mx(
-                        out=bank[:, t * P : (t + 1) * P],
-                        lhsT=wv_w[:, a, cols].bitcast(FP8X4),
-                        lhsT_scale=wv_s[:, a, cols],
-                        rhs=v_w[a, u][:, c * P : (c + 1) * P].bitcast(FP8X4),
-                        rhs_scale=v_plane(a, u * HALF + c * P, u * HALF + (c + 1) * P),
-                        start=(a == 1),
-                        stop=(a == 0),
-                    )
+                value_pass(b, u, c, bank, 0, t, t == 0, False)
+
+        def value_sums(b, u, c, bank, opened):
+            if opened:
+                for t in (2, 3, 0, 1):
+                    value_pass(b, u, c, bank, 1, t, False, t == 1)
+            else:
+                for t in range(4):
+                    for a in (1, 0):
+                        value_pass(b, u, c, bank, a, t, a == 1, a == 0)
+
+        def product(b, u, c, bank):
             nc.vector.tensor_tensor(
                 out=h_bf[b, u, c, c + 1].rearrange("p (j e t) -> p j t e", e=2, t=4),
                 in0=bank[:].rearrange("p (t j e) -> p j t e", t=4, e=2),
                 in1=gate[b, u][:, :, c * P : (c + 1) * P].rearrange("p t (j e) -> p j t e", e=2),
                 op=ALU.mult,
             )
+
+        def gated_values(b, u, c, bank, opened=False):
+            value_sums(b, u, c, bank, opened)
+            product(b, u, c, bank)
 
         def quantize_h(b, u, c0, c1):
             cols = slice(u * HALF + c0 * P, u * HALF + c1 * P)
@@ -243,9 +257,9 @@ def tile_list_clicked_item_candidates_kernel(
         load_wv(0, 0)
         load_wv(1, 0, 0, TAIL)
         load_wv(1, 0, TAIL, HALF)
-        load_wv(0, 1, 0, QUARTER)
-        load_wv(0, 1, QUARTER, HALF)
-        load_wv(1, 1)
+        for a in range(2):
+            load_wv(a, 1, 0, QUARTER)
+            load_wv(a, 1, QUARTER, HALF)
         nc.sync.dma_start(out=wd_w[:], in_=wd_words.rearrange("a p n i -> p a (n i)").bitcast(I32))
         load_planes(wd_s, wd_scales)
         with nc.allow_non_contiguous_dma(reason="one bias value for each partition"):
@@ -290,7 +304,7 @@ def tile_list_clicked_item_candidates_kernel(
         sigmoids(0, 1, high)
         for t in range(4):
             gate_sums(1, 0, [t], low)
-        sigmoids(1, 0, low, (0, 1))
+        sigmoids(1, 0, low)
 
         quantize_wv(0, 0, 0, 2)
         quantize_wv(0, 0, 2, 4)
@@ -302,24 +316,29 @@ def tile_list_clicked_item_candidates_kernel(
         for t0 in (0, 2):
             round_wv(nc.vector.tensor_copy, 0, 1, t0, 0, QUARTER)
         round_wv(nc.scalar.copy, 0, 1, 0, QUARTER, HALF, 4)
-        round_wv(nc.scalar.copy, 1, 1, 0, 0, HALF, 4)
+        round_wv(nc.scalar.copy, 1, 1, 0, 0, QUARTER, 4)
+        round_wv(nc.scalar.copy, 1, 1, 0, QUARTER, HALF, 4)
 
-        sigmoids(1, 0, low, (2, 3))
-        last = (4, 5, 6, 7)
-        gate_sums(1, 1, [0, 1], last)
+        last = (4, 6, 7, 0)
+        gate_sums(1, 1, [0], last)
+        for c in range(2):
+            open_values(0, 0, c, banks[5 + c])
         for c in range(4):
-            gated_values(0, 0, c, banks[(6, 7, 0, 1)[c]])
-        gated_values(0, 1, 0, banks[6])
-        gated_values(0, 1, 1, banks[7])
+            gated_values(0, 0, c, banks[(5, 6, 7, 0)[c]], c < 2)
+        gated_values(0, 1, 0, banks[1])
+        gated_values(0, 1, 1, banks[2])
         quantize_wv(0, 1, 0, 4)
-        quantize_wv(1, 1, 0, 4)
+        gated_values(0, 1, 2, banks[3])
+        gated_values(0, 1, 3, banks[5])
+        gate_sums(1, 1, [1, 2, 3], last)
+        ring = (1, 2, 3, 5)
+        for c in range(4):
+            open_values(1, 0, c, banks[ring[c]])
+        quantize_wv(1, 1, 2, 4)
+        quantize_wv(1, 1, 0, 2)
         quantize_h(0, 0, 0, 4)
-        quantize_h(0, 1, 0, 2)
-        gated_values(0, 1, 2, banks[0])
-        gated_values(0, 1, 3, banks[1])
-        gate_sums(1, 1, [2, 3], last)
+        quantize_h(0, 1, 0, 4)
         sigmoids(1, 1, last)
-        ring = (2, 3, 0, 1)
 
         def quantize_chunks(c0, c1):
             quantize_h(1, c0 // 4, c0 % 4, c0 % 4 + c1 - c0)
@@ -329,29 +348,32 @@ def tile_list_clicked_item_candidates_kernel(
             store(c0 * P, c1 * P, used)
 
         def values(c):
-            gated_values(1, c // 4, c % 4, banks[ring[c % 4]])
+            product(1, c // 4, c % 4, banks[ring[c % 4]])
+            if c < 4:
+                value_sums(1, 1, c, banks[ring[c]], False)
 
+        for c in range(4):
+            value_sums(1, 0, c, banks[ring[c]], True)
         values(0)
-        quantize_h(0, 1, 2, 4)
         values(1)
         values(2)
-        project_pass(0, 0, 2 * P, (4, 5))
+        project_pass(0, 0, 2 * P, (4, 6))
         quantize_chunks(0, 2)
-        finish(0, 2, (4, 5))
+        finish(0, 2, (4, 6))
         values(3)
         values(4)
-        project_pass(0, 2 * P, 4 * P, (6, 7))
+        project_pass(0, 2 * P, 4 * P, (7, 0))
         quantize_chunks(2, 4)
-        finish(2, 4, (6, 7))
+        finish(2, 4, (7, 0))
         values(5)
         values(6)
-        project_pass(0, 4 * P, 6 * P, (4, 5))
+        project_pass(0, 4 * P, 6 * P, (4, 6))
         quantize_chunks(4, 6)
-        finish(4, 6, (4, 5))
+        finish(4, 6, (4, 6))
         values(7)
-        project_pass(0, 6 * P, 7 * P, (2, 3))
-        project_pass(0, 7 * P, 8 * P, (6, 7))
+        project_pass(0, 6 * P, 7 * P, (1, 2))
+        project_pass(0, 7 * P, 8 * P, (7, 0))
         quantize_chunks(6, 7)
         quantize_chunks(7, 8)
-        finish(6, 7, (2, 3))
-        finish(7, 8, (6, 7))
+        finish(6, 7, (1, 2))
+        finish(7, 8, (7, 0))

@@ -53,8 +53,8 @@ def tile_list_clicked_item_candidates_kernel(
         wg_w = [sbuf("wg_w%d" % b, [P, 2, 2 * HALF], U8) for b in range(2)]
         wg_s = [sbuf("wg_s%d" % b, [P, 2, HALF], U8) for b in range(2)]
         wv_raw = {(a, b): sbuf("wv_raw%d%d" % (a, b), [P, 4 * HALF], F32)[:] for a, b in pairs}
-        shared = sbuf("shared", [P, 4, HALF], F32)
-        last_piece = shared[:, :, 0:QUARTER]
+        shared = sbuf("shared", [P, 8 * HALF], F32)
+        last_piece = shared[:, 3 * HALF : 8 * HALF].rearrange("p (i c) -> p i c", i=4)[:, :, 3 * P : 3 * P + QUARTER]
         wv_bf = {(a, b): sbuf("wv_bf%d%d" % (a, b), [P, 4 * HALF], BF16)[:] for a, b in pairs[:3]}
         turn = ctx.enter_context(tc.tile_pool(name="turn", bufs=1))
 
@@ -64,8 +64,9 @@ def tile_list_clicked_item_candidates_kernel(
         wv_bf[1, 1] = placed("wv_bf11", [P, 4 * HALF + MX_ALIGN // 2], BF16, 0)[:, 0 : 4 * HALF]
         wv_w = sbuf("wv_w", [P, 2, H], U32)
         wv_s = sbuf("wv_s", [P, 2, H], U8)
-        gate = {(b, u): sbuf("gate%d%d" % (b, u), [P, 4, HALF], F32)[:] for b, u in pairs[:3]}
-        gate[1, 1] = shared[:]
+        gate = {(b, u): sbuf("gate%d%d" % (b, u), [P, 4, HALF], F32)[:] for b, u in pairs[:2]}
+        for u in range(2):
+            gate[1, u] = shared[:, 4 * u * HALF : 4 * (u + 1) * HALF].rearrange("p (t j) -> p t j", t=4)
         h_bf = {}
         for b, u in pairs:
             whole = sbuf("h_bf%d%d" % (b, u), [P, 4 * HALF], BF16)
@@ -231,7 +232,10 @@ def tile_list_clicked_item_candidates_kernel(
                     nc.vector.tensor_scalar(out=y_sb[:, n, cols], in0=sums, scalar1=bias, scalar2=None, op0=ALU.add)
                 else:
                     nc.scalar.activation(out=y_sb[:, n, cols], in_=sums, func=ACT.Identity, bias=bias)
-            nc.sync.dma_start(out=out.rearrange("(n p) j -> p n j", n=2)[:, :, cols], in_=y_sb[:, :, cols])
+                if j1 - j0 > P:
+                    nc.sync.dma_start(out=out[n * P : (n + 1) * P, cols], in_=y_sb[:, n, cols])
+            if j1 - j0 == P:
+                nc.sync.dma_start(out=out.rearrange("(n p) j -> p n j", n=2)[:, :, cols], in_=y_sb[:, :, cols])
 
         nc.vector.memset(tab_s[:], 0)
         nc.gpsimd.memset(warm[:], 0.0)
@@ -260,7 +264,8 @@ def tile_list_clicked_item_candidates_kernel(
         for a in range(2):
             load_wv(a, 1, 0, QUARTER)
             load_wv(a, 1, QUARTER, HALF)
-        nc.sync.dma_start(out=wd_w[:], in_=wd_words.rearrange("a p n i -> p a (n i)").bitcast(I32))
+        for b in range(2):
+            nc.sync.dma_start(out=wd_w[:, b, :], in_=wd_words[b].rearrange("p n i -> p (n i)").bitcast(I32))
         load_planes(wd_s, wd_scales)
         with nc.allow_non_contiguous_dma(reason="one bias value for each partition"):
             nc.sync.dma_start(out=bd_sb[:], in_=bd.rearrange("(n p) -> p n", n=2))
@@ -304,7 +309,7 @@ def tile_list_clicked_item_candidates_kernel(
         sigmoids(0, 1, high)
         for t in range(4):
             gate_sums(1, 0, [t], low)
-        sigmoids(1, 0, low)
+        sigmoids(1, 0, low, (0, 1, 2))
 
         quantize_wv(0, 0, 0, 2)
         quantize_wv(0, 0, 2, 4)
@@ -319,20 +324,20 @@ def tile_list_clicked_item_candidates_kernel(
         round_wv(nc.scalar.copy, 1, 1, 0, 0, QUARTER, 4)
         round_wv(nc.scalar.copy, 1, 1, 0, QUARTER, HALF, 4)
 
-        last = (4, 6, 7, 0)
-        gate_sums(1, 1, [0], last)
+        sigmoids(1, 0, low, (3,))
+        last = (5, 6, 7, 0)
         for c in range(2):
-            open_values(0, 0, c, banks[5 + c])
+            open_values(0, 0, c, banks[high[c]])
         for c in range(4):
-            gated_values(0, 0, c, banks[(5, 6, 7, 0)[c]], c < 2)
-        gated_values(0, 1, 0, banks[1])
-        gated_values(0, 1, 1, banks[2])
+            gated_values(0, 0, c, banks[high[c]], c < 2)
+        gated_values(0, 1, 0, banks[0])
+        gated_values(0, 1, 1, banks[1])
         quantize_wv(0, 1, 0, 4)
-        gated_values(0, 1, 2, banks[3])
-        gated_values(0, 1, 3, banks[5])
-        gate_sums(1, 1, [1, 2, 3], last)
-        ring = (1, 2, 3, 5)
-        for c in range(4):
+        gated_values(0, 1, 2, banks[2])
+        gated_values(0, 1, 3, banks[4])
+        gate_sums(1, 1, range(4), last)
+        ring = (1, 2, 4, 3)
+        for c in range(3):
             open_values(1, 0, c, banks[ring[c]])
         quantize_wv(1, 1, 2, 4)
         quantize_wv(1, 1, 0, 2)
@@ -353,13 +358,13 @@ def tile_list_clicked_item_candidates_kernel(
                 value_sums(1, 1, c, banks[ring[c]], False)
 
         for c in range(4):
-            value_sums(1, 0, c, banks[ring[c]], True)
+            value_sums(1, 0, c, banks[ring[c]], c < 3)
         values(0)
         values(1)
         values(2)
-        project_pass(0, 0, 2 * P, (4, 6))
+        project_pass(0, 0, 2 * P, (5, 6))
         quantize_chunks(0, 2)
-        finish(0, 2, (4, 6))
+        finish(0, 2, (5, 6))
         values(3)
         values(4)
         project_pass(0, 2 * P, 4 * P, (7, 0))
@@ -367,9 +372,9 @@ def tile_list_clicked_item_candidates_kernel(
         finish(2, 4, (7, 0))
         values(5)
         values(6)
-        project_pass(0, 4 * P, 6 * P, (4, 6))
+        project_pass(0, 4 * P, 6 * P, (5, 6))
         quantize_chunks(4, 6)
-        finish(4, 6, (4, 6))
+        finish(4, 6, (5, 6))
         values(7)
         project_pass(0, 6 * P, 7 * P, (1, 2))
         project_pass(0, 7 * P, 8 * P, (7, 0))

@@ -20,8 +20,7 @@ P = 128
 HALF = 512
 QUARTER = 256
 TAIL = 384
-EARLY_WARM_UPS = 4
-WARM_UPS = 2
+WARM_UPS = 5
 MX_ALIGN = 64
 SHIFT = 16
 
@@ -34,9 +33,10 @@ def tile_list_clicked_item_candidates_kernel(
         keep = ctx.enter_context(tc.tile_pool(name="keep", bufs=1))
         psum = ctx.enter_context(tc.psum_pool(name="psum", bufs=1))
         banks = [psum.tile([P, HALF], F32, name="bank%d" % i) for i in range(8)]
+        low, high = banks[:4], banks[4:]
 
-        def sbuf(name, shape, dtype, tag=None):
-            return keep.tile(shape, dtype, name=name, tag=tag or name, align_bytes=MX_ALIGN)
+        def sbuf(name, shape, dtype):
+            return keep.tile(shape, dtype, name=name, align_bytes=MX_ALIGN)
 
         pairs = [(x, y) for x in range(2) for y in range(2)]
         offsets = keep.tile([P, S // 16], U16, name="offsets")
@@ -45,40 +45,37 @@ def tile_list_clicked_item_candidates_kernel(
         warm = sbuf("warm", [P, 2], F32)
         tab_w = [sbuf("tab_w%d" % a, [P, T], I32) for a in range(2)]
         tab_s = sbuf("tab_s", [P, T // 4], I32)
+        v_w = [sbuf("v_w%d" % a, [P, S], U32) for a in range(2)]
         v_s = sbuf("v_s", [P, S], U8)
         v_s_moved = sbuf("v_s_moved", [P, S // 4], I32)
-        v_w = {}
-        wg_w_raw = [sbuf("wg_w_raw%d" % b, [P, 2, HALF // 2], I32) for b in range(2)]
+        wg_raw = {(a, 0): sbuf("wg_raw%d0" % a, [P, HALF // 2], I32)[:] for a in range(2)}
+        wg_raw_late = sbuf("wg_raw_late", [P, 2, HALF // 2], I32)
+        for a in range(2):
+            wg_raw[a, 1] = wg_raw_late[:, a, :]
         wg_s_raw = sbuf("wg_s_raw", [P, 2, H // 4], I32)
-        wg_w = [sbuf("wg_w%d" % b, [P, 2, 2 * HALF], U8) for b in range(2)]
-        wg_s = [sbuf("wg_s%d" % b, [P, 2, HALF], U8) for b in range(2)]
-        wv_raw = {(a, b): sbuf("wv_raw%d%d" % (a, b), [P, 4 * HALF], F32)[:] for a, b in pairs}
-        shared = sbuf("shared", [P, 8 * HALF], F32)
-        last_piece = shared[:, 3 * HALF : 8 * HALF].rearrange("p (i c) -> p i c", i=4)[:, :, 3 * P : 3 * P + QUARTER]
-        wv_bf = {(a, b): sbuf("wv_bf%d%d" % (a, b), [P, 4 * HALF], BF16)[:] for a, b in pairs[:3]}
-        turn = ctx.enter_context(tc.tile_pool(name="turn", bufs=1))
-
-        def placed(name, shape, dtype, offset):
-            return turn.tile(shape, dtype, name=name, align_bytes=MX_ALIGN, offset=offset)[:]
-
-        wv_bf[1, 1] = placed("wv_bf11", [P, 4 * HALF + MX_ALIGN // 2], BF16, 0)[:, 0 : 4 * HALF]
-        wv_w = sbuf("wv_w", [P, 2, H], U32)
-        wv_s = sbuf("wv_s", [P, 2, H], U8)
-        gate = {(b, u): sbuf("gate%d%d" % (b, u), [P, 4, HALF], F32)[:] for b, u in pairs[:2]}
-        for u in range(2):
-            gate[1, u] = shared[:, 4 * u * HALF : 4 * (u + 1) * HALF].rearrange("p (t j) -> p t j", t=4)
-        h_bf = {}
-        for b, u in pairs:
-            whole = sbuf("h_bf%d%d" % (b, u), [P, 4 * HALF], BF16)
-            for c0, c1 in ((0, 4), (0, 2), (2, 4)) + tuple((c, c + 1) for c in range(4)):
-                h_bf[b, u, c0, c1] = whole[:, c0 * HALF : c1 * HALF]
-        h_w = {(b, u): sbuf("h_w%d%d" % (b, u), [P, HALF], U32)[:] for b, u in pairs[2:]}
-        for u in range(2):
-            h_w[0, u] = placed("h_w0%d" % u, [P, HALF], U32, 4 * HALF * (u + 1))
-        h_s = sbuf("h_s", [P, 2, S], U8)
+        wg_w = {(a, b): sbuf("wg_w%d%d" % (a, b), [P, 2 * HALF], U8) for a, b in pairs}
+        wg_s = {(a, b): sbuf("wg_s%d%d" % (a, b), [P, HALF], U8) for a, b in pairs}
+        cuts = {(0, 0): QUARTER, (1, 0): TAIL, (0, 1): P, (1, 1): QUARTER}
+        wv_parts = {}
+        for a, b in pairs:
+            ends = sorted({0, cuts[a, b], HALF})[: 2 if (a, b) == (1, 1) else 3]
+            wv_parts[a, b] = [
+                (c0, c1, sbuf("wv_raw%d%d_%d" % (a, b, c0), [P, 4, c1 - c0], F32)[:]) for c0, c1 in zip(ends, ends[1:])
+            ]
+        gate = {(b, u): sbuf("gate%d%d" % (b, u), [P, 4, HALF], F32) for b, u in pairs}
+        wv_parts[1, 1].append((QUARTER, HALF, gate[1, 1][:, :, 0:QUARTER]))
+        wv_bf = {(a, b): sbuf("wv_bf%d%d" % (a, b), [P, 4 * HALF], BF16) for a, b in pairs}
+        wv_w = {(a, b): sbuf("wv_w%d%d" % (a, b), [P, HALF], U32) for a, b in pairs}
+        wv_s = {(a, b): sbuf("wv_s%d%d" % (a, b), [P, HALF], U8) for a, b in pairs}
+        h_bf = [sbuf("h_bf%d" % b, [P, 4 * S], BF16) for b in range(2)]
+        h_w = [sbuf("h_w%d" % b, [P, S], U32) for b in range(2)]
+        h_s = [sbuf("h_s%d" % b, [P, S], U8) for b in range(2)]
         wd_w = sbuf("wd_w", [P, 2, N], I32)
         wd_s = sbuf("wd_s", [P, 2, N // 4], I32)
         y_sb = sbuf("y_sb", [P, 2, S], F32)
+        zeros_bf = sbuf("zeros_bf", [P, 4 * HALF], BF16)
+        zeros_w = sbuf("zeros_w", [P, HALF], U32)
+        zeros_s = sbuf("zeros_s", [P, HALF], U8)
 
         def scale_rows(scales, s):
             return scales.bitcast(I32).rearrange("a (q s) w -> s q a w", s=4)[s]
@@ -87,298 +84,251 @@ def tile_list_clicked_item_candidates_kernel(
             for s in range(4):
                 nc.sync.dma_start(out=planes[s:P:32, :, :], in_=scale_rows(scales, s))
 
-        def load_table_scales():
-            for s in range(4):
-                nc.sync.dma_start(out=tab_s[s:P:16, :], in_=scale_rows(tab_scales, s))
-
         def load_table_words(a):
             nc.sync.dma_start(out=tab_w[a][:], in_=tab_words[a].rearrange("p n i -> p (n i)").bitcast(I32))
 
-        def load_wg_words(b):
-            words = wg_words.bitcast(I32)[:, :, b * (HALF // 2) : (b + 1) * (HALF // 2)]
-            nc.sync.dma_start(out=wg_w_raw[b][:], in_=words.rearrange("a p w -> p a w"))
+        def load_wv(a, b):
+            for c0, c1, raw in wv_parts[a, b]:
+                rows = wv[a * HALF : (a + 1) * HALF, b * HALF + c0 : b * HALF + c1]
+                nc.sync.dma_start(out=raw, in_=rows.rearrange("(p i) c -> p i c", i=4))
 
-        def wv_piece(a, b, c0, c1):
-            if (a, b, c1) == (1, 1, HALF):
-                return last_piece
-            return wv_raw[a, b][:, 4 * c0 : 4 * c1].rearrange("p (i c) -> p i c", i=4)
-
-        def load_wv(a, b, c0=0, c1=HALF):
-            rows = wv[a * HALF : (a + 1) * HALF, b * HALF + c0 : b * HALF + c1]
-            nc.sync.dma_start(out=wv_piece(a, b, c0, c1), in_=rows.rearrange("(p i) c -> p i c", i=4))
-
-        def round_wv(copy, a, b, t0, c0=0, c1=HALF, width=2):
-            dst = wv_bf[a, b][:].rearrange("p (t m i) -> p m i t", t=4, i=4)[:, c0 // 4 : c1 // 4, :, :]
-            src = wv_piece(a, b, c0, c1).rearrange("p i (m t) -> p m i t", t=4)
-            copy(out=dst[:, :, :, t0 : t0 + width], in_=src[:, :, :, t0 : t0 + width])
+        def round_wv(copy, a, b, width, order=(0, 2), parts=slice(0, 2)):
+            for c0, c1, raw in wv_parts[a, b][parts]:
+                dst = wv_bf[a, b][:].rearrange("p (t m i) -> p m i t", t=4, i=4)[:, c0 // 4 : c1 // 4, :, :]
+                src = raw.rearrange("p i (m t) -> p m i t", t=4)
+                for t0 in order if width == 2 else (0,):
+                    copy(out=dst[:, :, :, t0 : t0 + width], in_=src[:, :, :, t0 : t0 + width])
 
         def quantize_wv(a, b, t0, t1):
-            cols = slice(b * HALF + t0 * P, b * HALF + t1 * P)
+            cols = slice(t0 * P, t1 * P)
             nc.vector.quantize_mx(
-                out=wv_w[:, a, cols].bitcast(FP8X4), scales=wv_s[:, a, cols], in_=wv_bf[a, b][:, t0 * HALF : t1 * HALF]
+                out=wv_w[a, b][:, cols].bitcast(FP8X4),
+                scales=wv_s[a, b][:, cols],
+                in_=wv_bf[a, b][:, t0 * HALF : t1 * HALF],
             )
 
-        def reorder_wg_words(b):
-            nc.vector.tensor_copy(
-                out=wg_w[b][:].bitcast(U16).rearrange("p a (t m) -> p a t m", t=4),
-                in_=wg_w_raw[b][:].bitcast(U16).rearrange("p a (m t) -> p a t m", t=4),
+        def reorder_wg_words(a, b):
+            nc.scalar.copy(
+                out=wg_w[a, b][:].bitcast(U16).rearrange("p (t m) -> p t m", t=4),
+                in_=wg_raw[a, b].bitcast(U16).rearrange("p (m t) -> p t m", t=4),
             )
 
-        def reorder_wg_scales(b, a0, a1):
+        def reorder_wg_scales(a, b):
             nc.gpsimd.tensor_copy(
-                out=wg_s[b][:, a0:a1, :].rearrange("p a (t m) -> p a t m", t=4),
-                in_=wg_s_raw[:].bitcast(U8)[:, a0:a1, b * HALF : (b + 1) * HALF].rearrange("p a (m t) -> p a t m", t=4),
+                out=wg_s[a, b][:].rearrange("p (t m) -> p t m", t=4),
+                in_=wg_s_raw[:].bitcast(U8)[:, a, b * HALF : (b + 1) * HALF].rearrange("p (m t) -> p t m", t=4),
             )
 
-        def gather_scales():
-            nc.vector.tensor_copy(out=v_s[:], in_=tab_s[:].bitcast(U8).indirect(offsets[:]))
-            for s in range(4):
-                nc.sync.dma_start(out=v_s_moved[s:P:32, :], in_=v_s[SHIFT + s : P : 32, :].bitcast(I32))
-
-        def gather_words(a, u, dst):
-            v_w[a, u] = dst
-            picks = offsets[:, u * (HALF // 16) : (u + 1) * (HALF // 16)]
-            nc.vector.tensor_copy(out=dst, in_=tab_w[a][:].bitcast(U32).indirect(picks))
+        def gather_words(a, q):
+            picks = offsets[:, q * (QUARTER // 16) : (q + 1) * (QUARTER // 16)]
+            nc.vector.tensor_copy(
+                out=v_w[a][:, q * QUARTER : (q + 1) * QUARTER], in_=tab_w[a][:].bitcast(U32).indirect(picks)
+            )
 
         def v_plane(a, j0, j1):
             return (v_s[:] if a == 0 else v_s_moved[:].bitcast(U8))[:, j0:j1]
 
-        def gate_pass(bank, a, b, t, u):
+        def gate_pass(bank, a, b, t, j0, j1, start, stop):
             nc.tensor.matmul_mx(
-                out=bank[:],
-                lhsT=wg_w[b][:, a, 2 * t * P : 2 * (t + 1) * P].bitcast(FP4X4),
-                lhsT_scale=wg_s[b][:, a, t * P : (t + 1) * P],
-                rhs=v_w[a, u].bitcast(FP8X4),
-                rhs_scale=v_plane(a, u * HALF, (u + 1) * HALF),
-                start=(a == 0),
-                stop=(a == 1),
-            )
-
-        def sigmoid(bank, b, t, u):
-            nc.scalar.activation(out=gate[b, u][:, t, :], in_=bank[:], func=ACT.Sigmoid, bias=bg_sb[:, b, t : t + 1])
-
-        def gate_sums(b, u, ts, used):
-            for t in ts:
-                for a in range(2):
-                    gate_pass(banks[used[t]], a, b, t, u)
-
-        def sigmoids(b, u, used, ts=range(4)):
-            for t in ts:
-                sigmoid(banks[used[t]], b, t, u)
-
-        def value_pass(b, u, c, bank, a, t, start, stop):
-            cols = slice(b * HALF + t * P, b * HALF + (t + 1) * P)
-            nc.tensor.matmul_mx(
-                out=bank[:, t * P : (t + 1) * P],
-                lhsT=wv_w[:, a, cols].bitcast(FP8X4),
-                lhsT_scale=wv_s[:, a, cols],
-                rhs=v_w[a, u][:, c * P : (c + 1) * P].bitcast(FP8X4),
-                rhs_scale=v_plane(a, u * HALF + c * P, u * HALF + (c + 1) * P),
+                out=bank[:, j0 % HALF : j0 % HALF + j1 - j0],
+                lhsT=wg_w[a, b][:, 2 * t * P : 2 * (t + 1) * P].bitcast(FP4X4),
+                lhsT_scale=wg_s[a, b][:, t * P : (t + 1) * P],
+                rhs=v_w[a][:, j0:j1].bitcast(FP8X4),
+                rhs_scale=v_plane(a, j0, j1),
                 start=start,
                 stop=stop,
             )
 
-        def open_values(b, u, c, bank):
+        def gate_sums(b, u, used, ts=range(4)):
+            for t in ts:
+                for a in range(2):
+                    gate_pass(used[t], a, b, t, u * HALF, (u + 1) * HALF, a == 0, a == 1)
+
+        def sigmoids(b, u, used):
             for t in range(4):
-                value_pass(b, u, c, bank, 0, t, t == 0, False)
+                nc.scalar.activation(
+                    out=gate[b, u][:, t, :], in_=used[t][:], func=ACT.Sigmoid, bias=bg_sb[:, b, t : t + 1]
+                )
 
-        def value_sums(b, u, c, bank, opened):
-            if opened:
-                for t in (2, 3, 0, 1):
-                    value_pass(b, u, c, bank, 1, t, False, t == 1)
-            else:
-                for t in range(4):
-                    for a in (1, 0):
-                        value_pass(b, u, c, bank, a, t, a == 1, a == 0)
+        def value_passes(b, c, bank, a, ts, start, stop):
+            for t in ts:
+                nc.tensor.matmul_mx(
+                    out=bank[:, t * P : (t + 1) * P],
+                    lhsT=wv_w[a, b][:, t * P : (t + 1) * P].bitcast(FP8X4),
+                    lhsT_scale=wv_s[a, b][:, t * P : (t + 1) * P],
+                    rhs=v_w[a][:, c * P : (c + 1) * P].bitcast(FP8X4),
+                    rhs_scale=v_plane(a, c * P, (c + 1) * P),
+                    start=start and t == ts[0],
+                    stop=stop and t == ts[-1],
+                )
 
-        def product(b, u, c, bank):
+        def open_values(b, c, bank):
+            value_passes(b, c, bank, 0, (0, 1, 2, 3), True, False)
+
+        def close_values(b, c, bank):
+            value_passes(b, c, bank, 1, (2, 3, 0, 1), False, True)
+
+        def product(b, c, bank):
             nc.vector.tensor_tensor(
-                out=h_bf[b, u, c, c + 1].rearrange("p (j e t) -> p j t e", e=2, t=4),
+                out=h_bf[b][:, c * HALF : (c + 1) * HALF].rearrange("p (j e t) -> p j t e", e=2, t=4),
                 in0=bank[:].rearrange("p (t j e) -> p j t e", t=4, e=2),
-                in1=gate[b, u][:, :, c * P : (c + 1) * P].rearrange("p t (j e) -> p j t e", e=2),
+                in1=gate[b, c // 4][:, :, (c % 4) * P : (c % 4 + 1) * P].rearrange("p t (j e) -> p j t e", e=2),
                 op=ALU.mult,
             )
 
-        def gated_values(b, u, c, bank, opened=False):
-            value_sums(b, u, c, bank, opened)
-            product(b, u, c, bank)
-
-        def quantize_h(b, u, c0, c1):
-            cols = slice(u * HALF + c0 * P, u * HALF + c1 * P)
+        def quantize_h(b, c0, c1):
+            cols = slice(c0 * P, c1 * P)
             nc.vector.quantize_mx(
-                out=h_w[b, u][:, c0 * P : c1 * P].bitcast(FP8X4),
-                scales=h_s[:, b, cols],
-                in_=h_bf[b, u, c0, c1],
+                out=h_w[b][:, cols].bitcast(FP8X4), scales=h_s[b][:, cols], in_=h_bf[b][:, c0 * HALF : c1 * HALF]
             )
 
-        def project_pass(b, j0, j1, used, first=0):
+        def project_pass(b, c0, c1, used):
             for n in range(2):
                 nc.tensor.matmul_mx(
-                    out=banks[used[n]][:, 0 : j1 - j0],
+                    out=used[n][:, 0 : (c1 - c0) * P],
                     lhsT=wd_w[:, b, n * P : (n + 1) * P].bitcast(FP8X4),
                     lhsT_scale=wd_s[:, b, :].bitcast(U8)[:, n * P : (n + 1) * P],
-                    rhs=h_w[b, j0 // HALF][:, j0 % HALF : j0 % HALF + j1 - j0].bitcast(FP8X4),
-                    rhs_scale=h_s[:, b, j0:j1],
-                    start=(b == first),
-                    stop=(b != first),
+                    rhs=h_w[b][:, c0 * P : c1 * P].bitcast(FP8X4),
+                    rhs_scale=h_s[b][:, c0 * P : c1 * P],
+                    start=(b == 0),
+                    stop=(b == 1),
                 )
 
-        def store(j0, j1, used):
-            cols = slice(j0, j1)
+        def store(c0, c1, used):
+            cols = slice(c0 * P, c1 * P)
             for n in range(2):
-                sums = banks[used[n]][:, 0 : j1 - j0]
+                sums = used[n][:, 0 : (c1 - c0) * P]
                 bias = bd_sb[:, n : n + 1]
-                if n == 1 and j1 - j0 == P:
+                if n == 1 and c1 - c0 == 1:
                     nc.vector.tensor_scalar(out=y_sb[:, n, cols], in0=sums, scalar1=bias, scalar2=None, op0=ALU.add)
                 else:
                     nc.scalar.activation(out=y_sb[:, n, cols], in_=sums, func=ACT.Identity, bias=bias)
-                if j1 - j0 > P:
+                if c1 - c0 > 1 and c0 > 0:
                     nc.sync.dma_start(out=out[n * P : (n + 1) * P, cols], in_=y_sb[:, n, cols])
-            if j1 - j0 == P:
+            if c1 - c0 == 1 or c0 == 0:
                 nc.sync.dma_start(out=out.rearrange("(n p) j -> p n j", n=2)[:, :, cols], in_=y_sb[:, :, cols])
 
-        nc.vector.memset(tab_s[:], 0)
+        nc.gpsimd.memset(tab_s[:], 0)
         nc.gpsimd.memset(warm[:], 0.0)
         for planes in (wg_s_raw, v_s_moved, wd_s):
             nc.gpsimd.memset(planes[:], 0)
-        zeros_bf = sbuf("zeros_bf", [P, 4 * P], BF16)
-        zeros_w = sbuf("zeros_w", [P, P], U32)
-        zeros_s = sbuf("zeros_s", [P, P], U8)
         nc.vector.memset(zeros_bf[:].bitcast(I32), 0)
         nc.vector.quantize_mx(out=zeros_w[:].bitcast(FP8X4), scales=zeros_s[:], in_=zeros_bf[:])
         nc.scalar.activation(out=warm[:, 1:2], in_=warm[:, 0:1], func=ACT.Sigmoid)
 
+        wg_i32 = wg_words.bitcast(I32)
+        nc.sync.dma_start(out=wg_raw[0, 0], in_=wg_i32[0, :, 0 : HALF // 2])
+        for s in range(4):
+            nc.sync.dma_start(out=tab_s[s:P:SHIFT, :], in_=scale_rows(tab_scales, s))
         nc.sync.dma_start(offsets[:], offs)
-        load_wg_words(0)
-        load_table_scales()
         load_table_words(0)
         load_planes(wg_s_raw, wg_scales)
         load_table_words(1)
-        nc.scalar.dma_start(out=bg_sb[:], in_=bg.rearrange("(b p t) -> p b t", b=2, t=4))
-        load_wg_words(1)
-        reorder_wg_words(0)
-        gather_scales()
-        load_wv(0, 0)
-        load_wv(1, 0, 0, TAIL)
-        load_wv(1, 0, TAIL, HALF)
-        for a in range(2):
-            load_wv(a, 1, 0, QUARTER)
-            load_wv(a, 1, QUARTER, HALF)
+        nc.sync.dma_start(out=wg_raw[1, 0], in_=wg_i32[1, :, 0 : HALF // 2])
+        nc.sync.dma_start(out=bg_sb[:], in_=bg.rearrange("(b p t) -> p b t", b=2, t=4))
+        nc.vector.tensor_copy(out=v_s[:], in_=tab_s[:].bitcast(U8).indirect(offsets[:]))
+        for s in range(4):
+            nc.sync.dma_start(out=v_s_moved[s:P:32, :], in_=v_s[SHIFT + s : P : 32, :].bitcast(I32))
+        nc.sync.dma_start(out=wg_raw_late[:], in_=wg_i32[:, :, HALF // 2 : HALF].rearrange("a p w -> p a w"))
         for b in range(2):
-            nc.sync.dma_start(out=wd_w[:, b, :], in_=wd_words[b].rearrange("p n i -> p (n i)").bitcast(I32))
+            for a in range(2):
+                load_wv(a, b)
+        nc.sync.dma_start(out=wd_w[:], in_=wd_words.rearrange("b p n i -> p b (n i)").bitcast(I32))
         load_planes(wd_s, wd_scales)
         with nc.allow_non_contiguous_dma(reason="one bias value for each partition"):
             nc.sync.dma_start(out=bd_sb[:], in_=bd.rearrange("(n p) -> p n", n=2))
 
-        for warm_up in range(EARLY_WARM_UPS):
-            nc.tensor.matmul_mx(
-                out=banks[7][:],
-                lhsT=zeros_w[:].bitcast(FP8X4),
-                lhsT_scale=zeros_s[:],
-                rhs=wg_w_raw[0][:, 0, :].bitcast(U8).bitcast(FP4X4),
-                rhs_scale=tab_s[:].bitcast(U8)[:, 0:HALF],
-                start=True,
-                stop=True,
-            )
         for warm_up in range(WARM_UPS):
             nc.tensor.matmul_mx(
                 out=banks[7][:],
-                lhsT=wg_w[0][:, 0, 0 : 2 * P].bitcast(FP4X4),
-                lhsT_scale=tab_s[:].bitcast(U8)[:, 0:P],
-                rhs=tab_w[0][:, 0:HALF].bitcast(FP8X4),
-                rhs_scale=tab_s[:].bitcast(U8)[:, 0:HALF],
+                lhsT=zeros_w[:, 0:P].bitcast(FP8X4),
+                lhsT_scale=zeros_s[:, 0:P],
+                rhs=wg_raw[0, 0].bitcast(U8).bitcast(FP4X4),
+                rhs_scale=zeros_s[:],
                 start=True,
                 stop=True,
             )
-        reorder_wg_scales(0, 0, 1)
-        reorder_wg_scales(0, 1, 2)
-        reorder_wg_scales(1, 0, 2)
-        v_all = sbuf("v_all", [P, 4 * HALF], U32)
-        for a in range(2):
-            for u in range(2):
-                gather_words(a, u, v_all[:, (2 * a + u) * HALF : (2 * a + u + 1) * HALF])
-        low, high = (0, 1, 2, 3), (4, 5, 6, 7)
-        reorder_wg_words(1)
-        round_wv(nc.vector.tensor_copy, 0, 0, 0)
-        round_wv(nc.vector.tensor_copy, 0, 0, 2)
-        for a in range(2):
-            for u in range(2):
-                for t in range(4):
-                    gate_pass(banks[4 * u + t], a, 0, t, u)
+        for b in range(2):
+            for a in range(2):
+                reorder_wg_words(a, b)
+                reorder_wg_scales(a, b)
+        for a, q in ((0, 0), (0, 1), (0, 2), (1, 0), (1, 1), (0, 3), (1, 2), (1, 3)):
+            gather_words(a, q)
+            for t in range(4):
+                first, final = (a, q % 2) == (0, 0), (a, q % 2) == (1, 1)
+                gate_pass(banks[4 * (q // 2) + t], a, 0, t, q * QUARTER, (q + 1) * QUARTER, first, final)
         sigmoids(0, 0, low)
         sigmoids(0, 1, high)
-        for t in range(4):
-            gate_sums(1, 0, [t], low)
-        sigmoids(1, 0, low, (0, 1, 2))
+        gate_sums(1, 0, low)
+        sigmoids(1, 0, low)
 
-        quantize_wv(0, 0, 0, 2)
-        quantize_wv(0, 0, 2, 4)
-        for c0, c1 in ((0, TAIL), (TAIL, HALF)):
-            for t0 in (2, 0):
-                round_wv(nc.vector.tensor_copy, 1, 0, t0, c0, c1)
+        round_wv(nc.vector.tensor_copy, 0, 0, 2)
+        quantize_wv(0, 0, 0, 4)
+        round_wv(nc.vector.tensor_copy, 1, 0, 2, (2, 0))
         quantize_wv(1, 0, 2, 4)
         quantize_wv(1, 0, 0, 2)
-        for t0 in (0, 2):
-            round_wv(nc.vector.tensor_copy, 0, 1, t0, 0, QUARTER)
-        round_wv(nc.scalar.copy, 0, 1, 0, QUARTER, HALF, 4)
-        round_wv(nc.scalar.copy, 1, 1, 0, 0, QUARTER, 4)
-        round_wv(nc.scalar.copy, 1, 1, 0, QUARTER, HALF, 4)
+        round_wv(nc.vector.tensor_copy, 0, 1, 2, parts=slice(0, 1))
+        round_wv(nc.scalar.copy, 0, 1, 4, parts=slice(1, 2))
+        round_wv(nc.scalar.copy, 1, 1, 4)
 
-        sigmoids(1, 0, low, (3,))
-        last = (5, 6, 7, 0)
-        for c in range(2):
-            open_values(0, 0, c, banks[high[c]])
-        for c in range(4):
-            gated_values(0, 0, c, banks[high[c]], c < 2)
-        gated_values(0, 1, 0, banks[0])
-        gated_values(0, 1, 1, banks[1])
-        quantize_wv(0, 1, 0, 4)
-        gated_values(0, 1, 2, banks[2])
-        gated_values(0, 1, 3, banks[4])
-        gate_sums(1, 1, range(4), last)
-        ring = (1, 2, 4, 3)
+        gate_sums(1, 1, high, (0,))
+        ring = high[1:] + low + high[1:2]
         for c in range(3):
-            open_values(1, 0, c, banks[ring[c]])
+            open_values(0, c, ring[c])
+        for c in range(8):
+            bank = ring[c]
+            if c >= 3:
+                open_values(0, c, bank)
+            close_values(0, c, bank)
+            product(0, c, bank)
+        last = [high[0], high[2], high[3], low[0]]
+        gate_sums(1, 1, last, (1, 2, 3))
+        quantize_wv(0, 1, 0, 4)
+        quantize_h(0, 0, 4)
         quantize_wv(1, 1, 2, 4)
         quantize_wv(1, 1, 0, 2)
-        quantize_h(0, 0, 0, 4)
-        quantize_h(0, 1, 0, 4)
+        quantize_h(0, 4, 8)
         sigmoids(1, 1, last)
+        ring = low[1:] + high[1:2] + last
 
-        def quantize_chunks(c0, c1):
-            quantize_h(1, c0 // 4, c0 % 4, c0 % 4 + c1 - c0)
-
-        def finish(c0, c1, used):
-            project_pass(1, c0 * P, c1 * P, used)
-            store(c0 * P, c1 * P, used)
+        for c in range(2):
+            open_values(1, c, ring[c])
+        for c in range(4):
+            if c >= 2:
+                open_values(1, c, ring[c])
+            close_values(1, c, ring[c])
 
         def values(c):
-            product(1, c // 4, c % 4, banks[ring[c % 4]])
-            if c < 4:
-                value_sums(1, 1, c, banks[ring[c]], False)
+            open_values(1, c, ring[c])
+            close_values(1, c, ring[c])
 
-        for c in range(4):
-            value_sums(1, 0, c, banks[ring[c]], c < 3)
-        values(0)
-        values(1)
-        values(2)
-        project_pass(0, 0, 2 * P, (5, 6))
-        quantize_chunks(0, 2)
-        finish(0, 2, (5, 6))
-        values(3)
+        def finish(c0, c1, used):
+            project_pass(1, c0, c1, used)
+            store(c0, c1, used)
+
         values(4)
-        project_pass(0, 2 * P, 4 * P, (7, 0))
-        quantize_chunks(2, 4)
-        finish(2, 4, (7, 0))
         values(5)
+        for c in range(3):
+            product(1, c, ring[c])
+        project_pass(0, 0, 2, ring[0:2])
+        quantize_h(1, 0, 2)
+        finish(0, 2, ring[0:2])
         values(6)
-        project_pass(0, 4 * P, 6 * P, (5, 6))
-        quantize_chunks(4, 6)
-        finish(4, 6, (5, 6))
         values(7)
-        project_pass(0, 6 * P, 7 * P, (1, 2))
-        project_pass(0, 7 * P, 8 * P, (7, 0))
-        quantize_chunks(6, 7)
-        quantize_chunks(7, 8)
-        finish(6, 7, (1, 2))
-        finish(7, 8, (7, 0))
+        product(1, 3, ring[3])
+        product(1, 4, ring[4])
+        project_pass(0, 2, 4, ring[2:4])
+        quantize_h(1, 2, 4)
+        finish(2, 4, ring[2:4])
+        product(1, 5, ring[5])
+        product(1, 6, ring[6])
+        project_pass(0, 4, 6, ring[4:6])
+        quantize_h(1, 4, 6)
+        finish(4, 6, ring[4:6])
+        product(1, 7, ring[7])
+        project_pass(0, 6, 7, ring[0:2])
+        project_pass(0, 7, 8, ring[2:4])
+        quantize_h(1, 6, 7)
+        quantize_h(1, 7, 8)
+        finish(6, 7, ring[0:2])
+        finish(7, 8, ring[2:4])

@@ -21,6 +21,7 @@ HALF = 512
 QUARTER = 256
 TAIL = 384
 WARM_UPS = 5
+LATE_WARM_UPS = 2
 MX_ALIGN = 64
 SHIFT = 16
 
@@ -73,9 +74,9 @@ def tile_list_clicked_item_candidates_kernel(
         wd_w = sbuf("wd_w", [P, 2, N], I32)
         wd_s = sbuf("wd_s", [P, 2, N // 4], I32)
         y_sb = sbuf("y_sb", [P, 2, S], F32)
-        zeros_bf = sbuf("zeros_bf", [P, 4 * HALF], BF16)
-        zeros_w = sbuf("zeros_w", [P, HALF], U32)
-        zeros_s = sbuf("zeros_s", [P, HALF], U8)
+        zeros_bf = sbuf("zeros_bf", [P, 4 * P], BF16)
+        zeros_w = sbuf("zeros_w", [P, P], U32)
+        zeros_s = sbuf("zeros_s", [P, P], U8)
 
         def scale_rows(scales, s):
             return scales.bitcast(I32).rearrange("a (q s) w -> s q a w", s=4)[s]
@@ -244,7 +245,17 @@ def tile_list_clicked_item_candidates_kernel(
                 lhsT=zeros_w[:, 0:P].bitcast(FP8X4),
                 lhsT_scale=zeros_s[:, 0:P],
                 rhs=wg_raw[0, 0].bitcast(U8).bitcast(FP4X4),
-                rhs_scale=zeros_s[:],
+                rhs_scale=tab_s[:].bitcast(U8)[:, 0:HALF],
+                start=True,
+                stop=True,
+            )
+        for warm_up in range(LATE_WARM_UPS):
+            nc.tensor.matmul_mx(
+                out=banks[7][:],
+                lhsT=zeros_w[:].bitcast(FP8X4),
+                lhsT_scale=zeros_s[:],
+                rhs=tab_w[0][:, 0:HALF].bitcast(FP8X4),
+                rhs_scale=tab_s[:].bitcast(U8)[:, 0:HALF],
                 start=True,
                 stop=True,
             )
@@ -252,7 +263,7 @@ def tile_list_clicked_item_candidates_kernel(
             for a in range(2):
                 reorder_wg_words(a, b)
                 reorder_wg_scales(a, b)
-        for a, q in ((0, 0), (0, 1), (0, 2), (1, 0), (1, 1), (0, 3), (1, 2), (1, 3)):
+        for a, q in [(a, q) for a in range(2) for q in range(4)]:
             gather_words(a, q)
             for t in range(4):
                 first, final = (a, q % 2) == (0, 0), (a, q % 2) == (1, 1)

@@ -22,7 +22,7 @@ QUARTER = 256
 TAIL = 384
 WARM_UPS = 5
 LATE_WARM_UPS = 2
-MX_ALIGN = 64
+MX_ALIGN = 256
 SHIFT = 16
 
 
@@ -56,7 +56,7 @@ def tile_list_clicked_item_candidates_kernel(
         wg_s_raw = sbuf("wg_s_raw", [P, 2, H // 4], I32)
         wg_w = {(a, b): sbuf("wg_w%d%d" % (a, b), [P, 2 * HALF], U8) for a, b in pairs}
         wg_s = {(a, b): sbuf("wg_s%d%d" % (a, b), [P, HALF], U8) for a, b in pairs}
-        cuts = {(0, 0): QUARTER, (1, 0): TAIL, (0, 1): P, (1, 1): QUARTER}
+        cuts = {(0, 0): HALF, (1, 0): TAIL, (0, 1): P, (1, 1): QUARTER}
         wv_parts = {}
         for a, b in pairs:
             ends = sorted({0, cuts[a, b], HALF})[: 2 if (a, b) == (1, 1) else 3]
@@ -169,6 +169,10 @@ def tile_list_clicked_item_candidates_kernel(
         def close_values(b, c, bank):
             value_passes(b, c, bank, 1, (2, 3, 0, 1), False, True)
 
+        def whole_values(b, c, bank):
+            value_passes(b, c, bank, 1, (2, 3, 0, 1), True, False)
+            value_passes(b, c, bank, 0, (0, 1, 2, 3), False, True)
+
         def product(b, c, bank):
             nc.vector.tensor_tensor(
                 out=h_bf[b][:, c * HALF : (c + 1) * HALF].rearrange("p (j e t) -> p j t e", e=2, t=4),
@@ -204,9 +208,9 @@ def tile_list_clicked_item_candidates_kernel(
                     nc.vector.tensor_scalar(out=y_sb[:, n, cols], in0=sums, scalar1=bias, scalar2=None, op0=ALU.add)
                 else:
                     nc.scalar.activation(out=y_sb[:, n, cols], in_=sums, func=ACT.Identity, bias=bias)
-                if c1 - c0 > 1 and c0 > 0:
+                if c1 - c0 > 1:
                     nc.sync.dma_start(out=out[n * P : (n + 1) * P, cols], in_=y_sb[:, n, cols])
-            if c1 - c0 == 1 or c0 == 0:
+            if c1 - c0 == 1:
                 nc.sync.dma_start(out=out.rearrange("(n p) j -> p n j", n=2)[:, :, cols], in_=y_sb[:, :, cols])
 
         nc.gpsimd.memset(tab_s[:], 0)
@@ -223,10 +227,10 @@ def tile_list_clicked_item_candidates_kernel(
             nc.sync.dma_start(out=tab_s[s:P:SHIFT, :], in_=scale_rows(tab_scales, s))
         nc.sync.dma_start(offsets[:], offs)
         load_table_words(0)
+        nc.scalar.dma_start(out=bg_sb[:], in_=bg.rearrange("(b p t) -> p b t", b=2, t=4))
         load_planes(wg_s_raw, wg_scales)
         load_table_words(1)
         nc.sync.dma_start(out=wg_raw[1, 0], in_=wg_i32[1, :, 0 : HALF // 2])
-        nc.sync.dma_start(out=bg_sb[:], in_=bg.rearrange("(b p t) -> p b t", b=2, t=4))
         nc.vector.tensor_copy(out=v_s[:], in_=tab_s[:].bitcast(U8).indirect(offsets[:]))
         for s in range(4):
             nc.sync.dma_start(out=v_s_moved[s:P:32, :], in_=v_s[SHIFT + s : P : 32, :].bitcast(I32))
@@ -274,7 +278,8 @@ def tile_list_clicked_item_candidates_kernel(
         sigmoids(1, 0, low)
 
         round_wv(nc.vector.tensor_copy, 0, 0, 2)
-        quantize_wv(0, 0, 0, 4)
+        quantize_wv(0, 0, 0, 2)
+        quantize_wv(0, 0, 2, 4)
         round_wv(nc.vector.tensor_copy, 1, 0, 2, (2, 0))
         quantize_wv(1, 0, 2, 4)
         quantize_wv(1, 0, 0, 2)
@@ -289,8 +294,9 @@ def tile_list_clicked_item_candidates_kernel(
         for c in range(8):
             bank = ring[c]
             if c >= 3:
-                open_values(0, c, bank)
-            close_values(0, c, bank)
+                whole_values(0, c, bank)
+            else:
+                close_values(0, c, bank)
             product(0, c, bank)
         last = [high[0], high[2], high[3], low[0]]
         gate_sums(1, 1, last, (1, 2, 3))
@@ -306,12 +312,12 @@ def tile_list_clicked_item_candidates_kernel(
             open_values(1, c, ring[c])
         for c in range(4):
             if c >= 2:
-                open_values(1, c, ring[c])
-            close_values(1, c, ring[c])
+                whole_values(1, c, ring[c])
+            else:
+                close_values(1, c, ring[c])
 
         def values(c):
-            open_values(1, c, ring[c])
-            close_values(1, c, ring[c])
+            whole_values(1, c, ring[c])
 
         def finish(c0, c1, used):
             project_pass(1, c0, c1, used)

@@ -108,23 +108,22 @@ def tile_list_clicked_item_candidates_kernel(
                 in_=wv_bf[a, b][:, t0 * HALF : t1 * HALF],
             )
 
-        def reorder_wg_words(a, b):
-            nc.scalar.copy(
-                out=wg_w[a, b][:].bitcast(U16).rearrange("p (t m) -> p t m", t=4),
-                in_=wg_raw[a, b].bitcast(U16).rearrange("p (m t) -> p t m", t=4),
+        def reorder_wg_words(a, b, t0=0, t1=4):
+            (nc.gpsimd.tensor_copy if b == 1 else nc.scalar.copy)(
+                out=wg_w[a, b][:].bitcast(U16).rearrange("p (t m) -> p t m", t=4)[:, t0:t1, :],
+                in_=wg_raw[a, b].bitcast(U16).rearrange("p (m t) -> p t m", t=4)[:, t0:t1, :],
             )
 
-        def reorder_wg_scales(a, b):
-            nc.gpsimd.tensor_copy(
-                out=wg_s[a, b][:].rearrange("p (t m) -> p t m", t=4),
-                in_=wg_s_raw[:].bitcast(U8)[:, a, b * HALF : (b + 1) * HALF].rearrange("p (m t) -> p t m", t=4),
+        def reorder_wg_scales(a, b, t0=0, t1=4, engine=nc.gpsimd):
+            raw = wg_s_raw[:].bitcast(U8)[:, a, b * HALF : (b + 1) * HALF]
+            engine.tensor_copy(
+                out=wg_s[a, b][:].rearrange("p (t m) -> p t m", t=4)[:, t0:t1, :],
+                in_=raw.rearrange("p (m t) -> p t m", t=4)[:, t0:t1, :],
             )
 
-        def gather_words(a, q):
-            picks = offsets[:, q * (QUARTER // 16) : (q + 1) * (QUARTER // 16)]
-            nc.vector.tensor_copy(
-                out=v_w[a][:, q * QUARTER : (q + 1) * QUARTER], in_=tab_w[a][:].bitcast(U32).indirect(picks)
-            )
+        def gather_words(a, j0, j1):
+            picks = offsets[:, j0 // 16 : j1 // 16]
+            nc.vector.tensor_copy(out=v_w[a][:, j0:j1], in_=tab_w[a][:].bitcast(U32).indirect(picks))
 
         def v_plane(a, j0, j1):
             return (v_s[:] if a == 0 else v_s_moved[:].bitcast(U8))[:, j0:j1]
@@ -145,8 +144,8 @@ def tile_list_clicked_item_candidates_kernel(
                 for a in range(2):
                     gate_pass(used[t], a, b, t, u * HALF, (u + 1) * HALF, a == 0, a == 1)
 
-        def sigmoids(b, u, used):
-            for t in range(4):
+        def sigmoids(b, u, used, ts=range(4)):
+            for t in ts:
                 nc.scalar.activation(
                     out=gate[b, u][:, t, :], in_=used[t][:], func=ACT.Sigmoid, bias=bg_sb[:, b, t : t + 1]
                 )
@@ -263,18 +262,30 @@ def tile_list_clicked_item_candidates_kernel(
                 start=True,
                 stop=True,
             )
-        for b in range(2):
+        reorder_wg_words(0, 0)
+        reorder_wg_words(1, 0, 0, 2)
+        reorder_wg_words(1, 0, 2, 4)
+        reorder_wg_scales(0, 0, 0, 2)
+        reorder_wg_scales(0, 0, 2, 4)
+        reorder_wg_scales(1, 0)
+        for reorder in (reorder_wg_scales, reorder_wg_words):
             for a in range(2):
-                reorder_wg_words(a, b)
-                reorder_wg_scales(a, b)
-        for a, q in [(a, q) for a in range(2) for q in range(4)]:
-            gather_words(a, q)
+                reorder(a, 1)
+        def gathered_gates(a, j0, j1):
+            gather_words(a, j0, j1)
             for t in range(4):
-                first, final = (a, q % 2) == (0, 0), (a, q % 2) == (1, 1)
-                gate_pass(banks[4 * (q // 2) + t], a, 0, t, q * QUARTER, (q + 1) * QUARTER, first, final)
+                first, final = a == 0 and j0 % HALF == 0, a == 1 and j1 % HALF == 0
+                gate_pass(banks[4 * (j0 // HALF) + t], a, 0, t, j0, j1, first, final)
+
+        for j0 in range(0, S, QUARTER):
+            gathered_gates(0, j0, j0 + QUARTER)
+        for j0, j1 in ((0, P), (P, QUARTER), (QUARTER, HALF), (HALF, HALF + QUARTER)):
+            gathered_gates(1, j0, j1)
         sigmoids(0, 0, low)
+        gate_sums(1, 0, low, (0,))
+        gathered_gates(1, HALF + QUARTER, S)
         sigmoids(0, 1, high)
-        gate_sums(1, 0, low)
+        gate_sums(1, 0, low, (1, 2, 3))
         sigmoids(1, 0, low)
 
         round_wv(nc.vector.tensor_copy, 0, 0, 2)
@@ -287,26 +298,25 @@ def tile_list_clicked_item_candidates_kernel(
         round_wv(nc.scalar.copy, 0, 1, 4, parts=slice(1, 2))
         round_wv(nc.scalar.copy, 1, 1, 4)
 
-        gate_sums(1, 1, high, (0,))
-        ring = high[1:] + low + high[1:2]
-        for c in range(3):
+        ring = high + low
+        for c in range(2):
             open_values(0, c, ring[c])
         for c in range(8):
             bank = ring[c]
-            if c >= 3:
+            if c >= 2:
                 whole_values(0, c, bank)
             else:
                 close_values(0, c, bank)
             product(0, c, bank)
-        last = [high[0], high[2], high[3], low[0]]
-        gate_sums(1, 1, last, (1, 2, 3))
+        last = high
+        gate_sums(1, 1, last)
         quantize_wv(0, 1, 0, 4)
         quantize_h(0, 0, 4)
         quantize_wv(1, 1, 2, 4)
         quantize_wv(1, 1, 0, 2)
         quantize_h(0, 4, 8)
         sigmoids(1, 1, last)
-        ring = low[1:] + high[1:2] + last
+        ring = low + last
 
         for c in range(2):
             open_values(1, c, ring[c])

@@ -85,8 +85,9 @@ def tile_list_clicked_item_candidates_kernel(
             for s in range(4):
                 nc.sync.dma_start(out=planes[s:P:32, :, :], in_=scale_rows(scales, s))
 
-        def load_table_words(a):
-            nc.sync.dma_start(out=tab_w[a][:], in_=tab_words[a].rearrange("p n i -> p (n i)").bitcast(I32))
+        def load_table_words(a, c0=0, c1=T):
+            words = tab_words[a].rearrange("p n i -> p (n i)").bitcast(I32)
+            nc.sync.dma_start(out=tab_w[a][:, c0:c1], in_=words[:, c0:c1])
 
         def load_wv(a, b):
             for c0, c1, raw in wv_parts[a, b]:
@@ -207,9 +208,9 @@ def tile_list_clicked_item_candidates_kernel(
                     nc.vector.tensor_scalar(out=y_sb[:, n, cols], in0=sums, scalar1=bias, scalar2=None, op0=ALU.add)
                 else:
                     nc.scalar.activation(out=y_sb[:, n, cols], in_=sums, func=ACT.Identity, bias=bias)
-                if c1 - c0 > 1:
+                if c1 - c0 > 1 and c0 > 0:
                     nc.sync.dma_start(out=out[n * P : (n + 1) * P, cols], in_=y_sb[:, n, cols])
-            if c1 - c0 == 1:
+            if c1 - c0 == 1 or c0 == 0:
                 nc.sync.dma_start(out=out.rearrange("(n p) j -> p n j", n=2)[:, :, cols], in_=y_sb[:, :, cols])
 
         nc.gpsimd.memset(tab_s[:], 0)
@@ -225,9 +226,10 @@ def tile_list_clicked_item_candidates_kernel(
         for s in range(4):
             nc.sync.dma_start(out=tab_s[s:P:SHIFT, :], in_=scale_rows(tab_scales, s))
         nc.sync.dma_start(offsets[:], offs)
-        load_table_words(0)
+        load_table_words(0, 0, T - HALF)
         nc.scalar.dma_start(out=bg_sb[:], in_=bg.rearrange("(b p t) -> p b t", b=2, t=4))
         load_planes(wg_s_raw, wg_scales)
+        load_table_words(0, T - HALF, T)
         load_table_words(1)
         nc.sync.dma_start(out=wg_raw[1, 0], in_=wg_i32[1, :, 0 : HALF // 2])
         nc.vector.tensor_copy(out=v_s[:], in_=tab_s[:].bitcast(U8).indirect(offsets[:]))
@@ -265,8 +267,7 @@ def tile_list_clicked_item_candidates_kernel(
         reorder_wg_words(0, 0)
         reorder_wg_words(1, 0, 0, 2)
         reorder_wg_words(1, 0, 2, 4)
-        reorder_wg_scales(0, 0, 0, 2)
-        reorder_wg_scales(0, 0, 2, 4)
+        reorder_wg_scales(0, 0)
         reorder_wg_scales(1, 0)
         for reorder in (reorder_wg_scales, reorder_wg_words):
             for a in range(2):
@@ -318,10 +319,10 @@ def tile_list_clicked_item_candidates_kernel(
         sigmoids(1, 1, last)
         ring = low + last
 
-        for c in range(2):
+        for c in range(3):
             open_values(1, c, ring[c])
         for c in range(4):
-            if c >= 2:
+            if c >= 3:
                 whole_values(1, c, ring[c])
             else:
                 close_values(1, c, ring[c])

from contextlib import ExitStack

import concourse.mybir as mybir

K, T, S, H, N = 1024, 2048, 1024, 1024, 256
FLOPS = 2 * K * H * S * 2 + 2 * H * N * S

F32 = mybir.dt.float32
BF16 = mybir.dt.bfloat16
I32 = mybir.dt.int32
U32 = mybir.dt.uint32
U16 = mybir.dt.uint16
U8 = mybir.dt.uint8
FP8X4 = mybir.dt.float8_e4m3fn_x4
FP4X4 = mybir.dt.float4_e2m1fn_x4
ACT = mybir.ActivationFunctionType
ALU = mybir.AluOpType

P = 128
HALF = 512
QUARTER = 256
TAIL = 384
WARM_UPS = 5
LATE_WARM_UPS = 2
MX_ALIGN = 256
SHIFT = 16


def tile_list_clicked_item_candidates_kernel(
    tc, tab_words, tab_scales, offs, wg_words, wg_scales, bg, wv, wd_words, wd_scales, bd, out
):
    nc = tc.nc
    with ExitStack() as ctx:
        keep = ctx.enter_context(tc.tile_pool(name="keep", bufs=1))
        psum = ctx.enter_context(tc.psum_pool(name="psum", bufs=1))
        banks = [psum.tile([P, HALF], F32, name="bank%d" % i) for i in range(8)]
        low, high = banks[:4], banks[4:]

        def sbuf(name, shape, dtype):
            return keep.tile(shape, dtype, name=name, align_bytes=MX_ALIGN)

        pairs = [(x, y) for x in range(2) for y in range(2)]
        offsets = keep.tile([P, S // 16], U16, name="offsets")
        bg_sb = sbuf("bg_sb", [P, 2, 4], F32)
        bd_sb = sbuf("bd_sb", [P, 2], F32)
        warm = sbuf("warm", [P, 2], F32)
        tab_w = [sbuf("tab_w%d" % a, [P, T], I32) for a in range(2)]
        tab_s = sbuf("tab_s", [P, T // 4], I32)
        v_w = [sbuf("v_w%d" % a, [P, S], U32) for a in range(2)]
        v_s = sbuf("v_s", [P, S], U8)
        v_s_moved = sbuf("v_s_moved", [P, S // 4], I32)
        wg_raw = {(a, 0): sbuf("wg_raw%d0" % a, [P, HALF // 2], I32)[:] for a in range(2)}
        wg_raw_late = sbuf("wg_raw_late", [P, 2, HALF // 2], I32)
        for a in range(2):
            wg_raw[a, 1] = wg_raw_late[:, a, :]
        wg_s_raw = sbuf("wg_s_raw", [P, 2, H // 4], I32)
        wg_w = {(a, b): sbuf("wg_w%d%d" % (a, b), [P, 2 * HALF], U8) for a, b in pairs}
        wg_s = {(a, b): sbuf("wg_s%d%d" % (a, b), [P, HALF], U8) for a, b in pairs}
        cuts = {(0, 0): HALF, (1, 0): TAIL, (0, 1): P, (1, 1): QUARTER}
        wv_parts = {}
        for a, b in pairs:
            ends = sorted({0, cuts[a, b], HALF})[: 2 if (a, b) == (1, 1) else 3]
            wv_parts[a, b] = [
                (c0, c1, sbuf("wv_raw%d%d_%d" % (a, b, c0), [P, 4, c1 - c0], F32)[:]) for c0, c1 in zip(ends, ends[1:])
            ]
        gate = {(b, u): sbuf("gate%d%d" % (b, u), [P, 4, HALF], F32) for b, u in pairs}
        wv_parts[1, 1].append((QUARTER, HALF, gate[1, 1][:, :, 0:QUARTER]))
        wv_bf = {(a, b): sbuf("wv_bf%d%d" % (a, b), [P, 4 * HALF], BF16) for a, b in pairs}
        wv_w = {(a, b): sbuf("wv_w%d%d" % (a, b), [P, HALF], U32) for a, b in pairs}
        wv_s = {(a, b): sbuf("wv_s%d%d" % (a, b), [P, HALF], U8) for a, b in pairs}
        h_bf = [sbuf("h_bf%d" % b, [P, 4 * S], BF16) for b in range(2)]
        h_w = [sbuf("h_w%d" % b, [P, S], U32) for b in range(2)]
        h_s = [sbuf("h_s%d" % b, [P, S], U8) for b in range(2)]
        wd_w = sbuf("wd_w", [P, 2, N], I32)
        wd_s = sbuf("wd_s", [P, 2, N // 4], I32)
        y_sb = sbuf("y_sb", [P, 2, S], F32)
        zeros_bf = sbuf("zeros_bf", [P, 4 * P], BF16)
        zeros_w = sbuf("zeros_w", [P, P], U32)
        zeros_s = sbuf("zeros_s", [P, P], U8)

        def scale_rows(scales, s):
            return scales.bitcast(I32).rearrange("a (q s) w -> s q a w", s=4)[s]

        def load_planes(planes, scales):
            for s in range(4):
                nc.sync.dma_start(out=planes[s:P:32, :, :], in_=scale_rows(scales, s))

        def load_table_words(a, c0=0, c1=T):
            words = tab_words[a].rearrange("p n i -> p (n i)").bitcast(I32)
            nc.sync.dma_start(out=tab_w[a][:, c0:c1], in_=words[:, c0:c1])

        def load_wv(a, b):
            for c0, c1, raw in wv_parts[a, b]:
                rows = wv[a * HALF : (a + 1) * HALF, b * HALF + c0 : b * HALF + c1]
                nc.sync.dma_start(out=raw, in_=rows.rearrange("(p i) c -> p i c", i=4))

        def round_wv(copy, a, b, width, order=(0, 2), parts=slice(0, 2)):
            for c0, c1, raw in wv_parts[a, b][parts]:
                dst = wv_bf[a, b][:].rearrange("p (t m i) -> p m i t", t=4, i=4)[:, c0 // 4 : c1 // 4, :, :]
                src = raw.rearrange("p i (m t) -> p m i t", t=4)
                for t0 in order if width == 2 else (0,):
                    copy(out=dst[:, :, :, t0 : t0 + width], in_=src[:, :, :, t0 : t0 + width])

        def quantize_wv(a, b, t0, t1):
            cols = slice(t0 * P, t1 * P)
            nc.vector.quantize_mx(
                out=wv_w[a, b][:, cols].bitcast(FP8X4),
                scales=wv_s[a, b][:, cols],
                in_=wv_bf[a, b][:, t0 * HALF : t1 * HALF],
            )

        def reorder_wg_words(a, b, t0=0, t1=4):
            (nc.gpsimd.tensor_copy if b == 1 else nc.scalar.copy)(
                out=wg_w[a, b][:].bitcast(U16).rearrange("p (t m) -> p t m", t=4)[:, t0:t1, :],
                in_=wg_raw[a, b].bitcast(U16).rearrange("p (m t) -> p t m", t=4)[:, t0:t1, :],
            )

        def reorder_wg_scales(a, b, t0=0, t1=4, engine=nc.gpsimd):
            raw = wg_s_raw[:].bitcast(U8)[:, a, b * HALF : (b + 1) * HALF]
            engine.tensor_copy(
                out=wg_s[a, b][:].rearrange("p (t m) -> p t m", t=4)[:, t0:t1, :],
                in_=raw.rearrange("p (m t) -> p t m", t=4)[:, t0:t1, :],
            )

        def gather_words(a, j0, j1):
            picks = offsets[:, j0 // 16 : j1 // 16]
            nc.vector.tensor_copy(out=v_w[a][:, j0:j1], in_=tab_w[a][:].bitcast(U32).indirect(picks))

        def v_plane(a, j0, j1):
            return (v_s[:] if a == 0 else v_s_moved[:].bitcast(U8))[:, j0:j1]

        def gate_pass(bank, a, b, t, j0, j1, start, stop):
            nc.tensor.matmul_mx(
                out=bank[:, j0 % HALF : j0 % HALF + j1 - j0],
                lhsT=wg_w[a, b][:, 2 * t * P : 2 * (t + 1) * P].bitcast(FP4X4),
                lhsT_scale=wg_s[a, b][:, t * P : (t + 1) * P],
                rhs=v_w[a][:, j0:j1].bitcast(FP8X4),
                rhs_scale=v_plane(a, j0, j1),
                start=start,
                stop=stop,
            )

        def gate_sums(b, u, used, ts=range(4)):
            for t in ts:
                for a in range(2):
                    gate_pass(used[t], a, b, t, u * HALF, (u + 1) * HALF, a == 0, a == 1)

        def sigmoids(b, u, used, ts=range(4)):
            for t in ts:
                nc.scalar.activation(
                    out=gate[b, u][:, t, :], in_=used[t][:], func=ACT.Sigmoid, bias=bg_sb[:, b, t : t + 1]
                )

        def value_passes(b, c, bank, a, ts, start, stop):
            for t in ts:
                nc.tensor.matmul_mx(
                    out=bank[:, t * P : (t + 1) * P],
                    lhsT=wv_w[a, b][:, t * P : (t + 1) * P].bitcast(FP8X4),
                    lhsT_scale=wv_s[a, b][:, t * P : (t + 1) * P],
                    rhs=v_w[a][:, c * P : (c + 1) * P].bitcast(FP8X4),
                    rhs_scale=v_plane(a, c * P, (c + 1) * P),
                    start=start and t == ts[0],
                    stop=stop and t == ts[-1],
                )

        def open_values(b, c, bank):
            value_passes(b, c, bank, 0, (0, 1, 2, 3), True, False)

        def close_values(b, c, bank):
            value_passes(b, c, bank, 1, (2, 3, 0, 1), False, True)

        def whole_values(b, c, bank):
            value_passes(b, c, bank, 1, (2, 3, 0, 1), True, False)
            value_passes(b, c, bank, 0, (0, 1, 2, 3), False, True)

        def product(b, c, bank):
            nc.vector.tensor_tensor(
                out=h_bf[b][:, c * HALF : (c + 1) * HALF].rearrange("p (j e t) -> p j t e", e=2, t=4),
                in0=bank[:].rearrange("p (t j e) -> p j t e", t=4, e=2),
                in1=gate[b, c // 4][:, :, (c % 4) * P : (c % 4 + 1) * P].rearrange("p t (j e) -> p j t e", e=2),
                op=ALU.mult,
            )

        def quantize_h(b, c0, c1):
            cols = slice(c0 * P, c1 * P)
            nc.vector.quantize_mx(
                out=h_w[b][:, cols].bitcast(FP8X4), scales=h_s[b][:, cols], in_=h_bf[b][:, c0 * HALF : c1 * HALF]
            )

        def project_pass(b, c0, c1, used):
            for n in range(2):
                nc.tensor.matmul_mx(
                    out=used[n][:, 0 : (c1 - c0) * P],
                    lhsT=wd_w[:, b, n * P : (n + 1) * P].bitcast(FP8X4),
                    lhsT_scale=wd_s[:, b, :].bitcast(U8)[:, n * P : (n + 1) * P],
                    rhs=h_w[b][:, c0 * P : c1 * P].bitcast(FP8X4),
                    rhs_scale=h_s[b][:, c0 * P : c1 * P],
                    start=(b == 0),
                    stop=(b == 1),
                )

        def store(c0, c1, used):
            cols = slice(c0 * P, c1 * P)
            for n in range(2):
                sums = used[n][:, 0 : (c1 - c0) * P]
                bias = bd_sb[:, n : n + 1]
                if n == 1 and c1 - c0 == 1:
                    nc.vector.tensor_scalar(out=y_sb[:, n, cols], in0=sums, scalar1=bias, scalar2=None, op0=ALU.add)
                else:
                    nc.scalar.activation(out=y_sb[:, n, cols], in_=sums, func=ACT.Identity, bias=bias)
                if c1 - c0 > 1 and c0 > 0:
                    nc.sync.dma_start(out=out[n * P : (n + 1) * P, cols], in_=y_sb[:, n, cols])
            if c1 - c0 == 1 or c0 == 0:
                nc.sync.dma_start(out=out.rearrange("(n p) j -> p n j", n=2)[:, :, cols], in_=y_sb[:, :, cols])

        nc.gpsimd.memset(tab_s[:], 0)
        nc.gpsimd.memset(warm[:], 0.0)
        for planes in (wg_s_raw, v_s_moved, wd_s):
            nc.gpsimd.memset(planes[:], 0)
        nc.vector.memset(zeros_bf[:].bitcast(I32), 0)
        nc.vector.quantize_mx(out=zeros_w[:].bitcast(FP8X4), scales=zeros_s[:], in_=zeros_bf[:])
        nc.scalar.activation(out=warm[:, 1:2], in_=warm[:, 0:1], func=ACT.Sigmoid)

        wg_i32 = wg_words.bitcast(I32)
        nc.sync.dma_start(out=wg_raw[0, 0], in_=wg_i32[0, :, 0 : HALF // 2])
        for s in range(4):
            nc.sync.dma_start(out=tab_s[s:P:SHIFT, :], in_=scale_rows(tab_scales, s))
        nc.sync.dma_start(offsets[:], offs)
        load_table_words(0, 0, T - HALF)
        nc.scalar.dma_start(out=bg_sb[:], in_=bg.rearrange("(b p t) -> p b t", b=2, t=4))
        load_planes(wg_s_raw, wg_scales)
        load_table_words(0, T - HALF, T)
        load_table_words(1)
        nc.sync.dma_start(out=wg_raw[1, 0], in_=wg_i32[1, :, 0 : HALF // 2])
        nc.vector.tensor_copy(out=v_s[:], in_=tab_s[:].bitcast(U8).indirect(offsets[:]))
        for s in range(4):
            nc.sync.dma_start(out=v_s_moved[s:P:32, :], in_=v_s[SHIFT + s : P : 32, :].bitcast(I32))
        nc.sync.dma_start(out=wg_raw_late[:], in_=wg_i32[:, :, HALF // 2 : HALF].rearrange("a p w -> p a w"))
        for b in range(2):
            for a in range(2):
                load_wv(a, b)
        nc.sync.dma_start(out=wd_w[:], in_=wd_words.rearrange("b p n i -> p b (n i)").bitcast(I32))
        load_planes(wd_s, wd_scales)
        with nc.allow_non_contiguous_dma(reason="one bias value for each partition"):
            nc.sync.dma_start(out=bd_sb[:], in_=bd.rearrange("(n p) -> p n", n=2))

        for warm_up in range(WARM_UPS):
            nc.tensor.matmul_mx(
                out=banks[7][:],
                lhsT=zeros_w[:, 0:P].bitcast(FP8X4),
                lhsT_scale=zeros_s[:, 0:P],
                rhs=wg_raw[0, 0].bitcast(U8).bitcast(FP4X4),
                rhs_scale=tab_s[:].bitcast(U8)[:, 0:HALF],
                start=True,
                stop=True,
            )
        for warm_up in range(LATE_WARM_UPS):
            nc.tensor.matmul_mx(
                out=banks[7][:],
                lhsT=zeros_w[:].bitcast(FP8X4),
                lhsT_scale=zeros_s[:],
                rhs=tab_w[0][:, 0:HALF].bitcast(FP8X4),
                rhs_scale=tab_s[:].bitcast(U8)[:, 0:HALF],
                start=True,
                stop=True,
            )
        reorder_wg_words(0, 0)
        reorder_wg_words(1, 0, 0, 2)
        reorder_wg_words(1, 0, 2, 4)
        reorder_wg_scales(0, 0)
        reorder_wg_scales(1, 0)
        for reorder in (reorder_wg_scales, reorder_wg_words):
            for a in range(2):
                reorder(a, 1)
        def gathered_gates(a, j0, j1):
            gather_words(a, j0, j1)
            for t in range(4):
                first, final = a == 0 and j0 % HALF == 0, a == 1 and j1 % HALF == 0
                gate_pass(banks[4 * (j0 // HALF) + t], a, 0, t, j0, j1, first, final)

        for j0 in range(0, S, QUARTER):
            gathered_gates(0, j0, j0 + QUARTER)
        for j0, j1 in ((0, P), (P, QUARTER), (QUARTER, HALF), (HALF, HALF + QUARTER)):
            gathered_gates(1, j0, j1)
        sigmoids(0, 0, low)
        gate_sums(1, 0, low, (0,))
        gathered_gates(1, HALF + QUARTER, S)
        sigmoids(0, 1, high)
        gate_sums(1, 0, low, (1, 2, 3))
        sigmoids(1, 0, low)

        round_wv(nc.vector.tensor_copy, 0, 0, 2)
        quantize_wv(0, 0, 0, 2)
        quantize_wv(0, 0, 2, 4)
        round_wv(nc.vector.tensor_copy, 1, 0, 2, (2, 0))
        quantize_wv(1, 0, 2, 4)
        quantize_wv(1, 0, 0, 2)
        round_wv(nc.vector.tensor_copy, 0, 1, 2, parts=slice(0, 1))
        round_wv(nc.scalar.copy, 0, 1, 4, parts=slice(1, 2))
        round_wv(nc.scalar.copy, 1, 1, 4)

        ring = high + low
        for c in range(2):
            open_values(0, c, ring[c])
        for c in range(8):
            bank = ring[c]
            if c >= 2:
                whole_values(0, c, bank)
            else:
                close_values(0, c, bank)
            product(0, c, bank)
        last = high
        gate_sums(1, 1, last)
        quantize_wv(0, 1, 0, 4)
        quantize_h(0, 0, 4)
        quantize_wv(1, 1, 2, 4)
        quantize_wv(1, 1, 0, 2)
        quantize_h(0, 4, 8)
        sigmoids(1, 1, last)
        ring = low + last

        for c in range(3):
            open_values(1, c, ring[c])
        for c in range(4):
            if c >= 3:
                whole_values(1, c, ring[c])
            else:
                close_values(1, c, ring[c])

        def values(c):
            whole_values(1, c, ring[c])

        def finish(c0, c1, used):
            project_pass(1, c0, c1, used)
            store(c0, c1, used)

        values(4)
        values(5)
        for c in range(3):
            product(1, c, ring[c])
        project_pass(0, 0, 2, ring[0:2])
        quantize_h(1, 0, 2)
        finish(0, 2, ring[0:2])
        values(6)
        values(7)
        product(1, 3, ring[3])
        product(1, 4, ring[4])
        project_pass(0, 2, 4, ring[2:4])
        quantize_h(1, 2, 4)
        finish(2, 4, ring[2:4])
        product(1, 5, ring[5])
        product(1, 6, ring[6])
        project_pass(0, 4, 6, ring[4:6])
        quantize_h(1, 4, 6)
        finish(4, 6, ring[4:6])
        product(1, 7, ring[7])
        project_pass(0, 6, 7, ring[0:2])
        project_pass(0, 7, 8, ring[2:4])
        quantize_h(1, 6, 7)
        quantize_h(1, 7, 8)
        finish(6, 7, ring[0:2])
        finish(7, 8, ring[2:4])
